import numpy as np, ml_dtypes
CORES = [1,5,17,21,33,37,49,53]
N = 8
import mx_ref
BF = ml_dtypes.bfloat16
def gentries(a):
    return np.ascontiguousarray(a.reshape(8, 16, -1).transpose(0, 2, 1)).reshape(8, -1)
def gtable(e):
    e = np.asarray(e); return np.ascontiguousarray(e.reshape(8, -1, 16).transpose(0, 2, 1)).reshape(128, -1).astype(np.int32)
def gcols(t, e):
    v = np.concatenate([t.reshape(8, 16, -1, 4), np.zeros((8, 16, 1, 4), BF)], axis=2)
    return np.ascontiguousarray(np.stack([v[g][:, e[g]] for g in range(8)])).reshape(128, -1)
def tile(rs):
    return np.stack(rs, axis=2).reshape(128, -1).astype(BF)
def pick(q, e):
    c = np.concatenate([q[0].reshape(128, -1, 4), np.zeros((128, 1, 4), np.uint8)], axis=1); s = np.concatenate([q[1], np.ones((16, 1), np.uint8)], axis=1)
    return (np.ascontiguousarray(c[:, e].reshape(128, -1)), np.ascontiguousarray(s[:, e]))
def join(*qs):
    return (np.concatenate([q[0] for q in qs], axis=1), np.concatenate([q[1] for q in qs], axis=1))
def put(q, e, v):
    c, s = q[0].reshape(128, -1, 4).copy(), q[1].copy(); c[:, e] = v[0].reshape(128, -1, 4); s[:, e] = v[1]
    return (c.reshape(128, -1), s)
def pk(c, s):
    return (np.ascontiguousarray(c), mx_ref.live(s))
def emit(q):
    return q[0], q[1]
def packed(v, rng):
    q = [mx_ref.quantize(np.ascontiguousarray(v[r])) for r in range(N)]
    return np.stack([a for a, b in q]), np.stack([mx_ref.plane(b, rng) for a, b in q])
def values_of_codes():
    e, c = np.zeros((128, 128, 4), np.float32), np.zeros((128, 2, 4), np.uint8)
    e[np.arange(128), np.arange(128), 0] = 1
    c[:127, :, 0] = np.arange(256).reshape(2, 128).T[:127]
    return mx_ref.matmul(mx_ref.quantize(e.reshape(128, 512).astype(BF)), (c.reshape(128, 8), np.full((16, 2), 127, np.uint8))).T.reshape(-1).astype(np.float64)
CODE_VALUE, SCALE_VALUE = values_of_codes(), 2.0 ** (np.arange(256) - 127.0)
def decode(q):
    return (CODE_VALUE[q[0]].reshape(16, 8, -1, 4) * SCALE_VALUE[q[1]][:, None, :, None] + 0.0).reshape(128, -1).astype(np.float32)
def f(rng, *shape):
    return mx_ref.flush((rng.standard_normal(shape, dtype=np.float32) * np.exp2(rng.integers(-2, 3, shape[:-1] + (1,)))).astype(BF))
def wide(rng, *shape, cols=0):
    v = rng.standard_normal(shape, dtype=np.float32) * np.exp2(rng.integers(-12, 13, shape)).astype(np.float32)
    if cols: v *= np.repeat(np.exp2(rng.integers(-cols, cols + 1, shape[:-2] + (1, shape[-1] // 4))) * (rng.random(shape[:-2] + (1, shape[-1] // 4)) > 0.0625), 4, axis=-1).astype(np.float32)
    return mx_ref.flush(v.astype(BF))
C, K = 256, 64
STRIDE = [1, 2, 4]
def at(t, e):
    return np.take_along_axis(t, e, axis=1)
def halved(a, b):
    return ((a.astype(np.float32) + b.astype(np.float32)) * np.float32(0.5)).astype(BF)
def big(v):
    v = np.array(v).astype(np.float32)
    v[np.abs(v) < np.float32(2.0 ** -16)] = 0
    return np.clip(v, -2.0 ** 21, 2.0 ** 21).astype(BF)
def numbers_of(rng):
    return {"x": big(f(rng, N, 128, 4 * C)), "u": np.array(f(rng, N, 128, 512)), "v": np.array(f(rng, N, 128, 512))}
def pairs(a, b):
    e = np.zeros(C, np.int64)
    e[a] = b
    e[b] = a
    return e
def pairing(rng):
    z = rng.permutation(C).reshape(2, -1)
    return pairs(z[0], z[1])
def pairings(rng):
    return np.stack([gtable(np.stack([pairing(rng) for g in range(8)])) for r in range(N)])
def layers(rng, still=[]):
    w = big(f(rng, N, 128, 2048).astype(np.float32) * np.float32(0.0625)).reshape(N, 8, 16, 4, 8, 16, 4)
    for i in still:
        w[:, :, i] = 0
        w[:, :, :, :, :, i] = 0
    return w
def weights(rng, w):
    c, s = packed(np.ascontiguousarray(w).reshape(N, 128, 2048), rng)
    return {"wc": c, "ws": s}
def setup_inputs(rng):
    return {**numbers_of(rng), "m": pairings(rng), **weights(rng, layers(rng))}
def setup_inputs_ties(rng):
    d = numbers_of(rng)
    x = d["x"].reshape(N, 8, 16, C, 4)
    x[:, :, 0] = 0
    x[:, :, 0, :, 0] = rng.integers(1, 4, (N, 8, C)).astype(np.float32).astype(BF)
    u = d["u"].reshape(N, 128, 128, 4)
    u[:, :, ::16] = 0
    o = rng.permutation(N)
    for r in range(N):
        for h in range(0, 128, 16): u[r, h, h, 0] = 0.0 if r == o[0] else -1.0 if r == o[1] else 1.0
    w = layers(rng, [0])
    a = 2 * int(rng.integers(N // 2))
    x[a, :, 8:] = 2.0 ** 18
    x[a + 1, :, 8:] = -2.0 ** 18
    w[a:a + 2, :, 8:] = 0
    return {"x": x.reshape(N, 128, 4 * C), "u": u.reshape(N, 128, 512), "v": d["v"], "m": pairings(rng), **weights(rng, w)}
def setup_inputs_near(rng):
    d = numbers_of(rng)
    x = d["x"].astype(np.float32).reshape(N, 8, 16, C, 4)
    x[:, :, 0] = 0
    x[:, :, 8:] = 0
    u = d["u"].reshape(N, 128, 128, 4)
    u[:, :, ::16] = 0
    s = rng.integers(0, 16, (N, 8, C))
    digits = ((s[:, :, :, None] >> np.arange(4)) & 1) * np.exp2(np.arange(4) - 23.0)
    o = rng.permutation(N) % 4
    for r in range(N):
        sign = rng.permutation(8) % 2 * 2.0 - 1.0
        k = 2.0 ** -4 if o[r] == 1 else 1.0
        c = 1.0 if o[r] == 0 else 2.0 ** -30
        if o[r] < 2:
            x[r, :, 0, :, 0] = k
            x[r, :, 11, :, 0] = k * 2.0 ** -10
        if o[r] < 3: x[r, :, 8] = k * digits[r]
        if o[r] == 2:
            for g in rng.permutation(8)[:4]:
                a = rng.permutation(C)
                x[r, g, 0, a[0], 0] = 2.0 ** 21
                x[r, g, 0, a[1], 0] = -2.0 ** 21
        if o[r] == 3:
            e = rng.integers(0, 2, (8, C))
            x[r, :, 9, :, 0] = e * 1.125 * 2.0 ** -27
            x[r, :, 10, :, 0] = (1 - e) * 2.0 ** -27
            x[r, :, 12, :, 0] = 2.0 ** -27
        for g in range(8):
            h = 16 * g
            if o[r] < 3:
                u[r, h, h, 0] = sign[g] * (c if o[r] < 2 else 2.0 ** 30)
                u[r, h + 8, h] = sign[g] * c
            if o[r] < 2: u[r, h + 11, h, 0] = sign[g] * c
            if o[r] == 3:
                u[r, h + 9, h, 0] = sign[g] * 1.125 * c
                u[r, h + 10, h, 0] = sign[g] * 1.25 * c
                u[r, h + 12, h, 0] = sign[g] * -1.125 * c
    return {"x": x.reshape(N, 128, 4 * C).astype(BF), "u": u.reshape(N, 128, 512), "v": d["v"], "m": pairings(rng), **weights(rng, layers(rng, [0, 8, 9, 10, 11, 12, 13, 14, 15]))}
def setup_inputs_blocks(rng):
    d = numbers_of(rng)
    k = rng.integers(-2, 3, (8, 1, 1, 1, 1))
    unit = np.exp2(k * 1.0).reshape(8, 1, 1, 1)
    e = np.arange(32).reshape(8, 1, 4)
    x = np.exp2(k - rng.integers(8, 15, (N, 8, 2, 8, C, 4))) * (1.0 + (2 * rng.integers(0, 64, (N, 8, 2, 8, C, 4)) + 1) * 2.0 ** -7)
    x[:, :, 0, 1, :, 0] = np.exp2(k.reshape(8, 1) - rng.integers(13, 15, (N, 8, C))) * (1.0 + (2 * rng.integers(0, 64, (N, 8, C)) + 1) * 2.0 ** -7)
    i = rng.integers(0, 31, (N, 8, 1, C, 1))
    i = np.where(i >= 4, i + 1, i)
    x[:, :, 0] = np.where(e == i, 1.96875 * unit, x[:, :, 0])
    x = x * (rng.integers(0, 2, x.shape) * 2.0 - 1.0)
    i = rng.integers(0, 32, (N, 8, 1, 1, 1))
    x[:, :, 1] = np.where(e == i, np.where(rng.random((N, 8, 1, C, 1)) < 0.5, 3.0, 0.9375) * unit, x[:, :, 1])
    m = np.stack([np.stack([pairing(rng) for g in range(8)]) for r in range(N)])
    for g in rng.permutation(8)[:4]:
        for a in range(0, N, 4):
            z = rng.permutation(C)
            t = np.roll(z, -1)
            m[a:a + 2, g] = pairs(z[::2], z[1::2])
            m[a + 2:a + 4, g] = pairs(t[::2], t[1::2])
            x[a:a + 4, g, 0, 1, :, 0] = -1.0
            x[a:a + 2, g, 0, 1, t[::4], 0] = 1.0
            x[a + 2:a + 4, g, 0, 1, z[::4], 0] = 1.0
    u = d["u"].reshape(N, 128, 128, 4)
    u[:, :, ::16] = 0
    for h in range(0, 128, 16): u[:, h + 1, h, 0] = 1.0
    w = layers(rng)
    w[:, :, :, :, :, 1] = 0
    w[:, :, :, :, :, 8:] = 0
    return {"x": x.astype(np.float32).reshape(N, 128, 4 * C).astype(BF), "u": u.reshape(N, 128, 512), "v": d["v"], "m": np.stack([gtable(m[r]) for r in range(N)]), **weights(rng, w)}
def setup_inputs_ends(rng):
    d = numbers_of(rng)
    v = np.array(d["v"]).astype(np.float32)
    u = d["u"].reshape(N, 128, 128, 4)
    u[:, :, ::16] = 0
    x = np.zeros((N, 8, 16, C, 4), np.float32)
    w = np.zeros((N, 128, 4, 128, 4), np.float32)
    m = np.zeros((N, 8, C), np.int64)
    high = rng.random((N, 8, C)) < 0.5
    kind = rng.permutation(N // 2)
    n = np.arange(128)
    for i in range(N // 2):
        a, b = 2 * i, 2 * i + 1
        for g in range(8):
            if kind[i] == 1:
                m[a, g] = np.arange(C)[::-1] if g % 2 else np.arange(C) ^ 1
                m[b, g] = m[a, g]
                continue
            z = rng.permutation(C).reshape(-1, 4 if kind[i] == 3 else C)
            t = np.roll(z, -1, axis=1)
            m[a, g] = pairs(z[:, ::2], z[:, 1::2])
            m[b, g] = pairs(t[:, ::2], t[:, 1::2])
            high[a, g] = False
            high[b, g] = False
            high[a, g, t[:, ::4]] = True
            high[b, g, z[:, ::4]] = True
        one = a + int(rng.integers(2))
        whole = rng.permutation(8)
        for r in (a, b):
            large = kind[i] == 2 or (kind[i] < 2 and r == one)
            below = kind[i] == 1 and r == one
            top = -1.0 if below else -0.5 if r == one and kind[i] in (0, 2) else 1.0
            x[r] = ((2.0 ** 21 if large else 2.0 ** -27) * np.where(high[r], top, -0.75 if below else -1.0))[:, None, :, None]
            k = 2.0 ** 30 if large else 2.0 ** -30
            for h in range(0, 128, 16):
                u[r, h:h + 16, h] = k
                if below and whole[h // 16] < 4: u[r, :, h] = k
                elif below:
                    g = (h + 16) % 128
                    u[r, g:g + 16, h] = -k
            v[r] = k * (rng.integers(0, 2, v[r].shape) * 2.0 - 1.0)
            for c in range(4): w[r, n, c, n, c] = 128.0 if below else 128.0 * (rng.integers(0, 2) * 2.0 - 1.0)
    return {"x": x.reshape(N, 128, 4 * C).astype(BF), "u": u.reshape(N, 128, 512), "v": v.astype(BF), "m": np.stack([gtable(m[r]) for r in range(N)]), **weights(rng, w.astype(BF))}
def setup_inputs_spread(rng):
    d = setup_inputs(rng)
    d["x"] = big(wide(rng, N, 128, 4 * C, cols=6))
    return d
def check_inputs(d):
    b = []
    for k, low, top in (("x", 2.0 ** -27, 2.0 ** 21), ("u", 2.0 ** -30, 2.0 ** 30), ("v", 2.0 ** -30, 2.0 ** 30)):
        a = np.abs(d[k].astype(np.float32))
        if not (np.isfinite(a).all() and ((a == 0) | (a >= low) & (a <= top)).all()): b.append("a value of " + k)
    none, least, most = [emit(mx_ref.quantize(np.full((128, 16), k, np.float32).astype(BF)))[1][0, 0] for k in (0.0, 2.0 ** -30, 2.0 ** 30)]
    for r in range(N):
        e = gentries(d["m"][r])
        if ((e < 0) | (e >= C)).any(): b.append("an entry of m")
        elif (e == np.arange(C)).any() or (at(e, e) != np.arange(C)).any(): b.append("m: no pairing")
        if ((d["wc"][r] & 0x7F) == 0x7F).any(): b.append("wc: a code that is no number")
        s = mx_ref.live(d["ws"][r])
        if ((s != none) & ((s < least) | (s > most))).any(): b.append("ws: a scale out of range")
        a = np.abs(decode(pk(d["wc"][r], d["ws"][r])).astype(np.float64)).reshape(128, 512, 4)
        if not (np.sum(a, axis=(0, 2)) <= 128).all(): b.append("W: the sizes of a column")
    return b
def reference(x, u, v, m, wc, ws):
    qu = [mx_ref.quantize(u[r]) for r in range(N)]
    lay = [pk(wc[r], ws[r]) for r in range(N)]
    now = [x[r] for r in range(N)]
    mate = [gentries(m[r]) for r in range(N)]
    j = np.arange(C)
    for h in STRIDE:
        q = [mx_ref.quantize(now[r]) for r in range(N)]
        have = [decode(q[r]).astype(BF) for r in range(N)]
        made, mates = [], []
        for r in range(N):
            e = r ^ h
            o, p = mate[r], mate[e]
            s = mx_ref.matmul(qu[r], q[r])[::16] + np.float32(0.0)
            val, low = np.maximum(s, at(s, p)), np.minimum(j, p)
            beats = (val > at(val, o)) | ((val == at(val, o)) & (low < at(low, o)))
            app = beats & at(beats, p)
            n = np.where(app, p, np.where(at(app, o), at(o, at(p, o)), o))
            one, two, slot = np.full((8, K), -1), np.full((8, K), -1), np.full((8, C), -1)
            for g in range(8):
                a = np.flatnonzero(app[g] & (j < p[g]))
                one[g, :len(a)], two[g, :len(a)] = a, p[g][a]
                slot[g, a] = np.arange(len(a))
                slot[g, p[g][a]] = np.arange(len(a))
            came = decode(mx_ref.quantize(halved(gcols(have[e], one), gcols(have[e], two)))).astype(BF)
            add = gcols(came, slot).astype(np.float32)
            own = have[r].astype(np.float32)
            z = mx_ref.quantize(halved(gcols(have[r], o), gcols(have[r], n)))
            made.append(tile([(mx_ref.matmul(pick(lay[r], np.arange(128 * b, 128 * b + 128)), z) * np.float32(0.03125) + own[:, b::4]) + add[:, b::4] for b in range(4)]))
            mates.append(n)
        now, mate = made, mates
    y, om = np.zeros((N, 128, C), np.float32), np.zeros((N, 8, C), np.float32)
    oc, osc = np.zeros((N, 128, 4 * C), np.uint8), np.zeros((N, 16, C), np.uint8)
    for r in range(N):
        q = mx_ref.quantize(now[r])
        y[r] = mx_ref.matmul(mx_ref.quantize(v[r]), q)
        om[r] = mate[r]
        oc[r], osc[r] = emit(q)
    return {"y": y, "om": om, "oc": oc, "osc": osc}

@@ -1,0 +1,360 @@
+from concourse.mybir import dt, AluOpType, ActivationFunctionType
+
+C = 256
+FW = 272
+ROUNDS = 3
+TINY = 2.0 ** -118
+OPT = dict(val2="v", sc2="v", fp="ssss", x="svsv", f="ssss", ta="ssss", two=0, fpo=[[0, 1], [2], [3], []], m1=2)
+
+SCRATCH = {
+    "PA": ("psum", [128, 2048], "float32"),
+    "PB": ("psum", [128, 2048], "float32"),
+    "xin": ("sbuf", [128, 4 * C], "bfloat16"),
+    "uin": ("sbuf", [128, 512], "bfloat16"),
+    "vin": ("sbuf", [128, 512], "bfloat16"),
+    "mi": ("sbuf", [128, 16], "int32"),
+    "xt": ("sbuf", [128, 4 * C], "bfloat16"),
+    "zt": ("sbuf", [128, 4 * C], "bfloat16"),
+    "at": ("sbuf", [128, 4 * C], "bfloat16"),
+    "fh": ("sbuf", [128, 4 * C], "bfloat16"),
+    "fo": ("sbuf", [128, 4 * C], "bfloat16"),
+    "fp": ("sbuf", [128, 4 * FW], "bfloat16"),
+    "fa": ("sbuf", [128, 4 * C], "bfloat16"),
+    "tt": ("sbuf", [128, 528], "bfloat16"),
+    "ia": ("sbuf", [128, 24], "int32"),
+    "ib": ("sbuf", [128, 24], "int32"),
+    "iota": ("sbuf", [128, C], "float32"),
+    "cols": ("sbuf", [128, 8], "float32"),
+    "e01": ("sbuf", [128, 32], "float32"),
+    "c16": ("sbuf", [128, 16], "bfloat16"),
+    "cw": ("sbuf", [128, 512], "bfloat16"),
+    "jw": ("sbuf", [128, 32], "float32"),
+    "poff": ("sbuf", [128, 32], "uint16"),
+    "uoff": ("sbuf", [128, 8], "uint16"),
+    "sc": ("sbuf", [128, 2 * C], "float32"),
+    "val": ("sbuf", [128, 2 * C], "float32"),
+    "dif": ("sbuf", [128, C], "bfloat16"),
+    "tdf": ("sbuf", [128, C], "bfloat16"),
+    "low": ("sbuf", [128, 2 * C], "bfloat16"),
+    "bts": ("sbuf", [128, 2 * C], "bfloat16"),
+    "apo": ("sbuf", [128, 2 * C], "bfloat16"),
+    "aof": ("sbuf", [128, C], "bfloat16"),
+    "ofr": ("sbuf", [128, C], "bfloat16"),
+    "opf": ("sbuf", [128, C], "bfloat16"),
+    "omf": ("sbuf", [128, C], "float32"),
+    "r1": ("sbuf", [128, 2 * C], "bfloat16"),
+    "r2": ("sbuf", [128, C], "bfloat16"),
+    "aw": ("sbuf", [128, 32], "float32"),
+    "sm": ("sbuf", [128, 128], "float32"),
+    "lou": ("sbuf", [128, 16], "uint16"),
+    "ysb": ("sbuf", [128, C], "float32"),
+}
+
+
+def _pair(name, n):
+    SCRATCH[name + "c"] = ("sbuf", [128, n], "float8_e4m3fn_x4")
+    SCRATCH[name + "s"] = ("sbuf", [128, n], "uint8")
+
+
+_pair("e", 4 * 128)
+_pair("qu", 128)
+_pair("pu", 128)
+_pair("qv", 128)
+_pair("qw", 512)
+for _r in range(ROUNDS + 1):
+    _pair("qx%d" % _r, C)
+    SCRATCH["w%d" % _r] = ("sbuf", [128, 48], "float32")
+    SCRATCH["off%d" % _r] = ("sbuf", [128, 48], "uint16")
+for _r in range(ROUNDS):
+    _pair("lx%d" % _r, C)
+    _pair("qa%d" % _r, C)
+    _pair("qz%d" % _r, C)
+    SCRATCH["lp%d" % _r] = ("sbuf", [128, 16], "int32" if _r == 0 else "float32")
+    SCRATCH["pp%d" % _r] = ("sbuf", [128, 16], "uint16")
+
+SEMAPHORES = ["cv", "cs", "cp", "cg", "snd", "ldm", "ldx", "ldu", "ldw", "lds", "ldv", "st1", "st2"]
+for _r in range(ROUNDS):
+    SEMAPHORES += ["ap%d" % _r, "ac%d" % _r, "as%d" % _r]
+
+
+def rank_program(g, core, T, topo):
+    rank = T.rank_of(core)
+    if rank is None:
+        return
+    A = AluOpType
+    COPY = ActivationFunctionType.Copy
+    Q = {"v": g.vector, "s": g.scalar, "p": g.tensor, "g": g, "y": g.sync}
+    CNT = {"v": "cv", "s": "cs", "p": "cp", "g": "cg"}
+    total = {}
+    waited = {}
+    known = {q: {} for q in Q}
+    behind = {}
+    wrote = {}
+    read = {}
+
+    def wait(q, marks):
+        need = {}
+        for s, n in marks:
+            if q == "p" and s == "cp":
+                continue
+            if n > need.get(s, 0):
+                need[s] = n
+        for s, n in sorted(need.items(), key=lambda t: -len(behind.get(t, {}))):
+            if known[q].get(s, 0) >= n:
+                continue
+            Q[q].wait_ge(T.sem[s], n)
+            waited[s] = max(waited.get(s, 0), n)
+            known[q][s] = n
+            for s2, n2 in behind.get((s, n), {}).items():
+                if n2 > known[q].get(s2, 0):
+                    known[q][s2] = n2
+
+    def op(q, call, rd, wr, sem=None, inc=1):
+        marks = [wrote[k] for k in list(rd) + list(wr) if k in wrote]
+        for k in wr:
+            marks += read.get(k, [])
+        wait(q, marks)
+        s = sem or CNT[q]
+        call().then_inc(T.sem[s], inc)
+        total[s] = total.get(s, 0) + inc
+        mark = (s, total[s])
+        behind[mark] = dict(known[q])
+        for k in wr:
+            wrote[k] = mark
+            read[k] = []
+        for k in rd:
+            read.setdefault(k, []).append(mark)
+
+    def dma(q, out, in_, rd, wr, sem):
+        op(q, lambda: Q[q].dma_start(out, in_), rd, wr, sem, 16)
+
+    def ts(out, in0, s1, s2, o0, o1, rd, wr):
+        if o1 is None:
+            op("v", lambda: g.vector.tensor_scalar(out, in0, s1, None, o0), rd, wr)
+        else:
+            op("v", lambda: g.vector.tensor_scalar(out, in0, s1, s2, o0, o1), rd, wr)
+
+    def tt(out, in0, in1, o, rd, wr):
+        op("v", lambda: g.vector.tensor_tensor(out, in0, in1, o), rd, wr)
+
+    def cp(out, in_, rd, wr):
+        op("v", lambda: g.vector.tensor_copy(out, in_), rd, wr)
+
+    def act(out, in_, rd, wr, scale=None):
+        if scale is None:
+            op("s", lambda: g.scalar.activation(out, in_, COPY), rd, wr)
+        else:
+            op("s", lambda: g.scalar.activation(out, in_, COPY, scale=scale), rd, wr)
+
+    def move(q, out, in_, rd, wr):
+        (cp if q == "v" else act)(out, in_, rd, wr)
+
+    def quant(name, a, b, tile, rd, key=None):
+        k = key or name
+        op("v", lambda: g.vector.quantize_mx(T[name + "c"][:, a:b], T[name + "s"][:, a:b], tile), rd, [k + "c", k + "s"])
+
+    def mm(ps, b, lname, la, lkey, rname, start, stop):
+        op("p", lambda: g.tensor.matmul_mx(
+            T[ps][:, 512 * b:512 * b + C], T[lname + "c"][:, la:la + 128], T[lname + "s"][:, la:la + 128],
+            T[rname + "c"][:, 0:C], T[rname + "s"][:, 0:C], start, stop),
+            [lkey + "c", lkey + "s", rname + "c", rname + "s"], ["%s%d" % (ps, b)])
+
+    def unpack(ps, rname, start, stop):
+        for b in range(4):
+            mm(ps, b, "e", 128 * b, "e%d" % b, rname, start, stop)
+
+    def leave(ps, b, q, out, scale, key):
+        src = T[ps][:, 512 * b:512 * b + C]
+        if q == "s":
+            act(out, src, [], ["%s%d" % (ps, b), key], scale)
+        else:
+            ts(out, src, scale, None, A.mult, None, [], ["%s%d" % (ps, b), key])
+
+    def twin(q, buf, key):
+        move(q, buf[:, C:2 * C], buf[:, 0:C], [key], [key + "2"])
+
+    partners = [T.cores[rank ^ (1 << r)] for r in range(ROUNDS)]
+    engines = [e for e in topo.engines(core, partners[0]) if all(e in topo.engines(core, c) for c in partners)]
+    mask = sum(1 << e for e in engines)
+
+    def send(r, out, in_, rd, sem, key):
+        wait("g", [wrote[k] for k in rd])
+        rid, pid, _ = topo.addr(partners[r])
+        g.remote_dma(out, in_, T.sem[sem], T.sem.snd, pid, rid, mask)
+        total["snd"] = total.get("snd", 0) + len(engines)
+        total[sem] = len(engines)
+        wrote[key] = (sem, len(engines))
+
+    def partner_lists(r):
+        lp = T["lp%d" % r]
+        cp(T["pp%d" % r][:, 0:16], lp[:, 0:16], ["lp%d" % r], ["pp%d" % r])
+        tt(T.sm[:, 0:16], lp[:, 0:16], T.jw[:, 0:16], A.min, ["lp%d" % r, "jw"], ["sm0"])
+        cp(T.lou[:, 0:16], T.sm[:, 0:16], ["sm0"], ["lou"])
+
+    def towards_partner(r):
+        lp = T["lp%d" % r]
+        tt(T.sm[:, 16:32], lp[:, 0:16], T["w%d" % r][:, 0:16], A.subtract, ["lp%d" % r, "wa%d" % r], ["sm1"])
+        ts(T.sm[:, 112:128], lp[:, 0:16], 1.0, None, A.add, None, ["lp%d" % r], ["sm7"])
+
+    def least_ends():
+        act(T.low[:, 0:C], T.iota[:, 0:C].indirect(T.lou[:, 0:16]), ["iota", "lou"], ["low"], TINY)
+
+    def tie_break(r, copy=True):
+        if copy:
+            twin("v", T.low, "low")
+        tt(T.tdf[:, 0:C], T.low[:, 0:C].indirect(T["off%d" % r][:, 0:16]), T.low[:, C:2 * C], A.subtract, ["low", "low2", "off%d" % r], ["tdf"])
+
+    dma("y", T.mi[:], T.m[:], [], ["mi"], "ldm")
+    dma("y", T.xin[:], T.x[:], [], ["xin"], "ldx")
+    dma("y", T.uin[:], T.u[:], [], ["uin"], "ldu")
+    op("g", lambda: g.iota(T.ia[:, 0:17], [[-1, 17]], 16, 1), [], ["ia"])
+    op("g", lambda: g.iota(T.iota[:], [[1, C]], 0, 0, allow_small_or_imprecise_dtypes=True), [], ["iota"])
+    send(0, T.lp0[:], T.mi[:], ["mi"], "ap0", "lp0")
+    op("v", lambda: g.vector.memset(T.tt[:], 0.0), [], ["tt"])
+    op("v", lambda: g.vector.memset(T.fp[:, 0:4 * FW:FW], 0.0), [], ["fpz"])
+    PCOL, PM, CC = [T.cols[:, i:i + 1] for i in range(3)]
+    cp(PCOL, T.ia[:, 16:17], ["ia"], ["pcol"])
+    ts(T.ib[:, 0:16], T.ia[:, 0:16], 15, None, A.bitwise_and, None, ["ia"], ["ib"])
+    cp(PM, T.ib[:, 0:1], ["ib"], ["pm"])
+    ts(CC, T.ib[:, 0:1], 15.0, 256.0, A.not_equal, A.mult, ["ib"], ["cc"])
+    ts(T.e01[:, 0:16], T.ib[:, 0:16], 0.0, 512.0, A.is_equal, A.mult, ["ib"], ["e0"])
+    ts(T.e01[:, 16:32], T.ib[:, 0:16], 15.0, -256.0, A.is_equal, A.mult, ["ib"], ["e1"])
+    tt(T.c16[:, 0:16], T.e01[:, 0:16], T.e01[:, 16:32], A.add, ["e0", "e1"], ["c16"])
+    ts(T.tt[:, 3:515:4], T.iota[:, 0:128], PCOL, 32.0, A.is_equal, A.mult, ["iota", "pcol"], ["tt"])
+    ts(T.poff[:, 0:32], T.iota[:, 0:32], 0.0, PM, A.mult, A.add, ["iota", "pm"], ["poff"])
+    cp(T.uoff[:, 0:8], T.iota[:, 0:128:16], ["iota"], ["uoff"])
+    ts(T.jw[:, 0:16], T.iota[:, 0:C:16], PM, None, A.add, None, ["iota", "pm"], ["jw"])
+    ts(T.jw[:, 16:32], T.iota[:, 0:C:16], PM, 1.0, A.add, A.add, ["iota", "pm"], ["jw1"])
+    act(T.cw[:, 0:512], T.c16[:, 0:16].indirect(T.poff[:, 0:32]), ["c16", "poff"], ["cw"])
+    for b in range(4):
+        quant("e", 128 * b, 128 * b + 128, T.tt[:, 3 - b:515 - b], ["tt"], "e%d" % b)
+    cp(T.off0[:, 0:16], T.mi[:, 0:16], ["mi"], ["off0"])
+    cp(T.w0[:, 0:16], T.mi[:, 0:16], ["mi"], ["wa0"])
+    act(T.ofr[:, 0:C], T.iota[:, 0:C].indirect(T.off0[:, 0:16]), ["iota", "off0"], ["ofr"])
+
+    for r in range(ROUNDS):
+        qx, lx, qa, qz = ["%s%d" % (n, r) for n in ("qx", "lx", "qa", "qz")]
+        noff, nkey = T["off%d" % (r + 1)], "off%d" % (r + 1)
+        ou, ouk = T["off%d" % r][:, 0:16], "off%d" % r
+        pp, ppk = T["pp%d" % r][:, 0:16], "pp%d" % r
+        w, wn = T["w%d" % r], T["w%d" % (r + 1)]
+        last = r + 1 == ROUNDS
+
+        def mates_of(bs):
+            for b in bs:
+                act(T.fo[:, C * b:C * b + C], T.fh[:, C * b:C * b + C].indirect(ou), ["fh%d" % b, ouk], ["fo%d" % b])
+
+        def twice_over():
+            act(T.opf[:, 0:C], T.ofr[:, 0:C].indirect(pp), ["ofr", ppk], ["opf"])
+            act(T.apo[:, C:2 * C], T.opf[:, 0:C].indirect(ou), ["opf", ouk], ["opo"])
+
+        if r == 0:
+            quant(qx, 0, C, T.xin[:], ["xin"])
+        else:
+            quant(qx, 0, C, T.xt[:], ["xt0", "xt1", "xt2", "xt3"])
+        send(r, T[lx + "c"][:].bitcast(dt.uint8), T[qx + "c"][:].bitcast(dt.uint8), [qx + "c"], "ac%d" % r, lx + "c")
+        send(r, T[lx + "s"][:], T[qx + "s"][:], [qx + "s"], "as%d" % r, lx + "s")
+        if r == 0:
+            unpack("PA", qx, True, True)
+            quant("qu", 0, 128, T.uin[:], ["uin"])
+            cp(T.puc[:, 0:128].bitcast(dt.uint32), T.quc[:, 0:128].bitcast(dt.uint32).indirect(T.uoff[:, 0:8]), ["quc", "uoff"], ["puc"])
+            act(T.pus[:, 0:128], T.qus[:, 0:128].indirect(T.uoff[:, 0:8]), ["qus", "uoff"], ["pus"])
+            mm("PB", 0, "pu", 0, "pu", qx, True, True)
+        else:
+            mm("PB", 0, "pu", 0, "pu", qx, True, True)
+            if OPT["two"]:
+                mm("PB", 1, "pu", 0, "pu", qx, True, True)
+            unpack("PA", qx, True, True)
+        act(T.sc[:, 0:C], T.PB[:, 0:C], [], ["PB0", "sc"])
+        if r > 0 and not OPT["two"]:
+            tie_break(r)
+        if r > 0 and OPT["two"]:
+            twin("v", T.low, "low")
+            cp(T.sc[:, C:2 * C], T.PB[:, 512:512 + C], [], ["PB1", "sc2"])
+        else:
+            move(OPT["sc2"], T.sc[:, C:2 * C], T.PB[:, 0:C], [], ["PB0", "sc2"])
+        late = OPT["two"] if r > 0 else 0
+        for b in range(4 - late):
+            leave("PA", b, "sv"[b % 2] if r == 0 else OPT["f"][b], T.fh[:, C * b:C * b + C], 2.0 ** -6, "fh%d" % b)
+        if r == 0:
+            mates_of(range(4))
+            partner_lists(0)
+            least_ends()
+            wait("y", [wrote["lp0"]])
+            dma("y", T.qwc[:].bitcast(dt.uint8), T.wc[:], [], ["qwc"], "ldw")
+            dma("y", T.qws[:], T.ws[:], [], ["qws"], "lds")
+            dma("y", T.vin[:], T.v[:], [], ["vin"], "ldv")
+        tt(T.val[:, 0:C], T.sc[:, 0:C].indirect(pp), T.sc[:, C:2 * C], A.max, ["sc", "sc2", ppk], ["val"])
+        twin("s" if r == 0 else OPT["val2"], T.val, "val")
+        if r == 0:
+            tie_break(0)
+        elif OPT["two"]:
+            tie_break(r, False)
+        for b in range(4 - late, 4):
+            leave("PA", b, OPT["f"][b], T.fh[:, C * b:C * b + C], 2.0 ** -6, "fh%d" % b)
+        unpack("PA", qx, True, False)
+        twice_over()
+        if r > 0:
+            mates_of(range(OPT["m1"]))
+        tt(T.dif[:, 0:C], T.val[:, 0:C].indirect(ou), T.val[:, C:2 * C], A.subtract, ["val", "val2", ouk], ["dif"])
+        tt(T.bts[:, 0:C], T.dif[:, 0:C], T.tdf[:, 0:C], A.is_lt, ["dif", "tdf"], ["bts"])
+        twin("v", T.bts, "bts")
+        tt(T.apo[:, 0:C], T.bts[:, 0:C].indirect(pp), T.bts[:, C:2 * C], A.mult, ["bts", "bts2", ppk], ["app"])
+        act(T.aof[:, 0:C], T.apo[:, 0:C].indirect(ou), ["app", ouk], ["aof"])
+        if r > 0:
+            mates_of(range(OPT["m1"], 4))
+        if r == 0:
+            towards_partner(0)
+        op("v", lambda: g.vector.tensor_tensor_scan(T.r1[:, 0:2 * C], T.cw[:, 0:2 * C], T.apo[:, 0:2 * C], 0.0, A.add, A.min), ["cw", "app", "opo"], ["r1"])
+        ts(T.aw[:, 0:32], T.r1[:, 15:2 * C:16], CC, None, A.add, None, ["r1", "cc"], ["aw"])
+        tt(T.sm[:, 32:48], T.aw[:, 0:16], T.sm[:, 16:32], A.mult, ["aw", "sm1"], ["sm2"])
+        tt(T.sm[:, 64:80], T.aw[:, 16:32], w[:, 0:16], A.subtract, ["aw", "wa%d" % r], ["sm4"])
+        op("v", lambda: g.vector.tensor_tensor_scan(T.r2[:, 0:C], T.cw[:, 0:C], T.aof[:, 0:C], 0.0, A.add, A.min), ["cw", "aof"], ["r2"])
+        tt(T.sm[:, 48:64], T.sm[:, 32:48], w[:, 0:16], A.add, ["sm2", "wa%d" % r], ["sm3"])
+        ts(T.sm[:, 80:96], T.r2[:, 15:C:16], CC, None, A.add, None, ["r2", "cc"], ["sm5"])
+        tt(wn[:, 16:32], T.aw[:, 0:16], T.jw[:, 16:32], A.mult, ["aw", "jw1"], ["wb%d" % (r + 1)])
+        tt(T.sm[:, 96:112], T.sm[:, 80:96], T.sm[:, 64:80], A.mult, ["sm5", "sm4"], ["sm6"])
+        tt(wn[:, 32:48], T.aw[:, 0:16], T.sm[:, 112:128], A.mult, ["aw", "sm7"], ["wc%d" % (r + 1)])
+        tt(wn[:, 0:16], T.sm[:, 96:112], T.sm[:, 48:64], A.add, ["sm6", "sm3"], ["wa%d" % (r + 1)])
+        if not last:
+            send(r + 1, T["lp%d" % (r + 1)][:], wn[:, 0:16], ["wa%d" % (r + 1)], "ap%d" % (r + 1), "lp%d" % (r + 1))
+        cp(noff[:, 0:48], wn[:, 0:48], ["w%s%d" % (k, r + 1) for k in "abc"], [nkey])
+        for b in range(4):
+            tt(T.zt[:, b:4 * C:4], T.fh[:, C * b:C * b + C].indirect(noff[:, 0:16]), T.fo[:, C * b:C * b + C], A.add, ["fh%d" % b, "fo%d" % b, nkey], ["zt%d" % b])
+        quant(qz, 0, C, T.zt[:], ["zt0", "zt1", "zt2", "zt3"])
+        unpack("PB", lx, True, True)
+        for b in range(4):
+            mm("PA", b, "qw", 128 * b, "qw", qz, False, False)
+        for b in range(4):
+            win = T.fp[:, FW * b:FW * b + C + 1]
+            for k in OPT["fpo"][b]:
+                leave("PB", k, OPT["fp"][k], T.fp[:, FW * k + 1:FW * k + C + 1], 2.0 ** -6, "fp%d" % k)
+            move(OPT["ta"][b], T.fa[:, C * b:C * b + C], win.indirect(noff[:, 16:32]), ["fp%d" % b, "fpz", nkey], ["fa%d" % b])
+            tt(T.at[:, b:4 * C:4], win.indirect(noff[:, 32:48]), T.fa[:, C * b:C * b + C], A.add, ["fp%d" % b, "fpz", "fa%d" % b, nkey], ["at%d" % b])
+        quant(qa, 0, C, T.at[:], ["at0", "at1", "at2", "at3"])
+        unpack("PA", qa, False, True)
+        if not last:
+            act(T.ofr[:, 0:C], T.iota[:, 0:C].indirect(noff[:, 0:16]), ["iota", nkey], ["ofr"])
+            partner_lists(r + 1)
+            towards_partner(r + 1)
+        else:
+            quant("qv", 0, 128, T.vin[:], ["vin"])
+            act(T.omf[:, 0:C], T.iota[:, 0:C].indirect(noff[:, 0:16]), ["iota", nkey], ["omf"])
+            for k in range(8):
+                dma("y", T.om[k:k + 1, :], T.omf[16 * k:16 * k + 1, :], ["omf"], [], "st1")
+        for b in range(4):
+            leave("PA", b, OPT["x"][b], T.xt[:, b:4 * C:4], 2.0 ** -5, "xt%d" % b)
+        if not last:
+            least_ends()
+
+    qx = "qx%d" % ROUNDS
+    quant(qx, 0, C, T.xt[:], ["xt0", "xt1", "xt2", "xt3"])
+    mm("PB", 0, "qv", 0, "qv", qx, True, True)
+    dma("y", T.oc[:], T[qx + "c"][:].bitcast(dt.uint8), [qx + "c"], [], "st1")
+    for k in range(4):
+        dma("ys"[k // 2], T.osc[4 * k:4 * k + 4, :], T[qx + "s"][32 * k:32 * k + 4, :], [qx + "s"], [], ["st1", "st2"][k // 2])
+    cp(T.ysb[:, 0:C], T.PB[:, 0:C], [], ["PB0", "ysb"])
+    dma("s", T.y[:], T.ysb[:], ["ysb"], [], "st2")
+    for s in sorted(total):
+        if waited.get(s, 0) < total[s]:
+            g.wait_ge(T.sem[s], total[s])

@@ -1,10 +1,10 @@
 from concourse.mybir import dt, AluOpType, ActivationFunctionType
 
 C = 256
+H = C // 2
 FW = 272
 ROUNDS = 3
 TINY = 2.0 ** -118
-OPT = dict(val2="v", sc2="v", fp="ssss", x="svsv", f="ssss", ta="ssss", two=0, fpo=[[0, 1], [2], [3], []], m1=2)
 
 SCRATCH = {
     "PA": ("psum", [128, 2048], "float32"),
@@ -13,6 +13,7 @@ SCRATCH = {
     "uin": ("sbuf", [128, 512], "bfloat16"),
     "vin": ("sbuf", [128, 512], "bfloat16"),
     "mi": ("sbuf", [128, 16], "int32"),
+    "lp0": ("sbuf", [128, 16], "int32"),
     "xt": ("sbuf", [128, 4 * C], "bfloat16"),
     "zt": ("sbuf", [128, 4 * C], "bfloat16"),
     "at": ("sbuf", [128, 4 * C], "bfloat16"),
@@ -45,8 +46,7 @@ SCRATCH = {
     "r1": ("sbuf", [128, 2 * C], "bfloat16"),
     "r2": ("sbuf", [128, C], "bfloat16"),
     "aw": ("sbuf", [128, 32], "float32"),
-    "sm": ("sbuf", [128, 128], "float32"),
-    "lou": ("sbuf", [128, 16], "uint16"),
+    "sm": ("sbuf", [128, 144], "float32"),
     "ysb": ("sbuf", [128, C], "float32"),
 }
 
@@ -63,14 +63,13 @@ _pair("qv", 128)
 _pair("qw", 512)
 for _r in range(ROUNDS + 1):
     _pair("qx%d" % _r, C)
-    SCRATCH["w%d" % _r] = ("sbuf", [128, 48], "float32")
-    SCRATCH["off%d" % _r] = ("sbuf", [128, 48], "uint16")
+    SCRATCH["w%d" % _r] = ("sbuf", [128, 64], "float32")
+    SCRATCH["off%d" % _r] = ("sbuf", [128, 64], "uint16")
 for _r in range(ROUNDS):
     _pair("lx%d" % _r, C)
     _pair("qa%d" % _r, C)
     _pair("qz%d" % _r, C)
-    SCRATCH["lp%d" % _r] = ("sbuf", [128, 16], "int32" if _r == 0 else "float32")
-    SCRATCH["pp%d" % _r] = ("sbuf", [128, 16], "uint16")
+    SCRATCH["pp%d" % _r] = ("sbuf", [128, 32], "uint16")
 
 SEMAPHORES = ["cv", "cs", "cp", "cg", "snd", "ldm", "ldx", "ldu", "ldw", "lds", "ldv", "st1", "st2"]
 for _r in range(ROUNDS):
@@ -146,67 +145,60 @@ def rank_program(g, core, T, topo):
         else:
             op("s", lambda: g.scalar.activation(out, in_, COPY, scale=scale), rd, wr)
 
-    def move(q, out, in_, rd, wr):
-        (cp if q == "v" else act)(out, in_, rd, wr)
+    def quant(name, a, b, tile, rd, keys):
+        op("v", lambda: g.vector.quantize_mx(T[name + "c"][:, a:b], T[name + "s"][:, a:b], tile), rd, [k + e for k in keys for e in "cs"])
 
-    def quant(name, a, b, tile, rd, key=None):
-        k = key or name
-        op("v", lambda: g.vector.quantize_mx(T[name + "c"][:, a:b], T[name + "s"][:, a:b], tile), rd, [k + "c", k + "s"])
-
-    def mm(ps, b, lname, la, lkey, rname, start, stop):
+    def mm(ps, b, lname, la, lkey, rname, start, stop, h=None):
+        a, n = (0, C) if h is None else (H * h, H)
         op("p", lambda: g.tensor.matmul_mx(
-            T[ps][:, 512 * b:512 * b + C], T[lname + "c"][:, la:la + 128], T[lname + "s"][:, la:la + 128],
-            T[rname + "c"][:, 0:C], T[rname + "s"][:, 0:C], start, stop),
-            [lkey + "c", lkey + "s", rname + "c", rname + "s"], ["%s%d" % (ps, b)])
+            T[ps][:, 512 * b:512 * b + n], T[lname + "c"][:, la:la + 128], T[lname + "s"][:, la:la + 128],
+            T[rname + "c"][:, a:a + n], T[rname + "s"][:, a:a + n], start, stop),
+            [lkey + "c", lkey + "s"] + ["%s%d%s" % (rname, k, e) for k in ((0, 1) if h is None else (h,)) for e in "cs"], ["%s%d" % (ps, b)])
 
-    def unpack(ps, rname, start, stop):
+    def unpack(ps, rname, start, stop, h=None):
         for b in range(4):
-            mm(ps, b, "e", 128 * b, "e%d" % b, rname, start, stop)
+            mm(ps, b, "e", 128 * b, "e%d" % b, rname, start, stop, h)
 
-    def leave(ps, b, q, out, scale, key):
-        src = T[ps][:, 512 * b:512 * b + C]
+    def leave(ps, b, q, out, scale, key, n=C):
+        src = T[ps][:, 512 * b:512 * b + n]
         if q == "s":
             act(out, src, [], ["%s%d" % (ps, b), key], scale)
         else:
             ts(out, src, scale, None, A.mult, None, [], ["%s%d" % (ps, b), key])
 
     def twin(q, buf, key):
-        move(q, buf[:, C:2 * C], buf[:, 0:C], [key], [key + "2"])
+        (cp if q == "v" else act)(buf[:, C:2 * C], buf[:, 0:C], [key], [key + "2"])
 
     partners = [T.cores[rank ^ (1 << r)] for r in range(ROUNDS)]
-    engines = [e for e in topo.engines(core, partners[0]) if all(e in topo.engines(core, c) for c in partners)]
-    mask = sum(1 << e for e in engines)
+    common = [e for e in topo.engines(core, partners[0]) if all(e in topo.engines(core, c) for c in partners)]
 
-    def send(r, out, in_, rd, sem, key):
+    def send(r, out, in_, rd, sem, *keys):
+        engines = common if sem.startswith("ap") else topo.engines(core, partners[r])
+        mask = sum(1 << e for e in engines)
         wait("g", [wrote[k] for k in rd])
         rid, pid, _ = topo.addr(partners[r])
         g.remote_dma(out, in_, T.sem[sem], T.sem.snd, pid, rid, mask)
         total["snd"] = total.get("snd", 0) + len(engines)
         total[sem] = len(engines)
-        wrote[key] = (sem, len(engines))
+        for key in keys:
+            wrote[key] = (sem, len(engines))
 
-    def partner_lists(r):
-        lp = T["lp%d" % r]
-        cp(T["pp%d" % r][:, 0:16], lp[:, 0:16], ["lp%d" % r], ["pp%d" % r])
-        tt(T.sm[:, 0:16], lp[:, 0:16], T.jw[:, 0:16], A.min, ["lp%d" % r, "jw"], ["sm0"])
-        cp(T.lou[:, 0:16], T.sm[:, 0:16], ["sm0"], ["lou"])
+    def scores(name, h):
+        for b in (0, 1):
+            mm(["PA", "PB"][h], b + 2 - 2 * h, "pu", 0, "pu", name, True, True, h)
 
-    def towards_partner(r):
-        lp = T["lp%d" % r]
-        tt(T.sm[:, 16:32], lp[:, 0:16], T["w%d" % r][:, 0:16], A.subtract, ["lp%d" % r, "wa%d" % r], ["sm1"])
-        ts(T.sm[:, 112:128], lp[:, 0:16], 1.0, None, A.add, None, ["lp%d" % r], ["sm7"])
+    def scores_out(h):
+        ps, b = ["PA", "PB"][h], 2 - 2 * h
+        cp(T.sc[:, C + H * h:C + H * h + H], T[ps][:, 512 * b:512 * b + H], [], ["%s%d" % (ps, b), "sc2%d" % h])
+        act(T.sc[:, H * h:H * h + H], T[ps][:, 512 * b + 512:512 * b + 512 + H], [], ["%s%d" % (ps, b + 1), "sc%d" % h])
 
-    def least_ends():
-        act(T.low[:, 0:C], T.iota[:, 0:C].indirect(T.lou[:, 0:16]), ["iota", "lou"], ["low"], TINY)
-
-    def tie_break(r, copy=True):
-        if copy:
-            twin("v", T.low, "low")
-        tt(T.tdf[:, 0:C], T.low[:, 0:C].indirect(T["off%d" % r][:, 0:16]), T.low[:, C:2 * C], A.subtract, ["low", "low2", "off%d" % r], ["tdf"])
+    def least_ends(r):
+        act(T.low[:, 0:C], T.iota[:, 0:C].indirect(T["pp%d" % r][:, 0:16]), ["iota", "pl%d" % r], ["low"], TINY)
 
     dma("y", T.mi[:], T.m[:], [], ["mi"], "ldm")
     dma("y", T.xin[:], T.x[:], [], ["xin"], "ldx")
     dma("y", T.uin[:], T.u[:], [], ["uin"], "ldu")
+    dma("y", T.vin[:], T.v[:], [], ["vin"], "ldv")
     op("g", lambda: g.iota(T.ia[:, 0:17], [[-1, 17]], 16, 1), [], ["ia"])
     op("g", lambda: g.iota(T.iota[:], [[1, C]], 0, 0, allow_small_or_imprecise_dtypes=True), [], ["iota"])
     send(0, T.lp0[:], T.mi[:], ["mi"], "ap0", "lp0")
@@ -227,134 +219,160 @@ def rank_program(g, core, T, topo):
     ts(T.jw[:, 16:32], T.iota[:, 0:C:16], PM, 1.0, A.add, A.add, ["iota", "pm"], ["jw1"])
     act(T.cw[:, 0:512], T.c16[:, 0:16].indirect(T.poff[:, 0:32]), ["c16", "poff"], ["cw"])
     for b in range(4):
-        quant("e", 128 * b, 128 * b + 128, T.tt[:, 3 - b:515 - b], ["tt"], "e%d" % b)
-    cp(T.off0[:, 0:16], T.mi[:, 0:16], ["mi"], ["off0"])
-    cp(T.w0[:, 0:16], T.mi[:, 0:16], ["mi"], ["wa0"])
-    act(T.ofr[:, 0:C], T.iota[:, 0:C].indirect(T.off0[:, 0:16]), ["iota", "off0"], ["ofr"])
+        quant("e", 128 * b, 128 * b + 128, T.tt[:, 3 - b:515 - b], ["tt"], ["e%d" % b])
+    cp(T.off0[:, 16:32], T.mi[:, 0:16], ["mi"], ["off0"])
+    cp(T.w0[:, 16:32], T.mi[:, 0:16], ["mi"], ["wa0"])
+    act(T.ofr[:, 0:C], T.iota[:, 0:C].indirect(T.off0[:, 16:32]), ["iota", "off0"], ["ofr"])
 
     for r in range(ROUNDS):
-        qx, lx, qa, qz = ["%s%d" % (n, r) for n in ("qx", "lx", "qa", "qz")]
+        qx, lx, qa, qz, nx = ["%s%d" % (n, r) for n in ("qx", "lx", "qa", "qz")] + ["qx%d" % (r + 1)]
         noff, nkey = T["off%d" % (r + 1)], "off%d" % (r + 1)
-        ou, ouk = T["off%d" % r][:, 0:16], "off%d" % r
-        pp, ppk = T["pp%d" % r][:, 0:16], "pp%d" % r
-        w, wn = T["w%d" % r], T["w%d" % (r + 1)]
+        ou, ouk = T["off%d" % r][:, 16:32], "off%d" % r
+        pp, ppk = T["pp%d" % r][:, 16:32], "pp%d" % r
+        w, wn = T["w%d" % r][:, 16:32], T["w%d" % (r + 1)]
+        wk = "wa%d" % r
         last = r + 1 == ROUNDS
+
+        def halves(bs, who):
+            for b in bs:
+                leave("PA", b, who[b], T.fh[:, C * b:C * b + C], 2.0 ** -6, "fh%d" % b)
 
         def mates_of(bs):
             for b in bs:
                 act(T.fo[:, C * b:C * b + C], T.fh[:, C * b:C * b + C].indirect(ou), ["fh%d" % b, ouk], ["fo%d" % b])
 
-        def twice_over():
-            act(T.opf[:, 0:C], T.ofr[:, 0:C].indirect(pp), ["ofr", ppk], ["opf"])
-            act(T.apo[:, C:2 * C], T.opf[:, 0:C].indirect(ou), ["opf", ouk], ["opo"])
-
         if r == 0:
-            quant(qx, 0, C, T.xin[:], ["xin"])
-        else:
-            quant(qx, 0, C, T.xt[:], ["xt0", "xt1", "xt2", "xt3"])
-        send(r, T[lx + "c"][:].bitcast(dt.uint8), T[qx + "c"][:].bitcast(dt.uint8), [qx + "c"], "ac%d" % r, lx + "c")
-        send(r, T[lx + "s"][:], T[qx + "s"][:], [qx + "s"], "as%d" % r, lx + "s")
+            quant(qx, 0, C, T.xin[:], ["xin"], [qx + "0", qx + "1"])
+        send(r, T[lx + "c"][:].bitcast(dt.uint8), T[qx + "c"][:].bitcast(dt.uint8), [qx + "0c", qx + "1c"], "ac%d" % r, lx + "0c", lx + "1c")
+        send(r, T[lx + "s"][:], T[qx + "s"][:], [qx + "0s", qx + "1s"], "as%d" % r, lx + "0s", lx + "1s")
         if r == 0:
             unpack("PA", qx, True, True)
-            quant("qu", 0, 128, T.uin[:], ["uin"])
+            quant("qu", 0, 128, T.uin[:], ["uin"], ["qu"])
             cp(T.puc[:, 0:128].bitcast(dt.uint32), T.quc[:, 0:128].bitcast(dt.uint32).indirect(T.uoff[:, 0:8]), ["quc", "uoff"], ["puc"])
             act(T.pus[:, 0:128], T.qus[:, 0:128].indirect(T.uoff[:, 0:8]), ["qus", "uoff"], ["pus"])
             mm("PB", 0, "pu", 0, "pu", qx, True, True)
-        else:
-            mm("PB", 0, "pu", 0, "pu", qx, True, True)
-            if OPT["two"]:
-                mm("PB", 1, "pu", 0, "pu", qx, True, True)
-            unpack("PA", qx, True, True)
-        act(T.sc[:, 0:C], T.PB[:, 0:C], [], ["PB0", "sc"])
-        if r > 0 and not OPT["two"]:
-            tie_break(r)
-        if r > 0 and OPT["two"]:
-            twin("v", T.low, "low")
-            cp(T.sc[:, C:2 * C], T.PB[:, 512:512 + C], [], ["PB1", "sc2"])
-        else:
-            move(OPT["sc2"], T.sc[:, C:2 * C], T.PB[:, 0:C], [], ["PB0", "sc2"])
-        late = OPT["two"] if r > 0 else 0
-        for b in range(4 - late):
-            leave("PA", b, "sv"[b % 2] if r == 0 else OPT["f"][b], T.fh[:, C * b:C * b + C], 2.0 ** -6, "fh%d" % b)
-        if r == 0:
-            mates_of(range(4))
-            partner_lists(0)
-            least_ends()
+            act(T.sc[:, 0:C], T.PB[:, 0:C], [], ["PB0", "sc0", "sc1"])
+            cp(T.sc[:, C:2 * C], T.PB[:, 0:C], [], ["PB0", "sc20", "sc21"])
+            halves(range(4), "svsv")
+            mates_of((0, 1))
+            quant("qv", 0, 128, T.vin[:], ["vin"], ["qv"])
+            tt(T.sm[:, 128:144], T.lp0[:, 0:16], T.jw[:, 0:16], A.min, ["lp0", "jw"], ["sm8"])
+            cp(T.pp0[:, 16:32], T.lp0[:, 0:16], ["lp0"], ["pp0"])
+            cp(T.pp0[:, 0:16], T.sm[:, 128:144], ["sm8"], ["pl0"])
+            least_ends(0)
             wait("y", [wrote["lp0"]])
             dma("y", T.qwc[:].bitcast(dt.uint8), T.wc[:], [], ["qwc"], "ldw")
             dma("y", T.qws[:], T.ws[:], [], ["qws"], "lds")
-            dma("y", T.vin[:], T.v[:], [], ["vin"], "ldv")
-        tt(T.val[:, 0:C], T.sc[:, 0:C].indirect(pp), T.sc[:, C:2 * C], A.max, ["sc", "sc2", ppk], ["val"])
-        twin("s" if r == 0 else OPT["val2"], T.val, "val")
+        else:
+            scores_out(1)
+            unpack("PA", qx, True, True)
+            halves((0, 1), "ssss")
+
+        tt(T.val[:, 0:C], T.sc[:, 0:C].indirect(pp), T.sc[:, C:2 * C], A.max, ["sc0", "sc1", "sc20", "sc21", ppk], ["val"])
+        twin("s", T.val, "val")
         if r == 0:
-            tie_break(0)
-        elif OPT["two"]:
-            tie_break(r, False)
-        for b in range(4 - late, 4):
-            leave("PA", b, OPT["f"][b], T.fh[:, C * b:C * b + C], 2.0 ** -6, "fh%d" % b)
-        unpack("PA", qx, True, False)
-        twice_over()
+            twin("v", T.low, "low")
+        tt(T.tdf[:, 0:C], T.low[:, 0:C].indirect(ou), T.low[:, C:2 * C], A.subtract, ["low", "low2", ouk], ["tdf"])
         if r > 0:
-            mates_of(range(OPT["m1"]))
+            halves((2, 3), "ssss")
+        unpack("PA", qx, True, False, 0)
+        if r == 0:
+            act(T.opf[:, 0:C], T.ofr[:, 0:C].indirect(pp), ["ofr", ppk], ["opf"])
+        act(T.apo[:, C:2 * C], T.opf[:, 0:C].indirect(ou), ["opf", ouk], ["opo"])
+        mates_of((0, 1) if r > 0 else (2,))
         tt(T.dif[:, 0:C], T.val[:, 0:C].indirect(ou), T.val[:, C:2 * C], A.subtract, ["val", "val2", ouk], ["dif"])
+        cp(T.sm[:, 0:16], pp, [ppk], ["sm0"])
         tt(T.bts[:, 0:C], T.dif[:, 0:C], T.tdf[:, 0:C], A.is_lt, ["dif", "tdf"], ["bts"])
+        tt(T.sm[:, 16:32], T.sm[:, 0:16], w, A.subtract, ["sm0", wk], ["sm1"])
         twin("v", T.bts, "bts")
         tt(T.apo[:, 0:C], T.bts[:, 0:C].indirect(pp), T.bts[:, C:2 * C], A.mult, ["bts", "bts2", ppk], ["app"])
         act(T.aof[:, 0:C], T.apo[:, 0:C].indirect(ou), ["app", ouk], ["aof"])
-        if r > 0:
-            mates_of(range(OPT["m1"], 4))
-        if r == 0:
-            towards_partner(0)
+        mates_of((2, 3) if r > 0 else (3,))
+
+        ts(T.sm[:, 112:128], pp, 1.0, None, A.add, None, [ppk], ["sm7"])
         op("v", lambda: g.vector.tensor_tensor_scan(T.r1[:, 0:2 * C], T.cw[:, 0:2 * C], T.apo[:, 0:2 * C], 0.0, A.add, A.min), ["cw", "app", "opo"], ["r1"])
         ts(T.aw[:, 0:32], T.r1[:, 15:2 * C:16], CC, None, A.add, None, ["r1", "cc"], ["aw"])
+        tt(T.sm[:, 64:80], T.aw[:, 16:32], w, A.subtract, ["aw", wk], ["sm4"])
         tt(T.sm[:, 32:48], T.aw[:, 0:16], T.sm[:, 16:32], A.mult, ["aw", "sm1"], ["sm2"])
-        tt(T.sm[:, 64:80], T.aw[:, 16:32], w[:, 0:16], A.subtract, ["aw", "wa%d" % r], ["sm4"])
         op("v", lambda: g.vector.tensor_tensor_scan(T.r2[:, 0:C], T.cw[:, 0:C], T.aof[:, 0:C], 0.0, A.add, A.min), ["cw", "aof"], ["r2"])
-        tt(T.sm[:, 48:64], T.sm[:, 32:48], w[:, 0:16], A.add, ["sm2", "wa%d" % r], ["sm3"])
+        tt(T.sm[:, 48:64], T.sm[:, 32:48], w, A.add, ["sm2", wk], ["sm3"])
         ts(T.sm[:, 80:96], T.r2[:, 15:C:16], CC, None, A.add, None, ["r2", "cc"], ["sm5"])
-        tt(wn[:, 16:32], T.aw[:, 0:16], T.jw[:, 16:32], A.mult, ["aw", "jw1"], ["wb%d" % (r + 1)])
+        tt(wn[:, 32:48], T.aw[:, 0:16], T.jw[:, 16:32], A.mult, ["aw", "jw1"], ["wb%d" % (r + 1)])
         tt(T.sm[:, 96:112], T.sm[:, 80:96], T.sm[:, 64:80], A.mult, ["sm5", "sm4"], ["sm6"])
-        tt(wn[:, 32:48], T.aw[:, 0:16], T.sm[:, 112:128], A.mult, ["aw", "sm7"], ["wc%d" % (r + 1)])
-        tt(wn[:, 0:16], T.sm[:, 96:112], T.sm[:, 48:64], A.add, ["sm6", "sm3"], ["wa%d" % (r + 1)])
+        tt(wn[:, 48:64], T.aw[:, 0:16], T.sm[:, 112:128], A.mult, ["aw", "sm7"], ["wc%d" % (r + 1)])
+        tt(wn[:, 16:32], T.sm[:, 96:112], T.sm[:, 48:64], A.add, ["sm6", "sm3"], ["wa%d" % (r + 1)])
+        cp(noff[:, 16:64], wn[:, 16:64], ["w%s%d" % (k, r + 1) for k in "abc"], [nkey])
         if not last:
-            send(r + 1, T["lp%d" % (r + 1)][:], wn[:, 0:16], ["wa%d" % (r + 1)], "ap%d" % (r + 1), "lp%d" % (r + 1))
-        cp(noff[:, 0:48], wn[:, 0:48], ["w%s%d" % (k, r + 1) for k in "abc"], [nkey])
-        for b in range(4):
-            tt(T.zt[:, b:4 * C:4], T.fh[:, C * b:C * b + C].indirect(noff[:, 0:16]), T.fo[:, C * b:C * b + C], A.add, ["fh%d" % b, "fo%d" % b, nkey], ["zt%d" % b])
-        quant(qz, 0, C, T.zt[:], ["zt0", "zt1", "zt2", "zt3"])
-        unpack("PB", lx, True, True)
-        for b in range(4):
-            mm("PA", b, "qw", 128 * b, "qw", qz, False, False)
-        for b in range(4):
-            win = T.fp[:, FW * b:FW * b + C + 1]
-            for k in OPT["fpo"][b]:
-                leave("PB", k, OPT["fp"][k], T.fp[:, FW * k + 1:FW * k + C + 1], 2.0 ** -6, "fp%d" % k)
-            move(OPT["ta"][b], T.fa[:, C * b:C * b + C], win.indirect(noff[:, 16:32]), ["fp%d" % b, "fpz", nkey], ["fa%d" % b])
-            tt(T.at[:, b:4 * C:4], win.indirect(noff[:, 32:48]), T.fa[:, C * b:C * b + C], A.add, ["fp%d" % b, "fpz", "fa%d" % b, nkey], ["at%d" % b])
-        quant(qa, 0, C, T.at[:], ["at0", "at1", "at2", "at3"])
-        unpack("PA", qa, False, True)
-        if not last:
-            act(T.ofr[:, 0:C], T.iota[:, 0:C].indirect(noff[:, 0:16]), ["iota", nkey], ["ofr"])
-            partner_lists(r + 1)
-            towards_partner(r + 1)
+            tt(wn[:, 0:16], wn[:, 16:32], T.jw[:, 0:16], A.min, ["wa%d" % (r + 1), "jw"], ["wl%d" % (r + 1)])
+            act(T.ofr[:, 0:C], T.iota[:, 0:C].indirect(noff[:, 16:32]), ["iota", nkey], ["ofr"])
         else:
-            quant("qv", 0, 128, T.vin[:], ["vin"])
-            act(T.omf[:, 0:C], T.iota[:, 0:C].indirect(noff[:, 0:16]), ["iota", nkey], ["omf"])
+            act(T.omf[:, 0:C], T.iota[:, 0:C].indirect(noff[:, 16:32]), ["iota", nkey], ["omf"])
             for k in range(8):
                 dma("y", T.om[k:k + 1, :], T.omf[16 * k:16 * k + 1, :], ["omf"], [], "st1")
+
         for b in range(4):
-            leave("PA", b, OPT["x"][b], T.xt[:, b:4 * C:4], 2.0 ** -5, "xt%d" % b)
+            tt(T.zt[:, b:4 * C:4], T.fh[:, C * b:C * b + C].indirect(noff[:, 16:32]), T.fo[:, C * b:C * b + C], A.add, ["fh%d" % b, "fo%d" % b, nkey], ["zt%d" % b])
+            if b == 0 and not last:
+                cp(noff[:, 0:16], wn[:, 0:16], ["wl%d" % (r + 1)], [nkey + "l"])
+                send(r + 1, T["pp%d" % (r + 1)][:], noff[:, 0:32], [nkey, nkey + "l"], "ap%d" % (r + 1), "pp%d" % (r + 1), "pl%d" % (r + 1))
+        quant(qz, 0, C, T.zt[:], ["zt0", "zt1", "zt2", "zt3"], [qz + "0", qz + "1"])
+        unpack("PB", lx, True, True)
+        for b in range(4):
+            mm("PA", b, "qw", 128 * b, "qw", qz, False, False, 0)
+
+        def edges(b, hs):
+            a, e = H * hs[0], H * hs[-1] + H
+            win = T.fp[:, FW * b:FW * b + C + 1]
+            fa, keys = T.fa[:, C * b + a:C * b + e], ["fa%d%d" % (b, h) for h in hs]
+            act(fa, win.indirect(noff[:, 32 + a // 16:32 + e // 16]), ["fp%d" % b, "fpz", nkey], keys)
+            tt(T.at[:, 4 * a + b:4 * e:4], win.indirect(noff[:, 48 + a // 16:48 + e // 16]), fa, A.add, ["fp%d" % b, "fpz", nkey] + keys, ["at%d%d" % (b, h) for h in hs])
+
+        def joined(h):
+            quant(qa, H * h, H * h + H, T.at[:, 4 * H * h:4 * H * (h + 1)], ["at%d%d" % (b, h) for b in range(4)], ["%s%d" % (qa, h)])
+            unpack(["PA", "PB"][h], qa, False, True, h)
+
+        def state_out(h, who):
+            for b in range(4):
+                leave(["PA", "PB"][h], b, who[b], T.xt[:, 4 * H * h + b:4 * H * (h + 1):4], 2.0 ** -5, "xt%d%d" % (b, h), H)
+
+        def state_packed(h):
+            quant(nx, H * h, H * h + H, T.xt[:, 4 * H * h:4 * H * (h + 1)], ["xt%d%d" % (b, h) for b in range(4)], ["%s%d" % (nx, h)])
+            if not last:
+                scores(nx, h)
+            else:
+                mm("PA", h, "qv", 0, "qv", nx, True, True, h)
+                dma("y", T.oc[:, 4 * H * h:4 * H * (h + 1)], T[nx + "c"][:, H * h:H * h + H].bitcast(dt.uint8), ["%s%dc" % (nx, h)], [], "st1")
+
+        for b, ks in enumerate([(0, 1), (2,), (3,), ()]):
+            for k in ks:
+                leave("PB", k, "s", T.fp[:, FW * k + 1:FW * k + C + 1], 2.0 ** -6, "fp%d" % k)
+            edges(b, (0, 1) if b == 0 else (0,))
+        for b in range(4):
+            mm("PB", b, "e", 128 * b, "e%d" % b, qx, True, False, 1)
+            mm("PB", b, "qw", 128 * b, "qw", qz, False, False, 1)
+        joined(0)
+        for b in range(1, 4):
+            edges(b, (1,))
+        joined(1)
+        state_out(0, "ssss")
+        state_packed(0)
         if not last:
-            least_ends()
+            least_ends(r + 1)
+        state_out(1, "svsv" if last else "vvsv")
+        if last:
+            act(T.ysb[:, 0:H], T.PA[:, 0:H], [], ["PA0", "ysb0"])
+            dma("s", T.y[:, 0:H], T.ysb[:, 0:H], ["ysb0"], [], "st2")
+        state_packed(1)
+        if not last:
+            scores_out(0)
+            twin("v", T.low, "low")
+            act(T.opf[:, 0:C], T.ofr[:, 0:C].indirect(T["pp%d" % (r + 1)][:, 16:32]), ["ofr", "pp%d" % (r + 1)], ["opf"])
 
     qx = "qx%d" % ROUNDS
-    quant(qx, 0, C, T.xt[:], ["xt0", "xt1", "xt2", "xt3"])
-    mm("PB", 0, "qv", 0, "qv", qx, True, True)
-    dma("y", T.oc[:], T[qx + "c"][:].bitcast(dt.uint8), [qx + "c"], [], "st1")
+    cp(T.ysb[:, H:C], T.PA[:, 512:512 + H], [], ["PA1", "ysb1"])
     for k in range(4):
-        dma("ys"[k // 2], T.osc[4 * k:4 * k + 4, :], T[qx + "s"][32 * k:32 * k + 4, :], [qx + "s"], [], ["st1", "st2"][k // 2])
-    cp(T.ysb[:, 0:C], T.PB[:, 0:C], [], ["PB0", "ysb"])
-    dma("s", T.y[:], T.ysb[:], ["ysb"], [], "st2")
+        dma("ys"[k // 2], T.osc[4 * k:4 * k + 4, :], T[qx + "s"][32 * k:32 * k + 4, :], [qx + "0s", qx + "1s"], [], ["st1", "st2"][k // 2])
+    dma("s", T.y[:, H:C], T.ysb[:, H:C], ["ysb1"], [], "st2")
     for s in sorted(total):
         if waited.get(s, 0) < total[s]:
             g.wait_ge(T.sem[s], total[s])

@@ -2,9 +2,16 @@ from concourse.mybir import dt, AluOpType, ActivationFunctionType
 
 C = 256
 H = C // 2
-FW = 272
 ROUNDS = 3
 TINY = 2.0 ** -118
+
+FIRST = """packX sendX unpackF half1:s packU half0:v half2:v half3:s scores lists0 loadW mate0 lows pf val dn lowtwin:v
+    restartF0 valtwin:s far tie dif beats beatstwin:v app listO listA of free d2 a cd mate1 apo mate3 a2 pc listB u m sel mate2 n"""
+HEAD = """sendX scoreout1 half0:s of half1:s val valtwin:s mate1 half2:s half3:s tie dif beats beatstwin:v app dn d2 listA
+    mate0 cd apo free pc mate3 a a2 listB u restartF0 m n mate2 sel"""
+TAIL = """low offs unpackL far0 far2 offs2 Z3 far1 fartwin0:y Z1 sendP Z0 Z2 neg2 far3 fartwin2:g fartwin3:g A2 fartwin1:y
+    neg0 neg3 packZ A00 neg1 FW1 row W0 A30 A10 A31 packA0 A01 lows+ far+ A11 out00:s out10:s pf+ out20:s packA1 packV
+    out30:s out01:s lowtwin+:g out21:s packX0 out11:v out31:v packX1 y0 scoreout0 listO+ unpackF+"""
 
 SCRATCH = {
     "PA": ("psum", [128, 2048], "float32"),
@@ -19,8 +26,8 @@ SCRATCH = {
     "at": ("sbuf", [128, 4 * C], "bfloat16"),
     "fh": ("sbuf", [128, 4 * C], "bfloat16"),
     "fo": ("sbuf", [128, 4 * C], "bfloat16"),
-    "fp": ("sbuf", [128, 4 * FW], "bfloat16"),
-    "fa": ("sbuf", [128, 4 * C], "bfloat16"),
+    "fp": ("sbuf", [128, 8 * C], "bfloat16"),
+    "fq": ("sbuf", [128, 4 * C], "bfloat16"),
     "tt": ("sbuf", [128, 528], "bfloat16"),
     "ia": ("sbuf", [128, 24], "int32"),
     "ib": ("sbuf", [128, 24], "int32"),
@@ -28,9 +35,9 @@ SCRATCH = {
     "cols": ("sbuf", [128, 8], "float32"),
     "e01": ("sbuf", [128, 32], "float32"),
     "c16": ("sbuf", [128, 16], "bfloat16"),
-    "cw": ("sbuf", [128, 512], "bfloat16"),
+    "cw": ("sbuf", [128, C], "bfloat16"),
     "jw": ("sbuf", [128, 32], "float32"),
-    "poff": ("sbuf", [128, 32], "uint16"),
+    "poff": ("sbuf", [128, 16], "uint16"),
     "uoff": ("sbuf", [128, 8], "uint16"),
     "sc": ("sbuf", [128, 2 * C], "float32"),
     "val": ("sbuf", [128, 2 * C], "float32"),
@@ -38,15 +45,16 @@ SCRATCH = {
     "tdf": ("sbuf", [128, C], "bfloat16"),
     "low": ("sbuf", [128, 2 * C], "bfloat16"),
     "bts": ("sbuf", [128, 2 * C], "bfloat16"),
-    "apo": ("sbuf", [128, 2 * C], "bfloat16"),
+    "app": ("sbuf", [128, C], "bfloat16"),
     "aof": ("sbuf", [128, C], "bfloat16"),
     "ofr": ("sbuf", [128, C], "bfloat16"),
     "opf": ("sbuf", [128, C], "bfloat16"),
+    "opo": ("sbuf", [128, C], "bfloat16"),
     "omf": ("sbuf", [128, C], "float32"),
-    "r1": ("sbuf", [128, 2 * C], "bfloat16"),
+    "r0": ("sbuf", [128, C], "bfloat16"),
+    "r1": ("sbuf", [128, C], "bfloat16"),
     "r2": ("sbuf", [128, C], "bfloat16"),
-    "aw": ("sbuf", [128, 32], "float32"),
-    "sm": ("sbuf", [128, 144], "float32"),
+    "sm": ("sbuf", [128, 192], "float32"),
     "ysb": ("sbuf", [128, C], "float32"),
 }
 
@@ -63,8 +71,8 @@ _pair("qv", 128)
 _pair("qw", 512)
 for _r in range(ROUNDS + 1):
     _pair("qx%d" % _r, C)
-    SCRATCH["w%d" % _r] = ("sbuf", [128, 64], "float32")
-    SCRATCH["off%d" % _r] = ("sbuf", [128, 64], "uint16")
+    SCRATCH["w%d" % _r] = ("sbuf", [128, 48], "float32")
+    SCRATCH["off%d" % _r] = ("sbuf", [128, 48], "uint16")
 for _r in range(ROUNDS):
     _pair("lx%d" % _r, C)
     _pair("qa%d" % _r, C)
@@ -72,6 +80,7 @@ for _r in range(ROUNDS):
     SCRATCH["pp%d" % _r] = ("sbuf", [128, 32], "uint16")
 
 SEMAPHORES = ["cv", "cs", "cp", "cg", "snd", "ldm", "ldx", "ldu", "ldw", "lds", "ldv", "st1", "st2"]
+SEMAPHORES += ["tw%d" % _b for _b in range(4)]
 for _r in range(ROUNDS):
     SEMAPHORES += ["ap%d" % _r, "ac%d" % _r, "as%d" % _r]
 
@@ -145,6 +154,17 @@ def rank_program(g, core, T, topo):
         else:
             op("s", lambda: g.scalar.activation(out, in_, COPY, scale=scale), rd, wr)
 
+    def twin(q, out, in_, rd, wr, sem=None):
+        if q == "g":
+            op("g", lambda: g.affine_select(out, in_, [[0, C]], A.is_gt, 0.0, 1, 0), rd, wr)
+        elif q == "y":
+            dma("y", out, in_, rd, wr, sem)
+        else:
+            (cp if q == "v" else act)(out, in_, rd, wr)
+
+    def listed(out, row, rd, wr):
+        op("v", lambda: g.vector.tensor_tensor_scan(out[:, 0:C], T.cw[:, 0:C], row[:, 0:C], 0.0, A.add, A.min), ["cw"] + rd, wr)
+
     def quant(name, a, b, tile, rd, keys):
         op("v", lambda: g.vector.quantize_mx(T[name + "c"][:, a:b], T[name + "s"][:, a:b], tile), rd, [k + e for k in keys for e in "cs"])
 
@@ -166,9 +186,6 @@ def rank_program(g, core, T, topo):
         else:
             ts(out, src, scale, None, A.mult, None, [], ["%s%d" % (ps, b), key])
 
-    def twin(q, buf, key):
-        (cp if q == "v" else act)(buf[:, C:2 * C], buf[:, 0:C], [key], [key + "2"])
-
     partners = [T.cores[rank ^ (1 << r)] for r in range(ROUNDS)]
     common = [e for e in topo.engines(core, partners[0]) if all(e in topo.engines(core, c) for c in partners)]
 
@@ -183,17 +200,162 @@ def rank_program(g, core, T, topo):
         for key in keys:
             wrote[key] = (sem, len(engines))
 
-    def scores(name, h):
-        for b in (0, 1):
-            mm(["PA", "PB"][h], b + 2 - 2 * h, "pu", 0, "pu", name, True, True, h)
+    def sm(k):
+        return T.sm[:, 16 * k:16 * k + 16]
 
-    def scores_out(h):
-        ps, b = ["PA", "PB"][h], 2 - 2 * h
-        cp(T.sc[:, C + H * h:C + H * h + H], T[ps][:, 512 * b:512 * b + H], [], ["%s%d" % (ps, b), "sc2%d" % h])
-        act(T.sc[:, H * h:H * h + H], T[ps][:, 512 * b + 512:512 * b + 512 + H], [], ["%s%d" % (ps, b + 1), "sc%d" % h])
+    PCOL, PM, CC = [T.cols[:, i:i + 1] for i in range(3)]
 
-    def least_ends(r):
-        act(T.low[:, 0:C], T.iota[:, 0:C].indirect(T["pp%d" % r][:, 0:16]), ["iota", "pl%d" % r], ["low"], TINY)
+    def steps(r):
+        qx, lx, qa, qz, nx = ["%s%d" % (n, r) for n in ("qx", "lx", "qa", "qz")] + ["qx%d" % (r + 1)]
+        noff, nkey = T["off%d" % (r + 1)], "off%d" % (r + 1)
+        ou, ouk = T["off%d" % r][:, 32:48], "off%d" % r
+        pp, ppk = T["pp%d" % r][:, 16:32], "pp%d" % r
+        w, wn = T["w%d" % r][:, 32:48], T["w%d" % (r + 1)]
+        wk, wnk, wsk, wlk = "wa%d" % r, "wa%d" % (r + 1), "ws%d" % (r + 1), "wl%d" % (r + 1)
+        last = r + 1 == ROUNDS
+        PS = ["PA", "PB"]
+
+        def send_x():
+            send(r, T[lx + "c"][:].bitcast(dt.uint8), T[qx + "c"][:].bitcast(dt.uint8), [qx + "0c", qx + "1c"], "ac%d" % r, lx + "0c", lx + "1c")
+            send(r, T[lx + "s"][:], T[qx + "s"][:], [qx + "0s", qx + "1s"], "as%d" % r, lx + "0s", lx + "1s")
+
+        def pack_u():
+            quant("qu", 0, 128, T.uin[:], ["uin"], ["qu"])
+            cp(T.puc[:, 0:128].bitcast(dt.uint32), T.quc[:, 0:128].bitcast(dt.uint32).indirect(T.uoff[:, 0:8]), ["quc", "uoff"], ["puc"])
+            act(T.pus[:, 0:128], T.qus[:, 0:128].indirect(T.uoff[:, 0:8]), ["qus", "uoff"], ["pus"])
+
+        def first_scores():
+            for b in (0, 1):
+                mm("PB", b, "pu", 0, "pu", qx, True, True)
+            act(T.sc[:, 0:C], T.PB[:, 0:C], [], ["PB0", "sc0", "sc1"])
+            cp(T.sc[:, C:2 * C], T.PB[:, 512:512 + C], [], ["PB1", "sc20", "sc21"])
+
+        def first_lists():
+            tt(sm(8), T.lp0[:, 0:16], T.jw[:, 0:16], A.min, ["lp0", "jw"], ["sm8"])
+            cp(T.pp0[:, 16:32], T.lp0[:, 0:16], ["lp0"], ["pp0"])
+            cp(T.pp0[:, 0:16], sm(8), ["sm8"], ["pl0"])
+
+        def load_w():
+            wait("y", [wrote["lp0"]])
+            dma("y", T.qwc[:].bitcast(dt.uint8), T.wc[:], [], ["qwc"], "ldw")
+            dma("y", T.qws[:], T.ws[:], [], ["qws"], "lds")
+
+        def scores_out(h):
+            ps, b = PS[h], 2 - 2 * h
+            cp(T.sc[:, C + H * h:C + H * h + H], T[ps][:, 512 * b:512 * b + H], [], ["%s%d" % (ps, b), "sc2%d" % h])
+            act(T.sc[:, H * h:H * h + H], T[ps][:, 512 * b + 512:512 * b + 512 + H], [], ["%s%d" % (ps, b + 1), "sc%d" % h])
+
+        def far_mates():
+            act(T.opf[:, 0:C], T.ofr[:, 0:C].indirect(pp), ["ofr", ppk], ["opf"])
+            act(T.opo[:, 0:C], T.opf[:, 0:C].indirect(ou), ["opf", ouk], ["opo"])
+
+        def row():
+            if not last:
+                act(T.ofr[:, 0:C], T.iota[:, 0:C].indirect(noff[:, 32:48]), ["iota", nkey], ["ofr"])
+                return
+            act(T.omf[:, 0:C], T.iota[:, 0:C].indirect(noff[:, 32:48]), ["iota", nkey], ["omf"])
+            for k in range(8):
+                dma("y", T.om[k:k + 1, :], T.omf[16 * k:16 * k + 1, :], ["omf"], [], "st1")
+
+        def edges(b, hs):
+            a, e = H * hs[0], H * hs[-1] + H
+            tt(T.at[:, 4 * a + b:4 * e:4], T.fp[:, 2 * C * b:2 * C * (b + 1)].indirect(noff[:, a // 16:e // 16]), T.fq[:, C * b + a:C * b + e], A.add,
+               ["fp%d" % b, "fn%d" % b, "fq%d" % b, nkey + "l"], ["at%d%d" % (b, h) for h in hs])
+
+        def f_and_w():
+            for b in range(4):
+                mm("PB", b, "e", 128 * b, "e%d" % b, qx, True, False, 1)
+                mm("PB", b, "qw", 128 * b, "qw", qz, False, False, 1)
+
+        def joined(h):
+            quant(qa, H * h, H * h + H, T.at[:, 4 * H * h:4 * H * (h + 1)], ["at%d%d" % (b, h) for b in range(4)], ["%s%d" % (qa, h)])
+            unpack(PS[h], qa, False, True, h)
+
+        def state_packed(h):
+            quant(nx, H * h, H * h + H, T.xt[:, 4 * H * h:4 * H * (h + 1)], ["xt%d%d" % (b, h) for b in range(4)], ["%s%d" % (nx, h)])
+            if not last:
+                for b in (0, 1):
+                    mm(PS[h], b + 2 - 2 * h, "pu", 0, "pu", nx, True, True, h)
+            else:
+                mm("PA", h, "qv", 0, "qv", nx, True, True, h)
+                dma("y", T.oc[:, 4 * H * h:4 * H * (h + 1)], T[nx + "c"][:, H * h:H * h + H].bitcast(dt.uint8), ["%s%dc" % (nx, h)], [], "st1")
+
+        def first_y():
+            act(T.ysb[:, 0:H], T.PA[:, 0:H], [], ["PA0", "ysb0"])
+            dma("s", T.y[:, 0:H], T.ysb[:, 0:H], ["ysb0"], [], "st2")
+
+        a0 = 16 if last else 32
+        S = {
+            "packX": lambda: quant(qx, 0, C, T.xin[:], ["xin"], [qx + "0", qx + "1"]),
+            "sendX": send_x, "packU": pack_u, "scores": first_scores, "lists0": first_lists, "loadW": load_w,
+            "unpackF": lambda: unpack("PA", qx, True, True),
+            "restartF0": lambda: unpack("PA", qx, True, False, 0),
+            "scoreout1": lambda: scores_out(1),
+            "lows": lambda: act(T.low[:, 0:C], T.iota[:, 0:C].indirect(T["pp%d" % r][:, 0:16]), ["iota", "pl%d" % r], ["low"], TINY),
+            "lowtwin": lambda q: twin(q, T.low[:, C:2 * C], T.low[:, 0:C], ["low"], ["low2"]),
+            "far": far_mates,
+            "val": lambda: tt(T.val[:, 0:C], T.sc[:, 0:C].indirect(pp), T.sc[:, C:2 * C], A.max, ["sc0", "sc1", "sc20", "sc21", ppk], ["val"]),
+            "valtwin": lambda q: twin(q, T.val[:, C:2 * C], T.val[:, 0:C], ["val"], ["val2"]),
+            "tie": lambda: tt(T.tdf[:, 0:C], T.low[:, 0:C].indirect(ou), T.low[:, C:2 * C], A.subtract, ["low", "low2", ouk], ["tdf"]),
+            "dif": lambda: tt(T.dif[:, 0:C], T.val[:, 0:C].indirect(ou), T.val[:, C:2 * C], A.subtract, ["val", "val2", ouk], ["dif"]),
+            "beats": lambda: tt(T.bts[:, 0:C], T.dif[:, 0:C], T.tdf[:, 0:C], A.is_lt, ["dif", "tdf"], ["bts"]),
+            "beatstwin": lambda q: twin(q, T.bts[:, C:2 * C], T.bts[:, 0:C], ["bts"], ["bts2"]),
+            "app": lambda: tt(T.app[:, 0:C], T.bts[:, 0:C].indirect(pp), T.bts[:, C:2 * C], A.mult, ["bts", "bts2", ppk], ["app"]),
+            "apo": lambda: act(T.aof[:, 0:C], T.app[:, 0:C].indirect(ou), ["app", ouk], ["aof"]),
+            "listO": lambda: listed(T.r0, T.opo, ["opo"], ["r0"]),
+            "listA": lambda: listed(T.r1, T.app, ["app"], ["r1"]),
+            "listB": lambda: listed(T.r2, T.aof, ["aof"], ["r2"]),
+            "pf": lambda: cp(sm(0), pp, [ppk], ["sm0"]),
+            "dn": lambda: tt(sm(1), w, sm(0), A.subtract, ["sm0", wk], ["sm1"]),
+            "of": lambda: ts(sm(2), T.r0[:, 15:C:16], CC, None, A.add, None, ["r0", "cc"], ["sm2"]),
+            "d2": lambda: tt(sm(3), sm(2), w, A.subtract, ["sm2", wk], ["sm3"]),
+            "cd": lambda: ts(sm(9), sm(3), CC, None, A.mult, None, ["sm3", "cc"], ["sm9"]),
+            "pc": lambda: tt(sm(11), sm(9), sm(0), A.add, ["sm9", "sm0"], ["sm11"]),
+            "free": lambda: ts(sm(4), T.r1[:, 15:C:16], CC, 0.5, A.add, A.is_lt, ["r1", "cc"], ["sm4"]),
+            "a": lambda: tt(sm(5), sm(4), sm(1), A.mult, ["sm4", "sm1"], ["sm5"]),
+            "a2": lambda: tt(sm(6), sm(4), T.jw[:, 16:32], A.mult, ["sm4", "jw1"], ["sm6"]),
+            "u": lambda: tt(sm(7), sm(5), sm(11), A.add, ["sm5", "sm11"], ["sm7"]),
+            "sel": lambda: tt(wn[:, 0:16], sm(6), sm(0), A.max, ["sm6", "sm0"], [wsk]),
+            "m": lambda: tt(sm(10), T.r2[:, 15:C:16], sm(3), A.mult, ["r2", "sm3"], ["sm10"]),
+            "n": lambda: tt(wn[:, 32:48], sm(10), sm(7), A.add, ["sm10", "sm7"], [wnk]),
+            "offs": lambda: cp(noff[:, 32:48], wn[:, 32:48], [wnk], [nkey]),
+            "offs2": lambda: cp(noff[:, 0:a0], wn[:, 0:a0], [wsk] + ([] if last else [wlk]), [nkey + "l"]),
+            "row": row,
+            "unpackL": lambda: unpack("PB", lx, True, True),
+            "packZ": lambda: quant(qz, 0, C, T.zt[:], ["zt0", "zt1", "zt2", "zt3"], [qz + "0", qz + "1"]),
+            "W0": lambda: [mm("PA", b, "qw", 128 * b, "qw", qz, False, False, 0) for b in range(4)],
+            "FW1": f_and_w,
+        }
+        if r == 0:
+            S["packV"] = lambda: quant("qv", 0, 128, T.vin[:], ["vin"], ["qv"])
+        if last:
+            S["y0"] = first_y
+        else:
+            S["low"] = lambda: tt(wn[:, 16:32], wn[:, 32:48], T.jw[:, 0:16], A.min, [wnk, "jw"], [wlk])
+            S["sendP"] = lambda: send(r + 1, T["pp%d" % (r + 1)][:], noff[:, 16:48], [nkey, nkey + "l"], "ap%d" % (r + 1), "pp%d" % (r + 1), "pl%d" % (r + 1))
+            S["scoreout0"] = lambda: scores_out(0)
+
+        def by_row(b):
+            fh, fo, fp, fn, fq = T.fh[:, C * b:C * b + C], T.fo[:, C * b:C * b + C], T.fp[:, 2 * C * b:2 * C * b + C], T.fp[:, 2 * C * b + C:2 * C * b + 2 * C], T.fq[:, C * b:C * b + C]
+            S["half%d" % b] = lambda q: leave("PA", b, q, fh, 2.0 ** -6, "fh%d" % b)
+            S["mate%d" % b] = lambda: act(fo, fh.indirect(ou), ["fh%d" % b, ouk], ["fo%d" % b])
+            S["Z%d" % b] = lambda: tt(T.zt[:, b:4 * C:4], fh.indirect(noff[:, 32:48]), fo, A.add, ["fh%d" % b, "fo%d" % b, nkey], ["zt%d" % b])
+            S["far%d" % b] = lambda: leave("PB", b, "s", fp, 2.0 ** -6, "fp%d" % b)
+            S["fartwin%d" % b] = lambda q: twin(q, fq, fp, ["fp%d" % b], ["fq%d" % b], "tw%d" % b)
+            S["neg%d" % b] = lambda: leave("PB", b, "s", fn, -2.0 ** -6, "fn%d" % b)
+            S["A%d" % b] = lambda: edges(b, (0, 1))
+            for h in (0, 1):
+                by_half(b, h)
+
+        def by_half(b, h):
+            S["A%d%d" % (b, h)] = lambda: edges(b, (h,))
+            S["out%d%d" % (b, h)] = lambda q: leave(PS[h], b, q, T.xt[:, 4 * H * h + b:4 * H * (h + 1):4], 2.0 ** -5, "xt%d%d" % (b, h), H)
+            S["packA%d" % h] = lambda: joined(h)
+            S["packX%d" % h] = lambda: state_packed(h)
+
+        for b in range(4):
+            by_row(b)
+        return S
 
     dma("y", T.mi[:], T.m[:], [], ["mi"], "ldm")
     dma("y", T.xin[:], T.x[:], [], ["xin"], "ldx")
@@ -203,8 +365,6 @@ def rank_program(g, core, T, topo):
     op("g", lambda: g.iota(T.iota[:], [[1, C]], 0, 0, allow_small_or_imprecise_dtypes=True), [], ["iota"])
     send(0, T.lp0[:], T.mi[:], ["mi"], "ap0", "lp0")
     op("v", lambda: g.vector.memset(T.tt[:], 0.0), [], ["tt"])
-    op("v", lambda: g.vector.memset(T.fp[:, 0:4 * FW:FW], 0.0), [], ["fpz"])
-    PCOL, PM, CC = [T.cols[:, i:i + 1] for i in range(3)]
     cp(PCOL, T.ia[:, 16:17], ["ia"], ["pcol"])
     ts(T.ib[:, 0:16], T.ia[:, 0:16], 15, None, A.bitwise_and, None, ["ia"], ["ib"])
     cp(PM, T.ib[:, 0:1], ["ib"], ["pm"])
@@ -213,160 +373,24 @@ def rank_program(g, core, T, topo):
     ts(T.e01[:, 16:32], T.ib[:, 0:16], 15.0, -256.0, A.is_equal, A.mult, ["ib"], ["e1"])
     tt(T.c16[:, 0:16], T.e01[:, 0:16], T.e01[:, 16:32], A.add, ["e0", "e1"], ["c16"])
     ts(T.tt[:, 3:515:4], T.iota[:, 0:128], PCOL, 32.0, A.is_equal, A.mult, ["iota", "pcol"], ["tt"])
-    ts(T.poff[:, 0:32], T.iota[:, 0:32], 0.0, PM, A.mult, A.add, ["iota", "pm"], ["poff"])
+    ts(T.poff[:, 0:16], T.iota[:, 0:16], 0.0, PM, A.mult, A.add, ["iota", "pm"], ["poff"])
     cp(T.uoff[:, 0:8], T.iota[:, 0:128:16], ["iota"], ["uoff"])
     ts(T.jw[:, 0:16], T.iota[:, 0:C:16], PM, None, A.add, None, ["iota", "pm"], ["jw"])
-    ts(T.jw[:, 16:32], T.iota[:, 0:C:16], PM, 1.0, A.add, A.add, ["iota", "pm"], ["jw1"])
-    act(T.cw[:, 0:512], T.c16[:, 0:16].indirect(T.poff[:, 0:32]), ["c16", "poff"], ["cw"])
+    ts(T.jw[:, 16:32], T.iota[:, 0:C:16], PM, 1.0 * C, A.add, A.add, ["iota", "pm"], ["jw1"])
+    act(T.cw[:, 0:C], T.c16[:, 0:16].indirect(T.poff[:, 0:16]), ["c16", "poff"], ["cw"])
     for b in range(4):
         quant("e", 128 * b, 128 * b + 128, T.tt[:, 3 - b:515 - b], ["tt"], ["e%d" % b])
-    cp(T.off0[:, 16:32], T.mi[:, 0:16], ["mi"], ["off0"])
-    cp(T.w0[:, 16:32], T.mi[:, 0:16], ["mi"], ["wa0"])
-    act(T.ofr[:, 0:C], T.iota[:, 0:C].indirect(T.off0[:, 16:32]), ["iota", "off0"], ["ofr"])
+    cp(T.off0[:, 32:48], T.mi[:, 0:16], ["mi"], ["off0"])
+    cp(T.w0[:, 32:48], T.mi[:, 0:16], ["mi"], ["wa0"])
+    act(T.ofr[:, 0:C], T.iota[:, 0:C].indirect(T.off0[:, 32:48]), ["iota", "off0"], ["ofr"])
 
+    rounds = [steps(r) for r in range(ROUNDS)] + [{}]
     for r in range(ROUNDS):
-        qx, lx, qa, qz, nx = ["%s%d" % (n, r) for n in ("qx", "lx", "qa", "qz")] + ["qx%d" % (r + 1)]
-        noff, nkey = T["off%d" % (r + 1)], "off%d" % (r + 1)
-        ou, ouk = T["off%d" % r][:, 16:32], "off%d" % r
-        pp, ppk = T["pp%d" % r][:, 16:32], "pp%d" % r
-        w, wn = T["w%d" % r][:, 16:32], T["w%d" % (r + 1)]
-        wk = "wa%d" % r
-        last = r + 1 == ROUNDS
-
-        def halves(bs, who):
-            for b in bs:
-                leave("PA", b, who[b], T.fh[:, C * b:C * b + C], 2.0 ** -6, "fh%d" % b)
-
-        def mates_of(bs):
-            for b in bs:
-                act(T.fo[:, C * b:C * b + C], T.fh[:, C * b:C * b + C].indirect(ou), ["fh%d" % b, ouk], ["fo%d" % b])
-
-        if r == 0:
-            quant(qx, 0, C, T.xin[:], ["xin"], [qx + "0", qx + "1"])
-        send(r, T[lx + "c"][:].bitcast(dt.uint8), T[qx + "c"][:].bitcast(dt.uint8), [qx + "0c", qx + "1c"], "ac%d" % r, lx + "0c", lx + "1c")
-        send(r, T[lx + "s"][:], T[qx + "s"][:], [qx + "0s", qx + "1s"], "as%d" % r, lx + "0s", lx + "1s")
-        if r == 0:
-            unpack("PA", qx, True, True)
-            quant("qu", 0, 128, T.uin[:], ["uin"], ["qu"])
-            cp(T.puc[:, 0:128].bitcast(dt.uint32), T.quc[:, 0:128].bitcast(dt.uint32).indirect(T.uoff[:, 0:8]), ["quc", "uoff"], ["puc"])
-            act(T.pus[:, 0:128], T.qus[:, 0:128].indirect(T.uoff[:, 0:8]), ["qus", "uoff"], ["pus"])
-            mm("PB", 0, "pu", 0, "pu", qx, True, True)
-            act(T.sc[:, 0:C], T.PB[:, 0:C], [], ["PB0", "sc0", "sc1"])
-            cp(T.sc[:, C:2 * C], T.PB[:, 0:C], [], ["PB0", "sc20", "sc21"])
-            halves(range(4), "svsv")
-            mates_of((0, 1))
-            quant("qv", 0, 128, T.vin[:], ["vin"], ["qv"])
-            tt(T.sm[:, 128:144], T.lp0[:, 0:16], T.jw[:, 0:16], A.min, ["lp0", "jw"], ["sm8"])
-            cp(T.pp0[:, 16:32], T.lp0[:, 0:16], ["lp0"], ["pp0"])
-            cp(T.pp0[:, 0:16], T.sm[:, 128:144], ["sm8"], ["pl0"])
-            least_ends(0)
-            wait("y", [wrote["lp0"]])
-            dma("y", T.qwc[:].bitcast(dt.uint8), T.wc[:], [], ["qwc"], "ldw")
-            dma("y", T.qws[:], T.ws[:], [], ["qws"], "lds")
-        else:
-            scores_out(1)
-            unpack("PA", qx, True, True)
-            halves((0, 1), "ssss")
-
-        tt(T.val[:, 0:C], T.sc[:, 0:C].indirect(pp), T.sc[:, C:2 * C], A.max, ["sc0", "sc1", "sc20", "sc21", ppk], ["val"])
-        twin("s", T.val, "val")
-        if r == 0:
-            twin("v", T.low, "low")
-        tt(T.tdf[:, 0:C], T.low[:, 0:C].indirect(ou), T.low[:, C:2 * C], A.subtract, ["low", "low2", ouk], ["tdf"])
-        if r > 0:
-            halves((2, 3), "ssss")
-        unpack("PA", qx, True, False, 0)
-        if r == 0:
-            act(T.opf[:, 0:C], T.ofr[:, 0:C].indirect(pp), ["ofr", ppk], ["opf"])
-        act(T.apo[:, C:2 * C], T.opf[:, 0:C].indirect(ou), ["opf", ouk], ["opo"])
-        mates_of((0, 1) if r > 0 else (2,))
-        tt(T.dif[:, 0:C], T.val[:, 0:C].indirect(ou), T.val[:, C:2 * C], A.subtract, ["val", "val2", ouk], ["dif"])
-        cp(T.sm[:, 0:16], pp, [ppk], ["sm0"])
-        tt(T.bts[:, 0:C], T.dif[:, 0:C], T.tdf[:, 0:C], A.is_lt, ["dif", "tdf"], ["bts"])
-        tt(T.sm[:, 16:32], T.sm[:, 0:16], w, A.subtract, ["sm0", wk], ["sm1"])
-        twin("v", T.bts, "bts")
-        tt(T.apo[:, 0:C], T.bts[:, 0:C].indirect(pp), T.bts[:, C:2 * C], A.mult, ["bts", "bts2", ppk], ["app"])
-        act(T.aof[:, 0:C], T.apo[:, 0:C].indirect(ou), ["app", ouk], ["aof"])
-        mates_of((2, 3) if r > 0 else (3,))
-
-        ts(T.sm[:, 112:128], pp, 1.0, None, A.add, None, [ppk], ["sm7"])
-        op("v", lambda: g.vector.tensor_tensor_scan(T.r1[:, 0:2 * C], T.cw[:, 0:2 * C], T.apo[:, 0:2 * C], 0.0, A.add, A.min), ["cw", "app", "opo"], ["r1"])
-        ts(T.aw[:, 0:32], T.r1[:, 15:2 * C:16], CC, None, A.add, None, ["r1", "cc"], ["aw"])
-        tt(T.sm[:, 64:80], T.aw[:, 16:32], w, A.subtract, ["aw", wk], ["sm4"])
-        tt(T.sm[:, 32:48], T.aw[:, 0:16], T.sm[:, 16:32], A.mult, ["aw", "sm1"], ["sm2"])
-        op("v", lambda: g.vector.tensor_tensor_scan(T.r2[:, 0:C], T.cw[:, 0:C], T.aof[:, 0:C], 0.0, A.add, A.min), ["cw", "aof"], ["r2"])
-        tt(T.sm[:, 48:64], T.sm[:, 32:48], w, A.add, ["sm2", wk], ["sm3"])
-        ts(T.sm[:, 80:96], T.r2[:, 15:C:16], CC, None, A.add, None, ["r2", "cc"], ["sm5"])
-        tt(wn[:, 32:48], T.aw[:, 0:16], T.jw[:, 16:32], A.mult, ["aw", "jw1"], ["wb%d" % (r + 1)])
-        tt(T.sm[:, 96:112], T.sm[:, 80:96], T.sm[:, 64:80], A.mult, ["sm5", "sm4"], ["sm6"])
-        tt(wn[:, 48:64], T.aw[:, 0:16], T.sm[:, 112:128], A.mult, ["aw", "sm7"], ["wc%d" % (r + 1)])
-        tt(wn[:, 16:32], T.sm[:, 96:112], T.sm[:, 48:64], A.add, ["sm6", "sm3"], ["wa%d" % (r + 1)])
-        cp(noff[:, 16:64], wn[:, 16:64], ["w%s%d" % (k, r + 1) for k in "abc"], [nkey])
-        if not last:
-            tt(wn[:, 0:16], wn[:, 16:32], T.jw[:, 0:16], A.min, ["wa%d" % (r + 1), "jw"], ["wl%d" % (r + 1)])
-            act(T.ofr[:, 0:C], T.iota[:, 0:C].indirect(noff[:, 16:32]), ["iota", nkey], ["ofr"])
-        else:
-            act(T.omf[:, 0:C], T.iota[:, 0:C].indirect(noff[:, 16:32]), ["iota", nkey], ["omf"])
-            for k in range(8):
-                dma("y", T.om[k:k + 1, :], T.omf[16 * k:16 * k + 1, :], ["omf"], [], "st1")
-
-        for b in range(4):
-            tt(T.zt[:, b:4 * C:4], T.fh[:, C * b:C * b + C].indirect(noff[:, 16:32]), T.fo[:, C * b:C * b + C], A.add, ["fh%d" % b, "fo%d" % b, nkey], ["zt%d" % b])
-            if b == 0 and not last:
-                cp(noff[:, 0:16], wn[:, 0:16], ["wl%d" % (r + 1)], [nkey + "l"])
-                send(r + 1, T["pp%d" % (r + 1)][:], noff[:, 0:32], [nkey, nkey + "l"], "ap%d" % (r + 1), "pp%d" % (r + 1), "pl%d" % (r + 1))
-        quant(qz, 0, C, T.zt[:], ["zt0", "zt1", "zt2", "zt3"], [qz + "0", qz + "1"])
-        unpack("PB", lx, True, True)
-        for b in range(4):
-            mm("PA", b, "qw", 128 * b, "qw", qz, False, False, 0)
-
-        def edges(b, hs):
-            a, e = H * hs[0], H * hs[-1] + H
-            win = T.fp[:, FW * b:FW * b + C + 1]
-            fa, keys = T.fa[:, C * b + a:C * b + e], ["fa%d%d" % (b, h) for h in hs]
-            act(fa, win.indirect(noff[:, 32 + a // 16:32 + e // 16]), ["fp%d" % b, "fpz", nkey], keys)
-            tt(T.at[:, 4 * a + b:4 * e:4], win.indirect(noff[:, 48 + a // 16:48 + e // 16]), fa, A.add, ["fp%d" % b, "fpz", nkey] + keys, ["at%d%d" % (b, h) for h in hs])
-
-        def joined(h):
-            quant(qa, H * h, H * h + H, T.at[:, 4 * H * h:4 * H * (h + 1)], ["at%d%d" % (b, h) for b in range(4)], ["%s%d" % (qa, h)])
-            unpack(["PA", "PB"][h], qa, False, True, h)
-
-        def state_out(h, who):
-            for b in range(4):
-                leave(["PA", "PB"][h], b, who[b], T.xt[:, 4 * H * h + b:4 * H * (h + 1):4], 2.0 ** -5, "xt%d%d" % (b, h), H)
-
-        def state_packed(h):
-            quant(nx, H * h, H * h + H, T.xt[:, 4 * H * h:4 * H * (h + 1)], ["xt%d%d" % (b, h) for b in range(4)], ["%s%d" % (nx, h)])
-            if not last:
-                scores(nx, h)
-            else:
-                mm("PA", h, "qv", 0, "qv", nx, True, True, h)
-                dma("y", T.oc[:, 4 * H * h:4 * H * (h + 1)], T[nx + "c"][:, H * h:H * h + H].bitcast(dt.uint8), ["%s%dc" % (nx, h)], [], "st1")
-
-        for b, ks in enumerate([(0, 1), (2,), (3,), ()]):
-            for k in ks:
-                leave("PB", k, "s", T.fp[:, FW * k + 1:FW * k + C + 1], 2.0 ** -6, "fp%d" % k)
-            edges(b, (0, 1) if b == 0 else (0,))
-        for b in range(4):
-            mm("PB", b, "e", 128 * b, "e%d" % b, qx, True, False, 1)
-            mm("PB", b, "qw", 128 * b, "qw", qz, False, False, 1)
-        joined(0)
-        for b in range(1, 4):
-            edges(b, (1,))
-        joined(1)
-        state_out(0, "ssss")
-        state_packed(0)
-        if not last:
-            least_ends(r + 1)
-        state_out(1, "svsv" if last else "vvsv")
-        if last:
-            act(T.ysb[:, 0:H], T.PA[:, 0:H], [], ["PA0", "ysb0"])
-            dma("s", T.y[:, 0:H], T.ysb[:, 0:H], ["ysb0"], [], "st2")
-        state_packed(1)
-        if not last:
-            scores_out(0)
-            twin("v", T.low, "low")
-            act(T.opf[:, 0:C], T.ofr[:, 0:C].indirect(T["pp%d" % (r + 1)][:, 16:32]), ["ofr", "pp%d" % (r + 1)], ["opf"])
+        for word in ((HEAD if r else FIRST) + " " + TAIL).split():
+            name, _, q = word.partition(":")
+            step = rounds[r + 1].get(name[:-1]) if name.endswith("+") else rounds[r].get(name)
+            if step is not None:
+                step(*q)
 
     qx = "qx%d" % ROUNDS
     cp(T.ysb[:, H:C], T.PA[:, 512:512 + H], [], ["PA1", "ysb1"])

@@ -5,13 +5,19 @@ H = C // 2
 ROUNDS = 3
 TINY = 2.0 ** -118
 
-FIRST = """packX sendX unpackF half1:s packU half0:v half2:v half3:s scores lists0 loadW mate0 lows pf val dn lowtwin:v
-    restartF0 valtwin:s far tie dif beats beatstwin:v app listO listA of free d2 a cd mate1 apo mate3 a2 pc listB u m sel mate2 n"""
-HEAD = """sendX scoreout1 half0:s of half1:s val valtwin:s mate1 half2:s half3:s tie dif beats beatstwin:v app dn d2 listA
-    mate0 cd apo free pc mate3 a a2 listB u restartF0 m n mate2 sel"""
-TAIL = """low offs unpackL far0 far2 offs2 Z3 far1 fartwin0:y Z1 sendP Z0 Z2 neg2 far3 fartwin2:g fartwin3:g A2 fartwin1:y
-    neg0 neg3 packZ A00 neg1 FW1 row W0 A30 A10 A31 packA0 A01 lows+ far+ A11 out00:s out10:s pf+ out20:s packA1 packV
-    out30:s out01:s lowtwin+:g out21:s packX0 out11:v out31:v packX1 y0 scoreout0 listO+ unpackF+"""
+FIRST = """pcol ib pm zero e0 uoff eye off0 e1 E3 c16 poff E0 jw1 row0 E2 cw E1 jw cl packU scaleU pickU packI0 packI1 sendX cwt
+    sd0:s sc0:s sd1:s lw0 pp0 pl0 loadW w0 sc1:s unpackF lows opf lowo val half2:v lf opo valtwin:v half1:s cc pf dif half0:s
+    listL sign mate2 tie lx listO bp of tw listS bq listP d2 nb dn half3:s nbp w2 free cd mate0 listQ a pc mate1 a2
+    restartF0 m u sel mate3 n"""
+HEAD = """sendX half1:s val tie half2:s valtwin:s half3:s mate1 dif tw d2 bp sign half0:s listS listP nb bq dn nbp mate2 w2 free
+    restartF0 cd listQ a pc m u a2 n sel mate0 mate3"""
+TAIL = """unpackL far3:s low neg1:s far2:s far1:s offs offs2 Z2 sendP Z1 fartwin2:g Z0 Z3 far0:s neg0:v fartwin3:y packZ neg2:s
+    fartwin1:s neg3:s pickA0 lows+ A2 W0 FW1 row A10 A30 addA00 A31 packA0 lowo+ addA01 A11 out20:s out00:v packA1 out10:v
+    out30:s pf+ opf+ packX0 out01:v out21:v out31:s opo+ out11:v sd0+:s lf+ packX1 listL+ sc0+:v listO+ lx+ packV of+
+    sd1+:s unpackF+ sc1+:s"""
+LAST = """offs unpackL far0:s offs2 Z2 neg1:s far2:s Z1 neg3:s Z3 fartwin2:g neg0:s far3:s Z0 far1:s pickA0 neg2:v fartwin3:g
+    packZ FW1 A2 addA00 pickA1 row A30 W0 addA10 addA01 packA0 out10:s addA11 A31 out20:s packA1 out00:v out30:s packX0
+    out11:v out01:s out21:v out31:s y0:s packX1 scales y1:v"""
 
 SCRATCH = {
     "PA": ("psum", [128, 2048], "float32"),
@@ -26,6 +32,7 @@ SCRATCH = {
     "at": ("sbuf", [128, 4 * C], "bfloat16"),
     "fh": ("sbuf", [128, 4 * C], "bfloat16"),
     "fo": ("sbuf", [128, 4 * C], "bfloat16"),
+    "fz": ("sbuf", [128, 4 * C], "bfloat16"),
     "fp": ("sbuf", [128, 8 * C], "bfloat16"),
     "fq": ("sbuf", [128, 4 * C], "bfloat16"),
     "tt": ("sbuf", [128, 528], "bfloat16"),
@@ -36,6 +43,7 @@ SCRATCH = {
     "e01": ("sbuf", [128, 32], "float32"),
     "c16": ("sbuf", [128, 16], "bfloat16"),
     "cw": ("sbuf", [128, C], "bfloat16"),
+    "cwt": ("sbuf", [128, C], "bfloat16"),
     "jw": ("sbuf", [128, 32], "float32"),
     "poff": ("sbuf", [128, 16], "uint16"),
     "uoff": ("sbuf", [128, 8], "uint16"),
@@ -44,17 +52,14 @@ SCRATCH = {
     "dif": ("sbuf", [128, C], "bfloat16"),
     "tdf": ("sbuf", [128, C], "bfloat16"),
     "low": ("sbuf", [128, 2 * C], "bfloat16"),
-    "bts": ("sbuf", [128, 2 * C], "bfloat16"),
-    "app": ("sbuf", [128, C], "bfloat16"),
-    "aof": ("sbuf", [128, C], "bfloat16"),
+    "sgn": ("sbuf", [128, C], "bfloat16"),
+    "bp": ("sbuf", [128, C], "bfloat16"),
+    "bq": ("sbuf", [128, C], "bfloat16"),
     "ofr": ("sbuf", [128, C], "bfloat16"),
     "opf": ("sbuf", [128, C], "bfloat16"),
     "opo": ("sbuf", [128, C], "bfloat16"),
     "omf": ("sbuf", [128, C], "float32"),
-    "r0": ("sbuf", [128, C], "bfloat16"),
-    "r1": ("sbuf", [128, C], "bfloat16"),
-    "r2": ("sbuf", [128, C], "bfloat16"),
-    "sm": ("sbuf", [128, 192], "float32"),
+    "sm": ("sbuf", [128, 320], "float32"),
     "ysb": ("sbuf", [128, C], "float32"),
 }
 
@@ -69,6 +74,8 @@ _pair("qu", 128)
 _pair("pu", 128)
 _pair("qv", 128)
 _pair("qw", 512)
+for _r in range(5):
+    SCRATCH["r%d" % _r] = ("sbuf", [128, C], "bfloat16")
 for _r in range(ROUNDS + 1):
     _pair("qx%d" % _r, C)
     SCRATCH["w%d" % _r] = ("sbuf", [128, 48], "float32")
@@ -79,7 +86,7 @@ for _r in range(ROUNDS):
     _pair("qz%d" % _r, C)
     SCRATCH["pp%d" % _r] = ("sbuf", [128, 32], "uint16")
 
-SEMAPHORES = ["cv", "cs", "cp", "cg", "snd", "ldm", "ldx", "ldu", "ldw", "lds", "ldv", "st1", "st2"]
+SEMAPHORES = ["cv", "cs", "cp", "cg", "snd", "ldm", "ldx0", "ldx1", "ldu", "ldw", "lds", "ldv", "st1", "st2"]
 SEMAPHORES += ["tw%d" % _b for _b in range(4)]
 for _r in range(ROUNDS):
     SEMAPHORES += ["ap%d" % _r, "ac%d" % _r, "as%d" % _r]
@@ -162,8 +169,8 @@ def rank_program(g, core, T, topo):
         else:
             (cp if q == "v" else act)(out, in_, rd, wr)
 
-    def listed(out, row, rd, wr):
-        op("v", lambda: g.vector.tensor_tensor_scan(out[:, 0:C], T.cw[:, 0:C], row[:, 0:C], 0.0, A.add, A.min), ["cw"] + rd, wr)
+    def listed(out, row, rd, wr, cw="cw"):
+        op("v", lambda: g.vector.tensor_tensor_scan(out[:, 0:C], T[cw][:, 0:C], row, 0.0, A.add, A.min), [cw] + rd, wr)
 
     def quant(name, a, b, tile, rd, keys):
         op("v", lambda: g.vector.quantize_mx(T[name + "c"][:, a:b], T[name + "s"][:, a:b], tile), rd, [k + e for k in keys for e in "cs"])
@@ -183,6 +190,8 @@ def rank_program(g, core, T, topo):
         src = T[ps][:, 512 * b:512 * b + n]
         if q == "s":
             act(out, src, [], ["%s%d" % (ps, b), key], scale)
+        elif scale is None:
+            cp(out, src, [], ["%s%d" % (ps, b), key])
         else:
             ts(out, src, scale, None, A.mult, None, [], ["%s%d" % (ps, b), key])
 
@@ -203,7 +212,59 @@ def rank_program(g, core, T, topo):
     def sm(k):
         return T.sm[:, 16 * k:16 * k + 16]
 
-    PCOL, PM, CC = [T.cols[:, i:i + 1] for i in range(3)]
+    PCOL, PM, CC, CL = [T.cols[:, i:i + 1] for i in range(4)]
+    PS = ["PA", "PB"]
+
+    def packed(name, tile, rd, h, side):
+        quant(name, H * h, H * h + H, tile[:, 4 * H * h:4 * H * (h + 1)], rd, ["%s%d" % (name, h)])
+        if side == "pu":
+            for b in (0, 1):
+                mm(PS[h], b + 2 - 2 * h, "pu", 0, "pu", name, True, True, h)
+        else:
+            mm("PA", h, "qv", 0, "qv", name, True, True, h)
+            dma("y", T.oc[:, 4 * H * h:4 * H * (h + 1)], T[name + "c"][:, H * h:H * h + H].bitcast(dt.uint8), ["%s%dc" % (name, h)], [], "st1")
+
+    def opening():
+        def load_w():
+            wait("y", [wrote["lp0"]])
+            dma("y", T.qwc[:].bitcast(dt.uint8), T.wc[:], [], ["qwc"], "ldw")
+            dma("y", T.qws[:], T.ws[:], [], ["qws"], "lds")
+            dma("y", T.vin[:], T.v[:], [], ["vin"], "ldv")
+
+        S = {
+            "zero": lambda: op("v", lambda: g.vector.memset(T.tt[:], 0.0), [], ["tt"]),
+            "pcol": lambda: cp(PCOL, T.ia[:, 16:17], ["ia"], ["pcol"]),
+            "ib": lambda: ts(T.ib[:, 0:16], T.ia[:, 0:16], 15, None, A.bitwise_and, None, ["ia"], ["ib"]),
+            "pm": lambda: cp(PM, T.ib[:, 0:1], ["ib"], ["pm"]),
+            "cc": lambda: ts(CC, T.ib[:, 0:1], 15.0, 4.0, A.not_equal, A.mult, ["ib"], ["cc"]),
+            "cl": lambda: ts(CL, T.ib[:, 0:1], 15.0, 3.5, A.not_equal, A.mult, ["ib"], ["cl"]),
+            "e0": lambda: ts(T.e01[:, 0:16], T.ib[:, 0:16], 0.0, 8.0, A.is_equal, A.mult, ["ib"], ["x0"]),
+            "e1": lambda: ts(T.e01[:, 16:32], T.ib[:, 0:16], 15.0, -4.0, A.is_equal, A.mult, ["ib"], ["x1"]),
+            "c16": lambda: tt(T.c16[:, 0:16], T.e01[:, 0:16], T.e01[:, 16:32], A.add, ["x0", "x1"], ["c16"]),
+            "eye": lambda: ts(T.tt[:, 3:515:4], T.iota[:, 0:128], PCOL, 32.0, A.is_equal, A.mult, ["iota", "pcol", "tt"], ["eye"]),
+            "poff": lambda: ts(T.poff[:, 0:16], T.iota[:, 0:16], 0.0, PM, A.mult, A.add, ["iota", "pm"], ["poff"]),
+            "uoff": lambda: cp(T.uoff[:, 0:8], T.iota[:, 0:128:16], ["iota"], ["uoff"]),
+            "jw": lambda: ts(T.jw[:, 0:16], T.iota[:, 0:C:16], PM, None, A.add, None, ["iota", "pm"], ["jw"]),
+            "jw1": lambda: ts(T.jw[:, 16:32], T.iota[:, 0:C:16], PM, 1.0 * C, A.add, A.add, ["iota", "pm"], ["jw1"]),
+            "cw": lambda: act(T.cw[:, 0:C], T.c16[:, 0:16].indirect(T.poff[:, 0:16]), ["c16", "poff"], ["cw"]),
+            "cwt": lambda: ts(T.cwt[:, 0:C], T.cw[:, 0:C], 64.0 * TINY, None, A.mult, None, ["cw"], ["cwt"]),
+            "off0": lambda: cp(T.off0[:, 32:48], T.mi[:, 0:16], ["mi"], ["off0"]),
+            "w0": lambda: cp(T.w0[:, 32:48], T.mi[:, 0:16], ["mi"], ["wa0"]),
+            "row0": lambda: act(T.ofr[:, 0:C], T.iota[:, 0:C].indirect(T.off0[:, 32:48]), ["iota", "off0"], ["ofr"]),
+            "packU": lambda: quant("qu", 0, 128, T.uin[:], ["uin"], ["qu"]),
+            "pickU": lambda: cp(T.puc[:, 0:128].bitcast(dt.uint32), T.quc[:, 0:128].bitcast(dt.uint32).indirect(T.uoff[:, 0:8]), ["quc", "uoff"], ["puc"]),
+            "scaleU": lambda: act(T.pus[:, 0:128], T.qus[:, 0:128].indirect(T.uoff[:, 0:8]), ["qus", "uoff"], ["pus"]),
+            "packI0": lambda: packed("qx0", T.xin, ["xin0"], 0, "pu"),
+            "packI1": lambda: packed("qx0", T.xin, ["xin1"], 1, "pu"),
+            "lw0": lambda: tt(sm(8), T.lp0[:, 0:16], T.jw[:, 0:16], A.min, ["lp0", "jw"], ["sm8"]),
+            "pp0": lambda: cp(T.pp0[:, 16:32], T.lp0[:, 0:16], ["lp0"], ["pp0"]),
+            "pl0": lambda: cp(T.pp0[:, 0:16], sm(8), ["sm8"], ["pl0"]),
+            "loadW": load_w,
+            "packV": lambda: quant("qv", 0, 128, T.vin[:], ["vin"], ["qv"]),
+        }
+        for b in range(4):
+            S["E%d" % b] = (lambda b: lambda: quant("e", 128 * b, 128 * b + 128, T.tt[:, 3 - b:515 - b], ["eye"], ["e%d" % b]))(b)
+        return S
 
     def steps(r):
         qx, lx, qa, qz, nx = ["%s%d" % (n, r) for n in ("qx", "lx", "qa", "qz")] + ["qx%d" % (r + 1)]
@@ -213,41 +274,10 @@ def rank_program(g, core, T, topo):
         w, wn = T["w%d" % r][:, 32:48], T["w%d" % (r + 1)]
         wk, wnk, wsk, wlk = "wa%d" % r, "wa%d" % (r + 1), "ws%d" % (r + 1), "wl%d" % (r + 1)
         last = r + 1 == ROUNDS
-        PS = ["PA", "PB"]
 
         def send_x():
             send(r, T[lx + "c"][:].bitcast(dt.uint8), T[qx + "c"][:].bitcast(dt.uint8), [qx + "0c", qx + "1c"], "ac%d" % r, lx + "0c", lx + "1c")
             send(r, T[lx + "s"][:], T[qx + "s"][:], [qx + "0s", qx + "1s"], "as%d" % r, lx + "0s", lx + "1s")
-
-        def pack_u():
-            quant("qu", 0, 128, T.uin[:], ["uin"], ["qu"])
-            cp(T.puc[:, 0:128].bitcast(dt.uint32), T.quc[:, 0:128].bitcast(dt.uint32).indirect(T.uoff[:, 0:8]), ["quc", "uoff"], ["puc"])
-            act(T.pus[:, 0:128], T.qus[:, 0:128].indirect(T.uoff[:, 0:8]), ["qus", "uoff"], ["pus"])
-
-        def first_scores():
-            for b in (0, 1):
-                mm("PB", b, "pu", 0, "pu", qx, True, True)
-            act(T.sc[:, 0:C], T.PB[:, 0:C], [], ["PB0", "sc0", "sc1"])
-            cp(T.sc[:, C:2 * C], T.PB[:, 512:512 + C], [], ["PB1", "sc20", "sc21"])
-
-        def first_lists():
-            tt(sm(8), T.lp0[:, 0:16], T.jw[:, 0:16], A.min, ["lp0", "jw"], ["sm8"])
-            cp(T.pp0[:, 16:32], T.lp0[:, 0:16], ["lp0"], ["pp0"])
-            cp(T.pp0[:, 0:16], sm(8), ["sm8"], ["pl0"])
-
-        def load_w():
-            wait("y", [wrote["lp0"]])
-            dma("y", T.qwc[:].bitcast(dt.uint8), T.wc[:], [], ["qwc"], "ldw")
-            dma("y", T.qws[:], T.ws[:], [], ["qws"], "lds")
-
-        def scores_out(h):
-            ps, b = PS[h], 2 - 2 * h
-            cp(T.sc[:, C + H * h:C + H * h + H], T[ps][:, 512 * b:512 * b + H], [], ["%s%d" % (ps, b), "sc2%d" % h])
-            act(T.sc[:, H * h:H * h + H], T[ps][:, 512 * b + 512:512 * b + 512 + H], [], ["%s%d" % (ps, b + 1), "sc%d" % h])
-
-        def far_mates():
-            act(T.opf[:, 0:C], T.ofr[:, 0:C].indirect(pp), ["ofr", ppk], ["opf"])
-            act(T.opo[:, 0:C], T.opf[:, 0:C].indirect(ou), ["opf", ouk], ["opo"])
 
         def row():
             if not last:
@@ -256,11 +286,6 @@ def rank_program(g, core, T, topo):
             act(T.omf[:, 0:C], T.iota[:, 0:C].indirect(noff[:, 32:48]), ["iota", nkey], ["omf"])
             for k in range(8):
                 dma("y", T.om[k:k + 1, :], T.omf[16 * k:16 * k + 1, :], ["omf"], [], "st1")
-
-        def edges(b, hs):
-            a, e = H * hs[0], H * hs[-1] + H
-            tt(T.at[:, 4 * a + b:4 * e:4], T.fp[:, 2 * C * b:2 * C * (b + 1)].indirect(noff[:, a // 16:e // 16]), T.fq[:, C * b + a:C * b + e], A.add,
-               ["fp%d" % b, "fn%d" % b, "fq%d" % b, nkey + "l"], ["at%d%d" % (b, h) for h in hs])
 
         def f_and_w():
             for b in range(4):
@@ -271,132 +296,127 @@ def rank_program(g, core, T, topo):
             quant(qa, H * h, H * h + H, T.at[:, 4 * H * h:4 * H * (h + 1)], ["at%d%d" % (b, h) for b in range(4)], ["%s%d" % (qa, h)])
             unpack(PS[h], qa, False, True, h)
 
-        def state_packed(h):
-            quant(nx, H * h, H * h + H, T.xt[:, 4 * H * h:4 * H * (h + 1)], ["xt%d%d" % (b, h) for b in range(4)], ["%s%d" % (nx, h)])
-            if not last:
-                for b in (0, 1):
-                    mm(PS[h], b + 2 - 2 * h, "pu", 0, "pu", nx, True, True, h)
-            else:
-                mm("PA", h, "qv", 0, "qv", nx, True, True, h)
-                dma("y", T.oc[:, 4 * H * h:4 * H * (h + 1)], T[nx + "c"][:, H * h:H * h + H].bitcast(dt.uint8), ["%s%dc" % (nx, h)], [], "st1")
+        def y_out(h, q):
+            leave("PA", h, q, T.ysb[:, H * h:H * h + H], None, "ysb%d" % h, H)
+            dma("s", T.y[:, H * h:H * h + H], T.ysb[:, H * h:H * h + H], ["ysb%d" % h], [], "st2")
 
-        def first_y():
-            act(T.ysb[:, 0:H], T.PA[:, 0:H], [], ["PA0", "ysb0"])
-            dma("s", T.y[:, 0:H], T.ysb[:, 0:H], ["ysb0"], [], "st2")
+        def scales():
+            for k in range(4):
+                dma("y", T.osc[4 * k:4 * k + 4, :], T[nx + "s"][32 * k:32 * k + 4, :], [nx + "0s", nx + "1s"], [], "st1")
 
         a0 = 16 if last else 32
         S = {
-            "packX": lambda: quant(qx, 0, C, T.xin[:], ["xin"], [qx + "0", qx + "1"]),
-            "sendX": send_x, "packU": pack_u, "scores": first_scores, "lists0": first_lists, "loadW": load_w,
+            "sendX": send_x,
             "unpackF": lambda: unpack("PA", qx, True, True),
             "restartF0": lambda: unpack("PA", qx, True, False, 0),
-            "scoreout1": lambda: scores_out(1),
             "lows": lambda: act(T.low[:, 0:C], T.iota[:, 0:C].indirect(T["pp%d" % r][:, 0:16]), ["iota", "pl%d" % r], ["low"], TINY),
-            "lowtwin": lambda q: twin(q, T.low[:, C:2 * C], T.low[:, 0:C], ["low"], ["low2"]),
-            "far": far_mates,
-            "val": lambda: tt(T.val[:, 0:C], T.sc[:, 0:C].indirect(pp), T.sc[:, C:2 * C], A.max, ["sc0", "sc1", "sc20", "sc21", ppk], ["val"]),
+            "lowo": lambda: act(T.low[:, C:2 * C], T.low[:, 0:C].indirect(ou), ["low", ouk], ["lowo"]),
+            "opf": lambda: act(T.opf[:, 0:C], T.ofr[:, 0:C].indirect(pp), ["ofr", ppk], ["opf"]),
+            "opo": lambda: act(T.opo[:, 0:C], T.opf[:, 0:C].indirect(ou), ["opf", ouk], ["opo"], 1.0 / 64),
+            "val": lambda: tt(T.val[:, 0:C], T.sc[:, 0:C].indirect(pp), T.sc[:, C:2 * C], A.max, ["sc0", "sc1", "sd0", "sd1", ppk], ["val"]),
             "valtwin": lambda q: twin(q, T.val[:, C:2 * C], T.val[:, 0:C], ["val"], ["val2"]),
-            "tie": lambda: tt(T.tdf[:, 0:C], T.low[:, 0:C].indirect(ou), T.low[:, C:2 * C], A.subtract, ["low", "low2", ouk], ["tdf"]),
+            "tie": lambda: tt(T.tdf[:, 0:C], T.low[:, C:2 * C].indirect(pp), T.low[:, 0:C], A.subtract, ["low", "lowo", ppk], ["tdf"]),
             "dif": lambda: tt(T.dif[:, 0:C], T.val[:, 0:C].indirect(ou), T.val[:, C:2 * C], A.subtract, ["val", "val2", ouk], ["dif"]),
-            "beats": lambda: tt(T.bts[:, 0:C], T.dif[:, 0:C], T.tdf[:, 0:C], A.is_lt, ["dif", "tdf"], ["bts"]),
-            "beatstwin": lambda q: twin(q, T.bts[:, C:2 * C], T.bts[:, 0:C], ["bts"], ["bts2"]),
-            "app": lambda: tt(T.app[:, 0:C], T.bts[:, 0:C].indirect(pp), T.bts[:, C:2 * C], A.mult, ["bts", "bts2", ppk], ["app"]),
-            "apo": lambda: act(T.aof[:, 0:C], T.app[:, 0:C].indirect(ou), ["app", ouk], ["aof"]),
-            "listO": lambda: listed(T.r0, T.opo, ["opo"], ["r0"]),
-            "listA": lambda: listed(T.r1, T.app, ["app"], ["r1"]),
-            "listB": lambda: listed(T.r2, T.aof, ["aof"], ["r2"]),
+            "sign": lambda: op("s", lambda: g.scalar.activation(T.sgn[:, 0:C], T.dif[:, 0:C], ActivationFunctionType.Sign), ["dif"], ["sgn"]),
+            "bp": lambda: tt(T.bp[:, 0:C], T.dif[:, 0:C].indirect(pp), T.tdf[:, 0:C], A.is_lt, ["dif", "tdf", ppk], ["bp"]),
+            "bq": lambda: act(T.bq[:, 0:C], T.bp[:, 0:C].indirect(ou), ["bp", ouk], ["bq"]),
+            "lowtwin": lambda q: twin(q, T.low[:, C:2 * C], T.low[:, 0:C], ["low"], ["lowo"]),
+            "tie0": lambda: tt(T.tdf[:, 0:C], T.low[:, 0:C].indirect(ou), T.low[:, C:2 * C], A.subtract, ["low", "lowo", ouk], ["tdf"]),
+            "beats": lambda: tt(T.sgn[:, 0:C], T.dif[:, 0:C], T.tdf[:, 0:C], A.is_lt, ["dif", "tdf"], ["sgn"]),
+            "bp0": lambda: cp(T.bp[:, 0:C], T.sgn[:, 0:C].indirect(pp), ["sgn", ppk], ["bp"]),
+            "nb0": lambda: ts(sm(15), T.r3[:, 15:C:16], CC, 0.5, A.add, A.is_lt, ["r3", "cc"], ["sm15"]),
+            "listO": lambda: listed(T.r0, T.opo[:, 0:C], ["opo"], ["r0"]),
+            "listP": lambda: listed(T.r1, T.bp[:, 0:C], ["bp"], ["r1"]),
+            "listQ": lambda: listed(T.r2, T.bq[:, 0:C], ["bq"], ["r2"]),
+            "listS": lambda: listed(T.r3, T.sgn[:, 0:C], ["sgn"], ["r3"]),
+            "listL": lambda: listed(T.r4, T.low[:, C:2 * C], ["lowo"], ["r4"], "cwt"),
+            "lx": lambda: ts(sm(12), T.r4[:, 15:C:16], 2.0 ** 60, 2.0 ** -69 / TINY, A.mult, A.mult, ["r4"], ["sm12"]),
+            "lf": lambda: ts(sm(13), T["pp%d" % r][:, 0:16], 1.0 / 512, CL, A.mult, A.add, ["pl%d" % r, "cl"], ["sm13"]),
+            "tw": lambda: tt(sm(14), sm(12), sm(13), A.subtract, ["sm12", "sm13"], ["sm14"]),
+            "nb": lambda: tt(sm(15), T.r3[:, 15:C:16], sm(14), A.is_ge, ["r3", "sm14"], ["sm15"]),
+            "nbp": lambda: ts(sm(16), T.r1[:, 15:C:16], CC, 0.5, A.add, A.is_lt, ["r1", "cc"], ["sm16"]),
+            "w2": lambda: tt(sm(17), sm(3), sm(15), A.mult, ["sm3", "sm15"], ["sm17"]),
             "pf": lambda: cp(sm(0), pp, [ppk], ["sm0"]),
             "dn": lambda: tt(sm(1), w, sm(0), A.subtract, ["sm0", wk], ["sm1"]),
-            "of": lambda: ts(sm(2), T.r0[:, 15:C:16], CC, None, A.add, None, ["r0", "cc"], ["sm2"]),
+            "of": lambda: ts(sm(2), T.r0[:, 15:C:16], CC, 64.0, A.add, A.mult, ["r0", "cc"], ["sm2"]),
             "d2": lambda: tt(sm(3), sm(2), w, A.subtract, ["sm2", wk], ["sm3"]),
-            "cd": lambda: ts(sm(9), sm(3), CC, None, A.mult, None, ["sm3", "cc"], ["sm9"]),
+            "cd": lambda: ts(sm(9), sm(17), CC, None, A.mult, None, ["sm17", "cc"], ["sm9"]),
             "pc": lambda: tt(sm(11), sm(9), sm(0), A.add, ["sm9", "sm0"], ["sm11"]),
-            "free": lambda: ts(sm(4), T.r1[:, 15:C:16], CC, 0.5, A.add, A.is_lt, ["r1", "cc"], ["sm4"]),
+            "free": lambda: tt(sm(4), sm(15), sm(16), A.max, ["sm15", "sm16"], ["sm4"]),
             "a": lambda: tt(sm(5), sm(4), sm(1), A.mult, ["sm4", "sm1"], ["sm5"]),
             "a2": lambda: tt(sm(6), sm(4), T.jw[:, 16:32], A.mult, ["sm4", "jw1"], ["sm6"]),
             "u": lambda: tt(sm(7), sm(5), sm(11), A.add, ["sm5", "sm11"], ["sm7"]),
             "sel": lambda: tt(wn[:, 0:16], sm(6), sm(0), A.max, ["sm6", "sm0"], [wsk]),
-            "m": lambda: tt(sm(10), T.r2[:, 15:C:16], sm(3), A.mult, ["r2", "sm3"], ["sm10"]),
+            "m": lambda: tt(sm(10), T.r2[:, 15:C:16], sm(17), A.mult, ["r2", "sm17"], ["sm10"]),
             "n": lambda: tt(wn[:, 32:48], sm(10), sm(7), A.add, ["sm10", "sm7"], [wnk]),
             "offs": lambda: cp(noff[:, 32:48], wn[:, 32:48], [wnk], [nkey]),
             "offs2": lambda: cp(noff[:, 0:a0], wn[:, 0:a0], [wsk] + ([] if last else [wlk]), [nkey + "l"]),
+            "low": lambda: tt(wn[:, 16:32], wn[:, 32:48], T.jw[:, 0:16], A.min, [wnk, "jw"], [wlk]),
+            "sendP": lambda: send(r + 1, T["pp%d" % (r + 1)][:], noff[:, 16:48], [nkey, nkey + "l"], "ap%d" % (r + 1), "pp%d" % (r + 1), "pl%d" % (r + 1)),
             "row": row,
             "unpackL": lambda: unpack("PB", lx, True, True),
             "packZ": lambda: quant(qz, 0, C, T.zt[:], ["zt0", "zt1", "zt2", "zt3"], [qz + "0", qz + "1"]),
             "W0": lambda: [mm("PA", b, "qw", 128 * b, "qw", qz, False, False, 0) for b in range(4)],
             "FW1": f_and_w,
+            "scales": scales,
         }
-        if r == 0:
-            S["packV"] = lambda: quant("qv", 0, 128, T.vin[:], ["vin"], ["qv"])
-        if last:
-            S["y0"] = first_y
-        else:
-            S["low"] = lambda: tt(wn[:, 16:32], wn[:, 32:48], T.jw[:, 0:16], A.min, [wnk, "jw"], [wlk])
-            S["sendP"] = lambda: send(r + 1, T["pp%d" % (r + 1)][:], noff[:, 16:48], [nkey, nkey + "l"], "ap%d" % (r + 1), "pp%d" % (r + 1), "pl%d" % (r + 1))
-            S["scoreout0"] = lambda: scores_out(0)
 
         def by_row(b):
-            fh, fo, fp, fn, fq = T.fh[:, C * b:C * b + C], T.fo[:, C * b:C * b + C], T.fp[:, 2 * C * b:2 * C * b + C], T.fp[:, 2 * C * b + C:2 * C * b + 2 * C], T.fq[:, C * b:C * b + C]
+            fh, fo, fz, fq = [t[:, C * b:C * b + C] for t in (T.fh, T.fo, T.fz, T.fq)]
+            fp, fn = T.fp[:, 2 * C * b:2 * C * b + C], T.fp[:, 2 * C * b + C:2 * C * b + 2 * C]
+            zt = T.zt[:, b:4 * C:4]
             S["half%d" % b] = lambda q: leave("PA", b, q, fh, 2.0 ** -6, "fh%d" % b)
             S["mate%d" % b] = lambda: act(fo, fh.indirect(ou), ["fh%d" % b, ouk], ["fo%d" % b])
-            S["Z%d" % b] = lambda: tt(T.zt[:, b:4 * C:4], fh.indirect(noff[:, 32:48]), fo, A.add, ["fh%d" % b, "fo%d" % b, nkey], ["zt%d" % b])
-            S["far%d" % b] = lambda: leave("PB", b, "s", fp, 2.0 ** -6, "fp%d" % b)
-            S["fartwin%d" % b] = lambda q: twin(q, fq, fp, ["fp%d" % b], ["fq%d" % b], "tw%d" % b)
-            S["neg%d" % b] = lambda: leave("PB", b, "s", fn, -2.0 ** -6, "fn%d" % b)
-            S["A%d" % b] = lambda: edges(b, (0, 1))
+            S["Z%d" % b] = lambda: tt(zt, fh.indirect(noff[:, 32:48]), fo, A.add, ["fh%d" % b, "fo%d" % b, nkey], ["zt%d" % b])
+            S["pickZ%d" % b] = lambda: act(fz, fh.indirect(noff[:, 32:48]), ["fh%d" % b, nkey], ["fz%d" % b])
+            S["addZ%d" % b] = lambda: tt(zt, fz, fo, A.add, ["fz%d" % b, "fo%d" % b], ["zt%d" % b])
+            S["far%d" % b] = lambda q: leave("PB", b, q, fp, 2.0 ** -6, "fp%d" % b)
+            S["fartwin%d" % b] = lambda q: twin(q, fq, fp, ["fp%d" % b], ["fq%d0" % b, "fq%d1" % b], "tw%d" % b)
+            S["neg%d" % b] = lambda q: leave("PB", b, q, fn, -2.0 ** -6, "fn%d" % b) if q == "s" else ts(fn, fp, -1.0, None, A.mult, None, ["fp%d" % b], ["fn%d" % b])
+            for name, hs in (("", (0, 1)), ("0", (0,)), ("1", (1,))):
+                by_part(b, "%d%s" % (b, name), hs)
             for h in (0, 1):
-                by_half(b, h)
+                S["out%d%d" % (b, h)] = (lambda h: lambda q: leave(PS[h], b, q, T.xt[:, 4 * H * h + b:4 * H * (h + 1):4], 2.0 ** -5, "xt%d%d" % (b, h), H))(h)
 
-        def by_half(b, h):
-            S["A%d%d" % (b, h)] = lambda: edges(b, (h,))
-            S["out%d%d" % (b, h)] = lambda q: leave(PS[h], b, q, T.xt[:, 4 * H * h + b:4 * H * (h + 1):4], 2.0 ** -5, "xt%d%d" % (b, h), H)
+        def by_part(b, name, hs):
+            a, e = H * hs[0], H * hs[-1] + H
+            at, fp, fq = T.at[:, 4 * a + b:4 * e:4], T.fp[:, 2 * C * b + a:2 * C * b + e], T.fq[:, C * b + a:C * b + e]
+            picked = T.fp[:, 2 * C * b:2 * C * (b + 1)].indirect(noff[:, a // 16:e // 16])
+            both, ak, qk = ["fp%d" % b, "fn%d" % b, nkey + "l"], ["at%d%d" % (b, h) for h in hs], ["fq%d%d" % (b, h) for h in hs]
+            S["A" + name] = lambda: tt(at, picked, fq, A.add, both + qk, ak)
+            S["pickA" + name] = lambda: act(fq, picked, both, qk)
+            S["addA" + name] = lambda: tt(at, fq, fp, A.add, ["fp%d" % b] + qk, ak)
+
+        def by_half(h):
+            S["sc%d" % h] = lambda q: leave(PS[h], 3 - 2 * h, q, T.sc[:, H * h:H * h + H], None, "sc%d" % h, H)
+            S["sd%d" % h] = lambda q: leave(PS[h], 2 - 2 * h, q, T.sc[:, C + H * h:C + H * h + H], None, "sd%d" % h, H)
             S["packA%d" % h] = lambda: joined(h)
-            S["packX%d" % h] = lambda: state_packed(h)
+            S["packX%d" % h] = lambda: packed(nx, T.xt, ["xt%d%d" % (b, h) for b in range(4)], h, "qv" if last else "pu")
+            S["y%d" % h] = lambda q: y_out(h, q)
 
         for b in range(4):
             by_row(b)
+        for h in (0, 1):
+            by_half(h)
         return S
 
     dma("y", T.mi[:], T.m[:], [], ["mi"], "ldm")
-    dma("y", T.xin[:], T.x[:], [], ["xin"], "ldx")
+    dma("y", T.xin[:, 0:2 * C], T.x[:, 0:2 * C], [], ["xin0"], "ldx0")
     dma("y", T.uin[:], T.u[:], [], ["uin"], "ldu")
-    dma("y", T.vin[:], T.v[:], [], ["vin"], "ldv")
+    dma("y", T.xin[:, 2 * C:4 * C], T.x[:, 2 * C:4 * C], [], ["xin1"], "ldx1")
     op("g", lambda: g.iota(T.ia[:, 0:17], [[-1, 17]], 16, 1), [], ["ia"])
     op("g", lambda: g.iota(T.iota[:], [[1, C]], 0, 0, allow_small_or_imprecise_dtypes=True), [], ["iota"])
     send(0, T.lp0[:], T.mi[:], ["mi"], "ap0", "lp0")
-    op("v", lambda: g.vector.memset(T.tt[:], 0.0), [], ["tt"])
-    cp(PCOL, T.ia[:, 16:17], ["ia"], ["pcol"])
-    ts(T.ib[:, 0:16], T.ia[:, 0:16], 15, None, A.bitwise_and, None, ["ia"], ["ib"])
-    cp(PM, T.ib[:, 0:1], ["ib"], ["pm"])
-    ts(CC, T.ib[:, 0:1], 15.0, 256.0, A.not_equal, A.mult, ["ib"], ["cc"])
-    ts(T.e01[:, 0:16], T.ib[:, 0:16], 0.0, 512.0, A.is_equal, A.mult, ["ib"], ["e0"])
-    ts(T.e01[:, 16:32], T.ib[:, 0:16], 15.0, -256.0, A.is_equal, A.mult, ["ib"], ["e1"])
-    tt(T.c16[:, 0:16], T.e01[:, 0:16], T.e01[:, 16:32], A.add, ["e0", "e1"], ["c16"])
-    ts(T.tt[:, 3:515:4], T.iota[:, 0:128], PCOL, 32.0, A.is_equal, A.mult, ["iota", "pcol"], ["tt"])
-    ts(T.poff[:, 0:16], T.iota[:, 0:16], 0.0, PM, A.mult, A.add, ["iota", "pm"], ["poff"])
-    cp(T.uoff[:, 0:8], T.iota[:, 0:128:16], ["iota"], ["uoff"])
-    ts(T.jw[:, 0:16], T.iota[:, 0:C:16], PM, None, A.add, None, ["iota", "pm"], ["jw"])
-    ts(T.jw[:, 16:32], T.iota[:, 0:C:16], PM, 1.0 * C, A.add, A.add, ["iota", "pm"], ["jw1"])
-    act(T.cw[:, 0:C], T.c16[:, 0:16].indirect(T.poff[:, 0:16]), ["c16", "poff"], ["cw"])
-    for b in range(4):
-        quant("e", 128 * b, 128 * b + 128, T.tt[:, 3 - b:515 - b], ["tt"], ["e%d" % b])
-    cp(T.off0[:, 32:48], T.mi[:, 0:16], ["mi"], ["off0"])
-    cp(T.w0[:, 32:48], T.mi[:, 0:16], ["mi"], ["wa0"])
-    act(T.ofr[:, 0:C], T.iota[:, 0:C].indirect(T.off0[:, 32:48]), ["iota", "off0"], ["ofr"])
 
-    rounds = [steps(r) for r in range(ROUNDS)] + [{}]
-    for r in range(ROUNDS):
-        for word in ((HEAD if r else FIRST) + " " + TAIL).split():
+    rounds = [steps(r) for r in range(ROUNDS)]
+    rounds[0].update(opening())
+    for r, order in enumerate([FIRST + " " + TAIL, HEAD + " " + TAIL, HEAD + " " + LAST]):
+        for word in order.split():
             name, _, q = word.partition(":")
             step = rounds[r + 1].get(name[:-1]) if name.endswith("+") else rounds[r].get(name)
             if step is not None:
                 step(*q)
 
-    qx = "qx%d" % ROUNDS
-    cp(T.ysb[:, H:C], T.PA[:, 512:512 + H], [], ["PA1", "ysb1"])
-    for k in range(4):
-        dma("ys"[k // 2], T.osc[4 * k:4 * k + 4, :], T[qx + "s"][32 * k:32 * k + 4, :], [qx + "0s", qx + "1s"], [], ["st1", "st2"][k // 2])
-    dma("s", T.y[:, H:C], T.ysb[:, H:C], ["ysb1"], [], "st2")
     for s in sorted(total):
         if waited.get(s, 0) < total[s]:
             g.wait_ge(T.sem[s], total[s])

@@ -3,21 +3,22 @@ from concourse.mybir import dt, AluOpType, ActivationFunctionType
 C = 256
 H = C // 2
 ROUNDS = 3
-TINY = 2.0 ** -118
+U = 1.0 / C
+TINY = 2.0 ** -107
 
-FIRST = """pcol ib pm zero e0 uoff eye off0 e1 E3 c16 poff E0 jw1 row0 E2 cw E1 jw cl packU scaleU pickU packI0 packI1 sendX cwt
-    sd0:s sc0:s sd1:s lw0 pp0 pl0 loadW w0 sc1:s unpackF lows opf lowo val half2:v lf opo valtwin:v half1:s cc pf dif half0:s
-    listL sign mate2 tie lx listO bp of tw listS bq listP d2 nb dn half3:s nbp w2 free cd mate0 listQ a pc mate1 a2
-    restartF0 m u sel mate3 n"""
-HEAD = """sendX half1:s val tie half2:s valtwin:s half3:s mate1 dif tw d2 bp sign half0:s listS listP nb bq dn nbp mate2 w2 free
-    restartF0 cd listQ a pc m u a2 n sel mate0 mate3"""
-TAIL = """unpackL far3:s low neg1:s far2:s far1:s offs offs2 Z2 sendP Z1 fartwin2:g Z0 Z3 far0:s neg0:v fartwin3:y packZ neg2:s
-    fartwin1:s neg3:s pickA0 lows+ A2 W0 FW1 row A10 A30 addA00 A31 packA0 lowo+ addA01 A11 out20:s out00:v packA1 out10:v
-    out30:s pf+ opf+ packX0 out01:v out21:v out31:s opo+ out11:v sd0+:s lf+ packX1 listL+ sc0+:v listO+ lx+ packV of+
-    sd1+:s unpackF+ sc1+:s"""
-LAST = """offs unpackL far0:s offs2 Z2 neg1:s far2:s Z1 neg3:s Z3 fartwin2:g neg0:s far3:s Z0 far1:s pickA0 neg2:v fartwin3:g
-    packZ FW1 A2 addA00 pickA1 row A30 W0 addA10 addA01 packA0 out10:s addA11 A31 out20:s packA1 out00:v out30:s packX0
-    out11:v out01:s out21:v out31:s y0:s packX1 scales y1:v"""
+FIRST = """zero ib pcol e0 cc e1 pm c16 eye uoff jw poff cw E2 packU E1 pickU jw0 scaleU off0 packI0 packI1 sendX loadW jw1 E0
+    E3 row0 cws sd0:s sd1:s pp0 lw0 sc1:v sc0:s opf pl0 w0 val pf cwt lows unpackF valtwin:v half2:v half3:s lowo dif
+    half1:s tie sign opo listL bp mate2 lx listS listO tw bq listP of half0:s nb nbp dn d2 mate1 mate0 free listQ w2 a m u
+    a2 n mate3 sel restartF0"""
+HEAD = """sendX half0:s half1:s val valtwin:s tie dif dn of mate1 half2:s bp sign listS half3:s listP nb d2 nbp w2 free bq
+    listQ a m u a2 n sel mate2 mate3 restartF0 mate0"""
+TAIL = """unpackL far0:s low offs offs2 Z2 Z1 far2:s neg0:v far1:s Z0 Z3 far3:s neg2:s neg3:s pickA0 sendP neg1:s fartwin2:g A2
+    fartwin3:g packZ lows+ A30 restartF1 W1 fartwin1:y W0 addA01 addA00 row A10 A11 packA0 A31 lowo+ packV packA1 out10:v
+    opf+ listL+ out20:v out00:s out30:s out11:v out21:v out01:s packX0 out31:s packX1 pf+ lx+ opo+ sc0+:v sd0+:s unpackF+
+    sd1+:v sc1+:s listO+ tw+"""
+LAST = """unpackL far0:s far2:s far1:s far3:s neg1:s neg3:s offs offs2 fartwin2:g Z2 fartwin3:g pickA1 Z1 Z3 Z0 neg2:v neg0:v
+    pickA0 packZ A2 row addA10 A30 addA00 restartF1 W1 W0 addA01 packA0 A31 addA11 packA1 out10:s out20:s out00:v out30:s
+    packX0 out21:v out01:s out31:v out11:s y0:s packX1 scales y1:s"""
 
 SCRATCH = {
     "PA": ("psum", [128, 2048], "float32"),
@@ -26,13 +27,13 @@ SCRATCH = {
     "uin": ("sbuf", [128, 512], "bfloat16"),
     "vin": ("sbuf", [128, 512], "bfloat16"),
     "mi": ("sbuf", [128, 16], "int32"),
+    "md": ("dram", [128, 16], "int32"),
     "lp0": ("sbuf", [128, 16], "int32"),
     "xt": ("sbuf", [128, 4 * C], "bfloat16"),
     "zt": ("sbuf", [128, 4 * C], "bfloat16"),
     "at": ("sbuf", [128, 4 * C], "bfloat16"),
     "fh": ("sbuf", [128, 4 * C], "bfloat16"),
     "fo": ("sbuf", [128, 4 * C], "bfloat16"),
-    "fz": ("sbuf", [128, 4 * C], "bfloat16"),
     "fp": ("sbuf", [128, 8 * C], "bfloat16"),
     "fq": ("sbuf", [128, 4 * C], "bfloat16"),
     "tt": ("sbuf", [128, 528], "bfloat16"),
@@ -44,6 +45,7 @@ SCRATCH = {
     "c16": ("sbuf", [128, 16], "bfloat16"),
     "cw": ("sbuf", [128, C], "bfloat16"),
     "cwt": ("sbuf", [128, C], "bfloat16"),
+    "cws": ("sbuf", [128, C], "bfloat16"),
     "jw": ("sbuf", [128, 32], "float32"),
     "poff": ("sbuf", [128, 16], "uint16"),
     "uoff": ("sbuf", [128, 8], "uint16"),
@@ -59,7 +61,7 @@ SCRATCH = {
     "opf": ("sbuf", [128, C], "bfloat16"),
     "opo": ("sbuf", [128, C], "bfloat16"),
     "omf": ("sbuf", [128, C], "float32"),
-    "sm": ("sbuf", [128, 320], "float32"),
+    "sm": ("sbuf", [128, 256], "float32"),
     "ysb": ("sbuf", [128, C], "float32"),
 }
 
@@ -86,7 +88,7 @@ for _r in range(ROUNDS):
     _pair("qz%d" % _r, C)
     SCRATCH["pp%d" % _r] = ("sbuf", [128, 32], "uint16")
 
-SEMAPHORES = ["cv", "cs", "cp", "cg", "snd", "ldm", "ldx0", "ldx1", "ldu", "ldw", "lds", "ldv", "st1", "st2"]
+SEMAPHORES = ["cv", "cs", "cp", "cg", "snd", "ldm", "ldd", "ldx0", "ldx1", "ldu", "ldw", "lds", "ldv", "st1", "st2"]
 SEMAPHORES += ["tw%d" % _b for _b in range(4)]
 for _r in range(ROUNDS):
     SEMAPHORES += ["ap%d" % _r, "ac%d" % _r, "as%d" % _r]
@@ -97,9 +99,10 @@ def rank_program(g, core, T, topo):
     if rank is None:
         return
     A = AluOpType
-    COPY = ActivationFunctionType.Copy
+    F = ActivationFunctionType
     Q = {"v": g.vector, "s": g.scalar, "p": g.tensor, "g": g, "y": g.sync}
     CNT = {"v": "cv", "s": "cs", "p": "cp", "g": "cg"}
+    PS = ["PA", "PB"]
     total = {}
     waited = {}
     known = {q: {} for q in Q}
@@ -125,11 +128,11 @@ def rank_program(g, core, T, topo):
                     known[q][s2] = n2
 
     def op(q, call, rd, wr, sem=None, inc=1):
-        marks = [wrote[k] for k in list(rd) + list(wr) if k in wrote]
+        s = sem or CNT[q]
+        marks = [wrote[k] for k in list(rd) + list(wr) if k in wrote and not (k[:2] in PS and wrote[k][0] == s)]
         for k in wr:
             marks += read.get(k, [])
         wait(q, marks)
-        s = sem or CNT[q]
         call().then_inc(T.sem[s], inc)
         total[s] = total.get(s, 0) + inc
         mark = (s, total[s])
@@ -155,11 +158,13 @@ def rank_program(g, core, T, topo):
     def cp(out, in_, rd, wr):
         op("v", lambda: g.vector.tensor_copy(out, in_), rd, wr)
 
-    def act(out, in_, rd, wr, scale=None):
-        if scale is None:
-            op("s", lambda: g.scalar.activation(out, in_, COPY), rd, wr)
+    def act(out, in_, rd, wr, scale=None, bias=None):
+        if bias is not None:
+            op("s", lambda: g.scalar.activation(out, in_, F.Identity, bias=bias, scale=scale), rd, wr)
+        elif scale is None:
+            op("s", lambda: g.scalar.activation(out, in_, F.Copy), rd, wr)
         else:
-            op("s", lambda: g.scalar.activation(out, in_, COPY, scale=scale), rd, wr)
+            op("s", lambda: g.scalar.activation(out, in_, F.Copy, scale=scale), rd, wr)
 
     def twin(q, out, in_, rd, wr, sem=None):
         if q == "g":
@@ -170,7 +175,7 @@ def rank_program(g, core, T, topo):
             (cp if q == "v" else act)(out, in_, rd, wr)
 
     def listed(out, row, rd, wr, cw="cw"):
-        op("v", lambda: g.vector.tensor_tensor_scan(out[:, 0:C], T[cw][:, 0:C], row, 0.0, A.add, A.min), [cw] + rd, wr)
+        op("v", lambda: g.vector.tensor_tensor_scan(out[:], T[cw][:], row, 0.0, A.add, A.min), [cw] + rd, wr)
 
     def quant(name, a, b, tile, rd, keys):
         op("v", lambda: g.vector.quantize_mx(T[name + "c"][:, a:b], T[name + "s"][:, a:b], tile), rd, [k + e for k in keys for e in "cs"])
@@ -187,13 +192,13 @@ def rank_program(g, core, T, topo):
             mm(ps, b, "e", 128 * b, "e%d" % b, rname, start, stop, h)
 
     def leave(ps, b, q, out, scale, key, n=C):
-        src = T[ps][:, 512 * b:512 * b + n]
+        src, wr = T[ps][:, 512 * b:512 * b + n], ["%s%d" % (ps, b)] + (key if isinstance(key, list) else [key])
         if q == "s":
-            act(out, src, [], ["%s%d" % (ps, b), key], scale)
+            act(out, src, [], wr, scale)
         elif scale is None:
-            cp(out, src, [], ["%s%d" % (ps, b), key])
+            cp(out, src, [], wr)
         else:
-            ts(out, src, scale, None, A.mult, None, [], ["%s%d" % (ps, b), key])
+            ts(out, src, scale, None, A.mult, None, [], wr)
 
     partners = [T.cores[rank ^ (1 << r)] for r in range(ROUNDS)]
     common = [e for e in topo.engines(core, partners[0]) if all(e in topo.engines(core, c) for c in partners)]
@@ -212,8 +217,7 @@ def rank_program(g, core, T, topo):
     def sm(k):
         return T.sm[:, 16 * k:16 * k + 16]
 
-    PCOL, PM, CC, CL = [T.cols[:, i:i + 1] for i in range(4)]
-    PS = ["PA", "PB"]
+    PCOL, PM, CC = [T.cols[:, i:i + 1] for i in range(3)]
 
     def packed(name, tile, rd, h, side):
         quant(name, H * h, H * h + H, tile[:, 4 * H * h:4 * H * (h + 1)], rd, ["%s%d" % (name, h)])
@@ -226,8 +230,7 @@ def rank_program(g, core, T, topo):
 
     def opening():
         def load_w():
-            wait("y", [wrote["lp0"]])
-            dma("y", T.qwc[:].bitcast(dt.uint8), T.wc[:], [], ["qwc"], "ldw")
+            dma("y", T.qwc[:].bitcast(dt.uint8), T.wc[:], ["lx00s"], ["qwc"], "ldw")
             dma("y", T.qws[:], T.ws[:], [], ["qws"], "lds")
             dma("y", T.vin[:], T.v[:], [], ["vin"], "ldv")
 
@@ -236,27 +239,28 @@ def rank_program(g, core, T, topo):
             "pcol": lambda: cp(PCOL, T.ia[:, 16:17], ["ia"], ["pcol"]),
             "ib": lambda: ts(T.ib[:, 0:16], T.ia[:, 0:16], 15, None, A.bitwise_and, None, ["ia"], ["ib"]),
             "pm": lambda: cp(PM, T.ib[:, 0:1], ["ib"], ["pm"]),
-            "cc": lambda: ts(CC, T.ib[:, 0:1], 15.0, 4.0, A.not_equal, A.mult, ["ib"], ["cc"]),
-            "cl": lambda: ts(CL, T.ib[:, 0:1], 15.0, 3.5, A.not_equal, A.mult, ["ib"], ["cl"]),
-            "e0": lambda: ts(T.e01[:, 0:16], T.ib[:, 0:16], 0.0, 8.0, A.is_equal, A.mult, ["ib"], ["x0"]),
-            "e1": lambda: ts(T.e01[:, 16:32], T.ib[:, 0:16], 15.0, -4.0, A.is_equal, A.mult, ["ib"], ["x1"]),
+            "cc": lambda: ts(CC, T.ib[:, 0:1], 15.0, None, A.not_equal, None, ["ib"], ["cc"]),
+            "e0": lambda: ts(T.e01[:, 0:16], T.ib[:, 0:16], 0.0, 2.0, A.is_equal, A.mult, ["ib"], ["x0"]),
+            "e1": lambda: ts(T.e01[:, 16:32], T.ib[:, 0:16], 15.0, -1.0, A.is_equal, A.mult, ["ib"], ["x1"]),
             "c16": lambda: tt(T.c16[:, 0:16], T.e01[:, 0:16], T.e01[:, 16:32], A.add, ["x0", "x1"], ["c16"]),
             "eye": lambda: ts(T.tt[:, 3:515:4], T.iota[:, 0:128], PCOL, 32.0, A.is_equal, A.mult, ["iota", "pcol", "tt"], ["eye"]),
             "poff": lambda: ts(T.poff[:, 0:16], T.iota[:, 0:16], 0.0, PM, A.mult, A.add, ["iota", "pm"], ["poff"]),
             "uoff": lambda: cp(T.uoff[:, 0:8], T.iota[:, 0:128:16], ["iota"], ["uoff"]),
-            "jw": lambda: ts(T.jw[:, 0:16], T.iota[:, 0:C:16], PM, None, A.add, None, ["iota", "pm"], ["jw"]),
-            "jw1": lambda: ts(T.jw[:, 16:32], T.iota[:, 0:C:16], PM, 1.0 * C, A.add, A.add, ["iota", "pm"], ["jw1"]),
+            "jw": lambda: ts(T.jw[:, 0:16], T.iota[:, 0:C:16], PM, U, A.add, A.mult, ["iota", "pm"], ["jw"]),
+            "jw1": lambda: ts(T.jw[:, 16:32], T.jw[:, 0:16], 1.0, None, A.add, None, ["jw"], ["jw1"]),
             "cw": lambda: act(T.cw[:, 0:C], T.c16[:, 0:16].indirect(T.poff[:, 0:16]), ["c16", "poff"], ["cw"]),
-            "cwt": lambda: ts(T.cwt[:, 0:C], T.cw[:, 0:C], 64.0 * TINY, None, A.mult, None, ["cw"], ["cwt"]),
+            "cwt": lambda: ts(T.cwt[:, 0:C], T.cw[:, 0:C], C * TINY, None, A.mult, None, ["cw"], ["cwt"]),
+            "cws": lambda: ts(T.cws[:, 0:C], T.cw[:, 0:C], 2.0, None, A.mult, None, ["cw"], ["cws"]),
             "off0": lambda: cp(T.off0[:, 32:48], T.mi[:, 0:16], ["mi"], ["off0"]),
-            "w0": lambda: cp(T.w0[:, 32:48], T.mi[:, 0:16], ["mi"], ["wa0"]),
+            "w0": lambda: ts(T.w0[:, 32:48], T.mi[:, 0:16], U, None, A.mult, None, ["mi"], ["wa0"]),
             "row0": lambda: act(T.ofr[:, 0:C], T.iota[:, 0:C].indirect(T.off0[:, 32:48]), ["iota", "off0"], ["ofr"]),
             "packU": lambda: quant("qu", 0, 128, T.uin[:], ["uin"], ["qu"]),
             "pickU": lambda: cp(T.puc[:, 0:128].bitcast(dt.uint32), T.quc[:, 0:128].bitcast(dt.uint32).indirect(T.uoff[:, 0:8]), ["quc", "uoff"], ["puc"]),
             "scaleU": lambda: act(T.pus[:, 0:128], T.qus[:, 0:128].indirect(T.uoff[:, 0:8]), ["qus", "uoff"], ["pus"]),
             "packI0": lambda: packed("qx0", T.xin, ["xin0"], 0, "pu"),
             "packI1": lambda: packed("qx0", T.xin, ["xin1"], 1, "pu"),
-            "lw0": lambda: tt(sm(8), T.lp0[:, 0:16], T.jw[:, 0:16], A.min, ["lp0", "jw"], ["sm8"]),
+            "jw0": lambda: ts(sm(13), T.iota[:, 0:C:16], PM, None, A.add, None, ["iota", "pm"], ["sm13"]),
+            "lw0": lambda: tt(sm(8), T.lp0[:, 0:16], sm(13), A.min, ["lp0", "sm13"], ["sm8"]),
             "pp0": lambda: cp(T.pp0[:, 16:32], T.lp0[:, 0:16], ["lp0"], ["pp0"]),
             "pl0": lambda: cp(T.pp0[:, 0:16], sm(8), ["sm8"], ["pl0"]),
             "loadW": load_w,
@@ -270,7 +274,7 @@ def rank_program(g, core, T, topo):
         qx, lx, qa, qz, nx = ["%s%d" % (n, r) for n in ("qx", "lx", "qa", "qz")] + ["qx%d" % (r + 1)]
         noff, nkey = T["off%d" % (r + 1)], "off%d" % (r + 1)
         ou, ouk = T["off%d" % r][:, 32:48], "off%d" % r
-        pp, ppk = T["pp%d" % r][:, 16:32], "pp%d" % r
+        pp, ppk, plk = T["pp%d" % r][:, 16:32], "pp%d" % r, "pl%d" % r
         w, wn = T["w%d" % r][:, 32:48], T["w%d" % (r + 1)]
         wk, wnk, wsk, wlk = "wa%d" % r, "wa%d" % (r + 1), "ws%d" % (r + 1), "wl%d" % (r + 1)
         last = r + 1 == ROUNDS
@@ -286,11 +290,6 @@ def rank_program(g, core, T, topo):
             act(T.omf[:, 0:C], T.iota[:, 0:C].indirect(noff[:, 32:48]), ["iota", nkey], ["omf"])
             for k in range(8):
                 dma("y", T.om[k:k + 1, :], T.omf[16 * k:16 * k + 1, :], ["omf"], [], "st1")
-
-        def f_and_w():
-            for b in range(4):
-                mm("PB", b, "e", 128 * b, "e%d" % b, qx, True, False, 1)
-                mm("PB", b, "qw", 128 * b, "qw", qz, False, False, 1)
 
         def joined(h):
             quant(qa, H * h, H * h + H, T.at[:, 4 * H * h:4 * H * (h + 1)], ["at%d%d" % (b, h) for b in range(4)], ["%s%d" % (qa, h)])
@@ -308,74 +307,62 @@ def rank_program(g, core, T, topo):
         S = {
             "sendX": send_x,
             "unpackF": lambda: unpack("PA", qx, True, True),
-            "restartF0": lambda: unpack("PA", qx, True, False, 0),
-            "lows": lambda: act(T.low[:, 0:C], T.iota[:, 0:C].indirect(T["pp%d" % r][:, 0:16]), ["iota", "pl%d" % r], ["low"], TINY),
+            "lows": lambda: act(T.low[:, 0:C], T.iota[:, 0:C].indirect(T["pp%d" % r][:, 0:16]), ["iota", plk], ["low"], TINY),
             "lowo": lambda: act(T.low[:, C:2 * C], T.low[:, 0:C].indirect(ou), ["low", ouk], ["lowo"]),
             "opf": lambda: act(T.opf[:, 0:C], T.ofr[:, 0:C].indirect(pp), ["ofr", ppk], ["opf"]),
-            "opo": lambda: act(T.opo[:, 0:C], T.opf[:, 0:C].indirect(ou), ["opf", ouk], ["opo"], 1.0 / 64),
+            "opo": lambda: act(T.opo[:, 0:C], T.opf[:, 0:C].indirect(ou), ["opf", ouk], ["opo"], U),
             "val": lambda: tt(T.val[:, 0:C], T.sc[:, 0:C].indirect(pp), T.sc[:, C:2 * C], A.max, ["sc0", "sc1", "sd0", "sd1", ppk], ["val"]),
             "valtwin": lambda q: twin(q, T.val[:, C:2 * C], T.val[:, 0:C], ["val"], ["val2"]),
             "tie": lambda: tt(T.tdf[:, 0:C], T.low[:, C:2 * C].indirect(pp), T.low[:, 0:C], A.subtract, ["low", "lowo", ppk], ["tdf"]),
             "dif": lambda: tt(T.dif[:, 0:C], T.val[:, 0:C].indirect(ou), T.val[:, C:2 * C], A.subtract, ["val", "val2", ouk], ["dif"]),
-            "sign": lambda: op("s", lambda: g.scalar.activation(T.sgn[:, 0:C], T.dif[:, 0:C], ActivationFunctionType.Sign), ["dif"], ["sgn"]),
+            "sign": lambda: op("s", lambda: g.scalar.activation(T.sgn[:, 0:C], T.dif[:, 0:C], F.Sign), ["dif"], ["sgn"]),
             "bp": lambda: tt(T.bp[:, 0:C], T.dif[:, 0:C].indirect(pp), T.tdf[:, 0:C], A.is_lt, ["dif", "tdf", ppk], ["bp"]),
-            "bq": lambda: act(T.bq[:, 0:C], T.bp[:, 0:C].indirect(ou), ["bp", ouk], ["bq"]),
-            "lowtwin": lambda q: twin(q, T.low[:, C:2 * C], T.low[:, 0:C], ["low"], ["lowo"]),
-            "tie0": lambda: tt(T.tdf[:, 0:C], T.low[:, 0:C].indirect(ou), T.low[:, C:2 * C], A.subtract, ["low", "lowo", ouk], ["tdf"]),
-            "beats": lambda: tt(T.sgn[:, 0:C], T.dif[:, 0:C], T.tdf[:, 0:C], A.is_lt, ["dif", "tdf"], ["sgn"]),
-            "bp0": lambda: cp(T.bp[:, 0:C], T.sgn[:, 0:C].indirect(pp), ["sgn", ppk], ["bp"]),
-            "nb0": lambda: ts(sm(15), T.r3[:, 15:C:16], CC, 0.5, A.add, A.is_lt, ["r3", "cc"], ["sm15"]),
+            "bq": lambda: act(T.bq[:, 0:C], T.bp[:, 0:C].indirect(ou), ["bp", ouk, "cc"], ["bq"], -1.0, CC),
             "listO": lambda: listed(T.r0, T.opo[:, 0:C], ["opo"], ["r0"]),
             "listP": lambda: listed(T.r1, T.bp[:, 0:C], ["bp"], ["r1"]),
             "listQ": lambda: listed(T.r2, T.bq[:, 0:C], ["bq"], ["r2"]),
-            "listS": lambda: listed(T.r3, T.sgn[:, 0:C], ["sgn"], ["r3"]),
+            "listS": lambda: listed(T.r3, T.sgn[:, 0:C], ["sgn"], ["r3"], "cws"),
             "listL": lambda: listed(T.r4, T.low[:, C:2 * C], ["lowo"], ["r4"], "cwt"),
-            "lx": lambda: ts(sm(12), T.r4[:, 15:C:16], 2.0 ** 60, 2.0 ** -69 / TINY, A.mult, A.mult, ["r4"], ["sm12"]),
-            "lf": lambda: ts(sm(13), T["pp%d" % r][:, 0:16], 1.0 / 512, CL, A.mult, A.add, ["pl%d" % r, "cl"], ["sm13"]),
-            "tw": lambda: tt(sm(14), sm(12), sm(13), A.subtract, ["sm12", "sm13"], ["sm14"]),
+            "pf": lambda: ts(T.sm[:, 0:32], T["pp%d" % r][:, 0:32], U, None, A.mult, None, [ppk, plk], ["sm0", "sm1"]),
+            "dn": lambda: tt(sm(2), w, sm(1), A.subtract, ["sm1", wk], ["sm2"]),
+            "of": lambda: ts(sm(9), T.r0[:, 15:C:16], CC, None, A.add, None, ["r0", "cc"], ["sm9"]),
+            "d2": lambda: tt(sm(3), w, sm(9), A.subtract, ["sm9", wk], ["sm3"]),
+            "lx": lambda: ts(sm(12), T.r4[:, 15:C:16], U / TINY, CC, A.mult, A.subtract, ["r4", "cc"], ["sm12"]),
+            "tw": lambda: tt(sm(14), sm(12), sm(0), A.subtract, ["sm12", "sm0"], ["sm14"]),
             "nb": lambda: tt(sm(15), T.r3[:, 15:C:16], sm(14), A.is_ge, ["r3", "sm14"], ["sm15"]),
-            "nbp": lambda: ts(sm(16), T.r1[:, 15:C:16], CC, 0.5, A.add, A.is_lt, ["r1", "cc"], ["sm16"]),
-            "w2": lambda: tt(sm(17), sm(3), sm(15), A.mult, ["sm3", "sm15"], ["sm17"]),
-            "pf": lambda: cp(sm(0), pp, [ppk], ["sm0"]),
-            "dn": lambda: tt(sm(1), w, sm(0), A.subtract, ["sm0", wk], ["sm1"]),
-            "of": lambda: ts(sm(2), T.r0[:, 15:C:16], CC, 64.0, A.add, A.mult, ["r0", "cc"], ["sm2"]),
-            "d2": lambda: tt(sm(3), sm(2), w, A.subtract, ["sm2", wk], ["sm3"]),
-            "cd": lambda: ts(sm(9), sm(17), CC, None, A.mult, None, ["sm17", "cc"], ["sm9"]),
-            "pc": lambda: tt(sm(11), sm(9), sm(0), A.add, ["sm9", "sm0"], ["sm11"]),
-            "free": lambda: tt(sm(4), sm(15), sm(16), A.max, ["sm15", "sm16"], ["sm4"]),
-            "a": lambda: tt(sm(5), sm(4), sm(1), A.mult, ["sm4", "sm1"], ["sm5"]),
+            "nbp": lambda: ts(sm(8), T.r1[:, 15:C:16], CC, 0.5, A.add, A.is_lt, ["r1", "cc"], ["sm8"]),
+            "w2": lambda: tt(sm(11), sm(3), sm(15), A.mult, ["sm3", "sm15"], ["sm11"]),
+            "free": lambda: tt(sm(4), sm(15), sm(8), A.max, ["sm15", "sm8"], ["sm4"]),
+            "a": lambda: tt(sm(5), sm(4), sm(2), A.mult, ["sm4", "sm2"], ["sm5"]),
             "a2": lambda: tt(sm(6), sm(4), T.jw[:, 16:32], A.mult, ["sm4", "jw1"], ["sm6"]),
-            "u": lambda: tt(sm(7), sm(5), sm(11), A.add, ["sm5", "sm11"], ["sm7"]),
-            "sel": lambda: tt(wn[:, 0:16], sm(6), sm(0), A.max, ["sm6", "sm0"], [wsk]),
-            "m": lambda: tt(sm(10), T.r2[:, 15:C:16], sm(17), A.mult, ["r2", "sm17"], ["sm10"]),
+            "u": lambda: tt(sm(7), sm(5), sm(1), A.add, ["sm5", "sm1"], ["sm7"]),
+            "sel": lambda: tt(wn[:, 0:16], sm(6), sm(1), A.max, ["sm6", "sm1"], [wsk]),
+            "m": lambda: tt(sm(10), T.r2[:, 15:C:16], sm(11), A.mult, ["r2", "sm11"], ["sm10"]),
             "n": lambda: tt(wn[:, 32:48], sm(10), sm(7), A.add, ["sm10", "sm7"], [wnk]),
-            "offs": lambda: cp(noff[:, 32:48], wn[:, 32:48], [wnk], [nkey]),
-            "offs2": lambda: cp(noff[:, 0:a0], wn[:, 0:a0], [wsk] + ([] if last else [wlk]), [nkey + "l"]),
+            "offs": lambda: ts(noff[:, 32:48], wn[:, 32:48], 1.0 * C, None, A.mult, None, [wnk], [nkey]),
+            "offs2": lambda: ts(noff[:, 0:a0], wn[:, 0:a0], 1.0 * C, None, A.mult, None, [wsk] + ([] if last else [wlk]), [nkey + "l"]),
             "low": lambda: tt(wn[:, 16:32], wn[:, 32:48], T.jw[:, 0:16], A.min, [wnk, "jw"], [wlk]),
             "sendP": lambda: send(r + 1, T["pp%d" % (r + 1)][:], noff[:, 16:48], [nkey, nkey + "l"], "ap%d" % (r + 1), "pp%d" % (r + 1), "pl%d" % (r + 1)),
             "row": row,
             "unpackL": lambda: unpack("PB", lx, True, True),
             "packZ": lambda: quant(qz, 0, C, T.zt[:], ["zt0", "zt1", "zt2", "zt3"], [qz + "0", qz + "1"]),
-            "W0": lambda: [mm("PA", b, "qw", 128 * b, "qw", qz, False, False, 0) for b in range(4)],
-            "FW1": f_and_w,
             "scales": scales,
         }
 
         def by_row(b):
-            fh, fo, fz, fq = [t[:, C * b:C * b + C] for t in (T.fh, T.fo, T.fz, T.fq)]
+            fh, fo, fq = [t[:, C * b:C * b + C] for t in (T.fh, T.fo, T.fq)]
             fp, fn = T.fp[:, 2 * C * b:2 * C * b + C], T.fp[:, 2 * C * b + C:2 * C * b + 2 * C]
-            zt = T.zt[:, b:4 * C:4]
-            S["half%d" % b] = lambda q: leave("PA", b, q, fh, 2.0 ** -6, "fh%d" % b)
-            S["mate%d" % b] = lambda: act(fo, fh.indirect(ou), ["fh%d" % b, ouk], ["fo%d" % b])
-            S["Z%d" % b] = lambda: tt(zt, fh.indirect(noff[:, 32:48]), fo, A.add, ["fh%d" % b, "fo%d" % b, nkey], ["zt%d" % b])
-            S["pickZ%d" % b] = lambda: act(fz, fh.indirect(noff[:, 32:48]), ["fh%d" % b, nkey], ["fz%d" % b])
-            S["addZ%d" % b] = lambda: tt(zt, fz, fo, A.add, ["fz%d" % b, "fo%d" % b], ["zt%d" % b])
+            fk = ["fh%d0" % b, "fh%d1" % b]
+            S["half%d" % b] = lambda q: leave("PA", b, q, fh, 2.0 ** -6, fk)
+            S["mate%d" % b] = lambda: act(fo, fh.indirect(ou), fk + [ouk], ["fo%d" % b])
+            S["Z%d" % b] = lambda: tt(T.zt[:, b:4 * C:4], fh.indirect(noff[:, 32:48]), fo, A.add, fk + ["fo%d" % b, nkey], ["zt%d" % b])
             S["far%d" % b] = lambda q: leave("PB", b, q, fp, 2.0 ** -6, "fp%d" % b)
-            S["fartwin%d" % b] = lambda q: twin(q, fq, fp, ["fp%d" % b], ["fq%d0" % b, "fq%d1" % b], "tw%d" % b)
             S["neg%d" % b] = lambda q: leave("PB", b, q, fn, -2.0 ** -6, "fn%d" % b) if q == "s" else ts(fn, fp, -1.0, None, A.mult, None, ["fp%d" % b], ["fn%d" % b])
+            S["fartwin%d" % b] = lambda q: twin(q, fq, fp, ["fp%d" % b], ["fq%d0" % b, "fq%d1" % b], "tw%d" % b)
             for name, hs in (("", (0, 1)), ("0", (0,)), ("1", (1,))):
                 by_part(b, "%d%s" % (b, name), hs)
             for h in (0, 1):
+                S["hf%d%d" % (b, h)] = (lambda h: lambda q: leave(PS[h], b, q, T.fh[:, C * b + H * h:C * b + H * h + H], 2.0 ** -6, "fh%d%d" % (b, h), H))(h)
                 S["out%d%d" % (b, h)] = (lambda h: lambda q: leave(PS[h], b, q, T.xt[:, 4 * H * h + b:4 * H * (h + 1):4], 2.0 ** -5, "xt%d%d" % (b, h), H))(h)
 
         def by_part(b, name, hs):
@@ -390,6 +377,9 @@ def rank_program(g, core, T, topo):
         def by_half(h):
             S["sc%d" % h] = lambda q: leave(PS[h], 3 - 2 * h, q, T.sc[:, H * h:H * h + H], None, "sc%d" % h, H)
             S["sd%d" % h] = lambda q: leave(PS[h], 2 - 2 * h, q, T.sc[:, C + H * h:C + H * h + H], None, "sd%d" % h, H)
+            S["unpackF%d" % h] = lambda: unpack(PS[h], qx, True, True, h)
+            S["restartF%d" % h] = lambda: unpack(PS[h], qx, True, False, h)
+            S["W%d" % h] = lambda: [mm(PS[h], b, "qw", 128 * b, "qw", qz, False, False, h) for b in range(4)]
             S["packA%d" % h] = lambda: joined(h)
             S["packX%d" % h] = lambda: packed(nx, T.xt, ["xt%d%d" % (b, h) for b in range(4)], h, "qv" if last else "pu")
             S["y%d" % h] = lambda q: y_out(h, q)
@@ -400,13 +390,14 @@ def rank_program(g, core, T, topo):
             by_half(h)
         return S
 
+    dma("y", T.md[:], T.m[:], [], ["md"], "ldd")
+    dma("s", T.uin[:], T.u[:], [], ["uin"], "ldu")
     dma("y", T.mi[:], T.m[:], [], ["mi"], "ldm")
-    dma("y", T.xin[:, 0:2 * C], T.x[:, 0:2 * C], [], ["xin0"], "ldx0")
-    dma("y", T.uin[:], T.u[:], [], ["uin"], "ldu")
+    dma("s", T.xin[:, 0:2 * C], T.x[:, 0:2 * C], [], ["xin0"], "ldx0")
     dma("y", T.xin[:, 2 * C:4 * C], T.x[:, 2 * C:4 * C], [], ["xin1"], "ldx1")
     op("g", lambda: g.iota(T.ia[:, 0:17], [[-1, 17]], 16, 1), [], ["ia"])
     op("g", lambda: g.iota(T.iota[:], [[1, C]], 0, 0, allow_small_or_imprecise_dtypes=True), [], ["iota"])
-    send(0, T.lp0[:], T.mi[:], ["mi"], "ap0", "lp0")
+    send(0, T.lp0[:], T.md[:], ["md"], "ap0", "lp0")
 
     rounds = [steps(r) for r in range(ROUNDS)]
     rounds[0].update(opening())

from concourse.mybir import dt, AluOpType, ActivationFunctionType

C = 256
H = C // 2
ROUNDS = 3
U = 1.0 / C
TINY = 2.0 ** -107

FIRST = """zero ib pcol e0 cc e1 pm c16 eye uoff jw poff cw E2 packU E1 pickU jw0 scaleU off0 packI0 packI1 sendX loadW jw1 E0
    E3 row0 cws sd0:s sd1:s pp0 lw0 sc1:v sc0:s opf pl0 w0 val pf cwt lows unpackF valtwin:v half2:v half3:s lowo dif
    half1:s tie sign opo listL bp mate2 lx listS listO tw bq listP of half0:s nb nbp dn d2 mate1 mate0 free listQ w2 a m u
    a2 n mate3 sel restartF0"""
HEAD = """sendX half0:s half1:s val valtwin:s tie dif dn of mate1 half2:s bp sign listS half3:s listP nb d2 nbp w2 free bq
    listQ a m u a2 n sel mate2 mate3 restartF0 mate0"""
TAIL = """unpackL far0:s low offs offs2 Z2 Z1 far2:s neg0:v far1:s Z0 Z3 far3:s neg2:s neg3:s pickA0 sendP neg1:s fartwin2:g A2
    fartwin3:g packZ lows+ A30 restartF1 W1 fartwin1:y W0 addA01 addA00 row A10 A11 packA0 A31 lowo+ packV packA1 out10:v
    opf+ listL+ out20:v out00:s out30:s out11:v out21:v out01:s packX0 out31:s packX1 pf+ lx+ opo+ sc0+:v sd0+:s unpackF+
    sd1+:v sc1+:s listO+ tw+"""
LAST = """unpackL far0:s far2:s far1:s far3:s neg1:s neg3:s offs offs2 fartwin2:g Z2 fartwin3:g pickA1 Z1 Z3 Z0 neg2:v neg0:v
    pickA0 packZ A2 row addA10 A30 addA00 restartF1 W1 W0 addA01 packA0 A31 addA11 packA1 out10:s out20:s out00:v out30:s
    packX0 out21:v out01:s out31:v out11:s y0:s packX1 scales y1:s"""

SCRATCH = {
    "PA": ("psum", [128, 2048], "float32"),
    "PB": ("psum", [128, 2048], "float32"),
    "xin": ("sbuf", [128, 4 * C], "bfloat16"),
    "uin": ("sbuf", [128, 512], "bfloat16"),
    "vin": ("sbuf", [128, 512], "bfloat16"),
    "mi": ("sbuf", [128, 16], "int32"),
    "md": ("dram", [128, 16], "int32"),
    "lp0": ("sbuf", [128, 16], "int32"),
    "xt": ("sbuf", [128, 4 * C], "bfloat16"),
    "zt": ("sbuf", [128, 4 * C], "bfloat16"),
    "at": ("sbuf", [128, 4 * C], "bfloat16"),
    "fh": ("sbuf", [128, 4 * C], "bfloat16"),
    "fo": ("sbuf", [128, 4 * C], "bfloat16"),
    "fp": ("sbuf", [128, 8 * C], "bfloat16"),
    "fq": ("sbuf", [128, 4 * C], "bfloat16"),
    "tt": ("sbuf", [128, 528], "bfloat16"),
    "ia": ("sbuf", [128, 24], "int32"),
    "ib": ("sbuf", [128, 24], "int32"),
    "iota": ("sbuf", [128, C], "float32"),
    "cols": ("sbuf", [128, 8], "float32"),
    "e01": ("sbuf", [128, 32], "float32"),
    "c16": ("sbuf", [128, 16], "bfloat16"),
    "cw": ("sbuf", [128, C], "bfloat16"),
    "cwt": ("sbuf", [128, C], "bfloat16"),
    "cws": ("sbuf", [128, C], "bfloat16"),
    "jw": ("sbuf", [128, 32], "float32"),
    "poff": ("sbuf", [128, 16], "uint16"),
    "uoff": ("sbuf", [128, 8], "uint16"),
    "sc": ("sbuf", [128, 2 * C], "float32"),
    "val": ("sbuf", [128, 2 * C], "float32"),
    "dif": ("sbuf", [128, C], "bfloat16"),
    "tdf": ("sbuf", [128, C], "bfloat16"),
    "low": ("sbuf", [128, 2 * C], "bfloat16"),
    "sgn": ("sbuf", [128, C], "bfloat16"),
    "bp": ("sbuf", [128, C], "bfloat16"),
    "bq": ("sbuf", [128, C], "bfloat16"),
    "ofr": ("sbuf", [128, C], "bfloat16"),
    "opf": ("sbuf", [128, C], "bfloat16"),
    "opo": ("sbuf", [128, C], "bfloat16"),
    "omf": ("sbuf", [128, C], "float32"),
    "sm": ("sbuf", [128, 256], "float32"),
    "ysb": ("sbuf", [128, C], "float32"),
}


def _pair(name, n):
    SCRATCH[name + "c"] = ("sbuf", [128, n], "float8_e4m3fn_x4")
    SCRATCH[name + "s"] = ("sbuf", [128, n], "uint8")


_pair("e", 4 * 128)
_pair("qu", 128)
_pair("pu", 128)
_pair("qv", 128)
_pair("qw", 512)
for _r in range(5):
    SCRATCH["r%d" % _r] = ("sbuf", [128, C], "bfloat16")
for _r in range(ROUNDS + 1):
    _pair("qx%d" % _r, C)
    SCRATCH["w%d" % _r] = ("sbuf", [128, 48], "float32")
    SCRATCH["off%d" % _r] = ("sbuf", [128, 48], "uint16")
for _r in range(ROUNDS):
    _pair("lx%d" % _r, C)
    _pair("qa%d" % _r, C)
    _pair("qz%d" % _r, C)
    SCRATCH["pp%d" % _r] = ("sbuf", [128, 32], "uint16")

SEMAPHORES = ["cv", "cs", "cp", "cg", "snd", "ldm", "ldd", "ldx0", "ldx1", "ldu", "ldw", "lds", "ldv", "st1", "st2"]
SEMAPHORES += ["tw%d" % _b for _b in range(4)]
for _r in range(ROUNDS):
    SEMAPHORES += ["ap%d" % _r, "ac%d" % _r, "as%d" % _r]


def rank_program(g, core, T, topo):
    rank = T.rank_of(core)
    if rank is None:
        return
    A = AluOpType
    F = ActivationFunctionType
    Q = {"v": g.vector, "s": g.scalar, "p": g.tensor, "g": g, "y": g.sync}
    CNT = {"v": "cv", "s": "cs", "p": "cp", "g": "cg"}
    PS = ["PA", "PB"]
    total = {}
    waited = {}
    known = {q: {} for q in Q}
    behind = {}
    wrote = {}
    read = {}

    def wait(q, marks):
        need = {}
        for s, n in marks:
            if q == "p" and s == "cp":
                continue
            if n > need.get(s, 0):
                need[s] = n
        for s, n in sorted(need.items(), key=lambda t: -len(behind.get(t, {}))):
            if known[q].get(s, 0) >= n:
                continue
            Q[q].wait_ge(T.sem[s], n)
            waited[s] = max(waited.get(s, 0), n)
            known[q][s] = n
            for s2, n2 in behind.get((s, n), {}).items():
                if n2 > known[q].get(s2, 0):
                    known[q][s2] = n2

    def op(q, call, rd, wr, sem=None, inc=1):
        s = sem or CNT[q]
        marks = [wrote[k] for k in list(rd) + list(wr) if k in wrote and not (k[:2] in PS and wrote[k][0] == s)]
        for k in wr:
            marks += read.get(k, [])
        wait(q, marks)
        call().then_inc(T.sem[s], inc)
        total[s] = total.get(s, 0) + inc
        mark = (s, total[s])
        behind[mark] = dict(known[q])
        for k in wr:
            wrote[k] = mark
            read[k] = []
        for k in rd:
            read.setdefault(k, []).append(mark)

    def dma(q, out, in_, rd, wr, sem):
        op(q, lambda: Q[q].dma_start(out, in_), rd, wr, sem, 16)

    def ts(out, in0, s1, s2, o0, o1, rd, wr):
        if o1 is None:
            op("v", lambda: g.vector.tensor_scalar(out, in0, s1, None, o0), rd, wr)
        else:
            op("v", lambda: g.vector.tensor_scalar(out, in0, s1, s2, o0, o1), rd, wr)

    def tt(out, in0, in1, o, rd, wr):
        op("v", lambda: g.vector.tensor_tensor(out, in0, in1, o), rd, wr)

    def cp(out, in_, rd, wr):
        op("v", lambda: g.vector.tensor_copy(out, in_), rd, wr)

    def act(out, in_, rd, wr, scale=None, bias=None):
        if bias is not None:
            op("s", lambda: g.scalar.activation(out, in_, F.Identity, bias=bias, scale=scale), rd, wr)
        elif scale is None:
            op("s", lambda: g.scalar.activation(out, in_, F.Copy), rd, wr)
        else:
            op("s", lambda: g.scalar.activation(out, in_, F.Copy, scale=scale), rd, wr)

    def twin(q, out, in_, rd, wr, sem=None):
        if q == "g":
            op("g", lambda: g.affine_select(out, in_, [[0, C]], A.is_gt, 0.0, 1, 0), rd, wr)
        elif q == "y":
            dma("y", out, in_, rd, wr, sem)
        else:
            (cp if q == "v" else act)(out, in_, rd, wr)

    def listed(out, row, rd, wr, cw="cw"):
        op("v", lambda: g.vector.tensor_tensor_scan(out[:], T[cw][:], row, 0.0, A.add, A.min), [cw] + rd, wr)

    def quant(name, a, b, tile, rd, keys):
        op("v", lambda: g.vector.quantize_mx(T[name + "c"][:, a:b], T[name + "s"][:, a:b], tile), rd, [k + e for k in keys for e in "cs"])

    def mm(ps, b, lname, la, lkey, rname, start, stop, h=None):
        a, n = (0, C) if h is None else (H * h, H)
        op("p", lambda: g.tensor.matmul_mx(
            T[ps][:, 512 * b:512 * b + n], T[lname + "c"][:, la:la + 128], T[lname + "s"][:, la:la + 128],
            T[rname + "c"][:, a:a + n], T[rname + "s"][:, a:a + n], start, stop),
            [lkey + "c", lkey + "s"] + ["%s%d%s" % (rname, k, e) for k in ((0, 1) if h is None else (h,)) for e in "cs"], ["%s%d" % (ps, b)])

    def unpack(ps, rname, start, stop, h=None):
        for b in range(4):
            mm(ps, b, "e", 128 * b, "e%d" % b, rname, start, stop, h)

    def leave(ps, b, q, out, scale, key, n=C):
        src, wr = T[ps][:, 512 * b:512 * b + n], ["%s%d" % (ps, b)] + (key if isinstance(key, list) else [key])
        if q == "s":
            act(out, src, [], wr, scale)
        elif scale is None:
            cp(out, src, [], wr)
        else:
            ts(out, src, scale, None, A.mult, None, [], wr)

    partners = [T.cores[rank ^ (1 << r)] for r in range(ROUNDS)]
    common = [e for e in topo.engines(core, partners[0]) if all(e in topo.engines(core, c) for c in partners)]

    def send(r, out, in_, rd, sem, *keys):
        engines = common if sem.startswith("ap") else topo.engines(core, partners[r])
        mask = sum(1 << e for e in engines)
        wait("g", [wrote[k] for k in rd])
        rid, pid, _ = topo.addr(partners[r])
        g.remote_dma(out, in_, T.sem[sem], T.sem.snd, pid, rid, mask)
        total["snd"] = total.get("snd", 0) + len(engines)
        total[sem] = len(engines)
        for key in keys:
            wrote[key] = (sem, len(engines))

    def sm(k):
        return T.sm[:, 16 * k:16 * k + 16]

    PCOL, PM, CC = [T.cols[:, i:i + 1] for i in range(3)]

    def packed(name, tile, rd, h, side):
        quant(name, H * h, H * h + H, tile[:, 4 * H * h:4 * H * (h + 1)], rd, ["%s%d" % (name, h)])
        if side == "pu":
            for b in (0, 1):
                mm(PS[h], b + 2 - 2 * h, "pu", 0, "pu", name, True, True, h)
        else:
            mm("PA", h, "qv", 0, "qv", name, True, True, h)
            dma("y", T.oc[:, 4 * H * h:4 * H * (h + 1)], T[name + "c"][:, H * h:H * h + H].bitcast(dt.uint8), ["%s%dc" % (name, h)], [], "st1")

    def opening():
        def load_w():
            dma("y", T.qwc[:].bitcast(dt.uint8), T.wc[:], ["lx00s"], ["qwc"], "ldw")
            dma("y", T.qws[:], T.ws[:], [], ["qws"], "lds")
            dma("y", T.vin[:], T.v[:], [], ["vin"], "ldv")

        S = {
            "zero": lambda: op("v", lambda: g.vector.memset(T.tt[:], 0.0), [], ["tt"]),
            "pcol": lambda: cp(PCOL, T.ia[:, 16:17], ["ia"], ["pcol"]),
            "ib": lambda: ts(T.ib[:, 0:16], T.ia[:, 0:16], 15, None, A.bitwise_and, None, ["ia"], ["ib"]),
            "pm": lambda: cp(PM, T.ib[:, 0:1], ["ib"], ["pm"]),
            "cc": lambda: ts(CC, T.ib[:, 0:1], 15.0, None, A.not_equal, None, ["ib"], ["cc"]),
            "e0": lambda: ts(T.e01[:, 0:16], T.ib[:, 0:16], 0.0, 2.0, A.is_equal, A.mult, ["ib"], ["x0"]),
            "e1": lambda: ts(T.e01[:, 16:32], T.ib[:, 0:16], 15.0, -1.0, A.is_equal, A.mult, ["ib"], ["x1"]),
            "c16": lambda: tt(T.c16[:, 0:16], T.e01[:, 0:16], T.e01[:, 16:32], A.add, ["x0", "x1"], ["c16"]),
            "eye": lambda: ts(T.tt[:, 3:515:4], T.iota[:, 0:128], PCOL, 32.0, A.is_equal, A.mult, ["iota", "pcol", "tt"], ["eye"]),
            "poff": lambda: ts(T.poff[:, 0:16], T.iota[:, 0:16], 0.0, PM, A.mult, A.add, ["iota", "pm"], ["poff"]),
            "uoff": lambda: cp(T.uoff[:, 0:8], T.iota[:, 0:128:16], ["iota"], ["uoff"]),
            "jw": lambda: ts(T.jw[:, 0:16], T.iota[:, 0:C:16], PM, U, A.add, A.mult, ["iota", "pm"], ["jw"]),
            "jw1": lambda: ts(T.jw[:, 16:32], T.jw[:, 0:16], 1.0, None, A.add, None, ["jw"], ["jw1"]),
            "cw": lambda: act(T.cw[:, 0:C], T.c16[:, 0:16].indirect(T.poff[:, 0:16]), ["c16", "poff"], ["cw"]),
            "cwt": lambda: ts(T.cwt[:, 0:C], T.cw[:, 0:C], C * TINY, None, A.mult, None, ["cw"], ["cwt"]),
            "cws": lambda: ts(T.cws[:, 0:C], T.cw[:, 0:C], 2.0, None, A.mult, None, ["cw"], ["cws"]),
            "off0": lambda: cp(T.off0[:, 32:48], T.mi[:, 0:16], ["mi"], ["off0"]),
            "w0": lambda: ts(T.w0[:, 32:48], T.mi[:, 0:16], U, None, A.mult, None, ["mi"], ["wa0"]),
            "row0": lambda: act(T.ofr[:, 0:C], T.iota[:, 0:C].indirect(T.off0[:, 32:48]), ["iota", "off0"], ["ofr"]),
            "packU": lambda: quant("qu", 0, 128, T.uin[:], ["uin"], ["qu"]),
            "pickU": lambda: cp(T.puc[:, 0:128].bitcast(dt.uint32), T.quc[:, 0:128].bitcast(dt.uint32).indirect(T.uoff[:, 0:8]), ["quc", "uoff"], ["puc"]),
            "scaleU": lambda: act(T.pus[:, 0:128], T.qus[:, 0:128].indirect(T.uoff[:, 0:8]), ["qus", "uoff"], ["pus"]),
            "packI0": lambda: packed("qx0", T.xin, ["xin0"], 0, "pu"),
            "packI1": lambda: packed("qx0", T.xin, ["xin1"], 1, "pu"),
            "jw0": lambda: ts(sm(13), T.iota[:, 0:C:16], PM, None, A.add, None, ["iota", "pm"], ["sm13"]),
            "lw0": lambda: tt(sm(8), T.lp0[:, 0:16], sm(13), A.min, ["lp0", "sm13"], ["sm8"]),
            "pp0": lambda: cp(T.pp0[:, 16:32], T.lp0[:, 0:16], ["lp0"], ["pp0"]),
            "pl0": lambda: cp(T.pp0[:, 0:16], sm(8), ["sm8"], ["pl0"]),
            "loadW": load_w,
            "packV": lambda: quant("qv", 0, 128, T.vin[:], ["vin"], ["qv"]),
        }
        for b in range(4):
            S["E%d" % b] = (lambda b: lambda: quant("e", 128 * b, 128 * b + 128, T.tt[:, 3 - b:515 - b], ["eye"], ["e%d" % b]))(b)
        return S

    def steps(r):
        qx, lx, qa, qz, nx = ["%s%d" % (n, r) for n in ("qx", "lx", "qa", "qz")] + ["qx%d" % (r + 1)]
        noff, nkey = T["off%d" % (r + 1)], "off%d" % (r + 1)
        ou, ouk = T["off%d" % r][:, 32:48], "off%d" % r
        pp, ppk, plk = T["pp%d" % r][:, 16:32], "pp%d" % r, "pl%d" % r
        w, wn = T["w%d" % r][:, 32:48], T["w%d" % (r + 1)]
        wk, wnk, wsk, wlk = "wa%d" % r, "wa%d" % (r + 1), "ws%d" % (r + 1), "wl%d" % (r + 1)
        last = r + 1 == ROUNDS

        def send_x():
            send(r, T[lx + "c"][:].bitcast(dt.uint8), T[qx + "c"][:].bitcast(dt.uint8), [qx + "0c", qx + "1c"], "ac%d" % r, lx + "0c", lx + "1c")
            send(r, T[lx + "s"][:], T[qx + "s"][:], [qx + "0s", qx + "1s"], "as%d" % r, lx + "0s", lx + "1s")

        def row():
            if not last:
                act(T.ofr[:, 0:C], T.iota[:, 0:C].indirect(noff[:, 32:48]), ["iota", nkey], ["ofr"])
                return
            act(T.omf[:, 0:C], T.iota[:, 0:C].indirect(noff[:, 32:48]), ["iota", nkey], ["omf"])
            for k in range(8):
                dma("y", T.om[k:k + 1, :], T.omf[16 * k:16 * k + 1, :], ["omf"], [], "st1")

        def joined(h):
            quant(qa, H * h, H * h + H, T.at[:, 4 * H * h:4 * H * (h + 1)], ["at%d%d" % (b, h) for b in range(4)], ["%s%d" % (qa, h)])
            unpack(PS[h], qa, False, True, h)

        def y_out(h, q):
            leave("PA", h, q, T.ysb[:, H * h:H * h + H], None, "ysb%d" % h, H)
            dma("s", T.y[:, H * h:H * h + H], T.ysb[:, H * h:H * h + H], ["ysb%d" % h], [], "st2")

        def scales():
            for k in range(4):
                dma("y", T.osc[4 * k:4 * k + 4, :], T[nx + "s"][32 * k:32 * k + 4, :], [nx + "0s", nx + "1s"], [], "st1")

        a0 = 16 if last else 32
        S = {
            "sendX": send_x,
            "unpackF": lambda: unpack("PA", qx, True, True),
            "lows": lambda: act(T.low[:, 0:C], T.iota[:, 0:C].indirect(T["pp%d" % r][:, 0:16]), ["iota", plk], ["low"], TINY),
            "lowo": lambda: act(T.low[:, C:2 * C], T.low[:, 0:C].indirect(ou), ["low", ouk], ["lowo"]),
            "opf": lambda: act(T.opf[:, 0:C], T.ofr[:, 0:C].indirect(pp), ["ofr", ppk], ["opf"]),
            "opo": lambda: act(T.opo[:, 0:C], T.opf[:, 0:C].indirect(ou), ["opf", ouk], ["opo"], U),
            "val": lambda: tt(T.val[:, 0:C], T.sc[:, 0:C].indirect(pp), T.sc[:, C:2 * C], A.max, ["sc0", "sc1", "sd0", "sd1", ppk], ["val"]),
            "valtwin": lambda q: twin(q, T.val[:, C:2 * C], T.val[:, 0:C], ["val"], ["val2"]),
            "tie": lambda: tt(T.tdf[:, 0:C], T.low[:, C:2 * C].indirect(pp), T.low[:, 0:C], A.subtract, ["low", "lowo", ppk], ["tdf"]),
            "dif": lambda: tt(T.dif[:, 0:C], T.val[:, 0:C].indirect(ou), T.val[:, C:2 * C], A.subtract, ["val", "val2", ouk], ["dif"]),
            "sign": lambda: op("s", lambda: g.scalar.activation(T.sgn[:, 0:C], T.dif[:, 0:C], F.Sign), ["dif"], ["sgn"]),
            "bp": lambda: tt(T.bp[:, 0:C], T.dif[:, 0:C].indirect(pp), T.tdf[:, 0:C], A.is_lt, ["dif", "tdf", ppk], ["bp"]),
            "bq": lambda: act(T.bq[:, 0:C], T.bp[:, 0:C].indirect(ou), ["bp", ouk, "cc"], ["bq"], -1.0, CC),
            "listO": lambda: listed(T.r0, T.opo[:, 0:C], ["opo"], ["r0"]),
            "listP": lambda: listed(T.r1, T.bp[:, 0:C], ["bp"], ["r1"]),
            "listQ": lambda: listed(T.r2, T.bq[:, 0:C], ["bq"], ["r2"]),
            "listS": lambda: listed(T.r3, T.sgn[:, 0:C], ["sgn"], ["r3"], "cws"),
            "listL": lambda: listed(T.r4, T.low[:, C:2 * C], ["lowo"], ["r4"], "cwt"),
            "pf": lambda: ts(T.sm[:, 0:32], T["pp%d" % r][:, 0:32], U, None, A.mult, None, [ppk, plk], ["sm0", "sm1"]),
            "dn": lambda: tt(sm(2), w, sm(1), A.subtract, ["sm1", wk], ["sm2"]),
            "of": lambda: ts(sm(9), T.r0[:, 15:C:16], CC, None, A.add, None, ["r0", "cc"], ["sm9"]),
            "d2": lambda: tt(sm(3), w, sm(9), A.subtract, ["sm9", wk], ["sm3"]),
            "lx": lambda: ts(sm(12), T.r4[:, 15:C:16], U / TINY, CC, A.mult, A.subtract, ["r4", "cc"], ["sm12"]),
            "tw": lambda: tt(sm(14), sm(12), sm(0), A.subtract, ["sm12", "sm0"], ["sm14"]),
            "nb": lambda: tt(sm(15), T.r3[:, 15:C:16], sm(14), A.is_ge, ["r3", "sm14"], ["sm15"]),
            "nbp": lambda: ts(sm(8), T.r1[:, 15:C:16], CC, 0.5, A.add, A.is_lt, ["r1", "cc"], ["sm8"]),
            "w2": lambda: tt(sm(11), sm(3), sm(15), A.mult, ["sm3", "sm15"], ["sm11"]),
            "free": lambda: tt(sm(4), sm(15), sm(8), A.max, ["sm15", "sm8"], ["sm4"]),
            "a": lambda: tt(sm(5), sm(4), sm(2), A.mult, ["sm4", "sm2"], ["sm5"]),
            "a2": lambda: tt(sm(6), sm(4), T.jw[:, 16:32], A.mult, ["sm4", "jw1"], ["sm6"]),
            "u": lambda: tt(sm(7), sm(5), sm(1), A.add, ["sm5", "sm1"], ["sm7"]),
            "sel": lambda: tt(wn[:, 0:16], sm(6), sm(1), A.max, ["sm6", "sm1"], [wsk]),
            "m": lambda: tt(sm(10), T.r2[:, 15:C:16], sm(11), A.mult, ["r2", "sm11"], ["sm10"]),
            "n": lambda: tt(wn[:, 32:48], sm(10), sm(7), A.add, ["sm10", "sm7"], [wnk]),
            "offs": lambda: ts(noff[:, 32:48], wn[:, 32:48], 1.0 * C, None, A.mult, None, [wnk], [nkey]),
            "offs2": lambda: ts(noff[:, 0:a0], wn[:, 0:a0], 1.0 * C, None, A.mult, None, [wsk] + ([] if last else [wlk]), [nkey + "l"]),
            "low": lambda: tt(wn[:, 16:32], wn[:, 32:48], T.jw[:, 0:16], A.min, [wnk, "jw"], [wlk]),
            "sendP": lambda: send(r + 1, T["pp%d" % (r + 1)][:], noff[:, 16:48], [nkey, nkey + "l"], "ap%d" % (r + 1), "pp%d" % (r + 1), "pl%d" % (r + 1)),
            "row": row,
            "unpackL": lambda: unpack("PB", lx, True, True),
            "packZ": lambda: quant(qz, 0, C, T.zt[:], ["zt0", "zt1", "zt2", "zt3"], [qz + "0", qz + "1"]),
            "scales": scales,
        }

        def by_row(b):
            fh, fo, fq = [t[:, C * b:C * b + C] for t in (T.fh, T.fo, T.fq)]
            fp, fn = T.fp[:, 2 * C * b:2 * C * b + C], T.fp[:, 2 * C * b + C:2 * C * b + 2 * C]
            fk = ["fh%d0" % b, "fh%d1" % b]
            S["half%d" % b] = lambda q: leave("PA", b, q, fh, 2.0 ** -6, fk)
            S["mate%d" % b] = lambda: act(fo, fh.indirect(ou), fk + [ouk], ["fo%d" % b])
            S["Z%d" % b] = lambda: tt(T.zt[:, b:4 * C:4], fh.indirect(noff[:, 32:48]), fo, A.add, fk + ["fo%d" % b, nkey], ["zt%d" % b])
            S["far%d" % b] = lambda q: leave("PB", b, q, fp, 2.0 ** -6, "fp%d" % b)
            S["neg%d" % b] = lambda q: leave("PB", b, q, fn, -2.0 ** -6, "fn%d" % b) if q == "s" else ts(fn, fp, -1.0, None, A.mult, None, ["fp%d" % b], ["fn%d" % b])
            S["fartwin%d" % b] = lambda q: twin(q, fq, fp, ["fp%d" % b], ["fq%d0" % b, "fq%d1" % b], "tw%d" % b)
            for name, hs in (("", (0, 1)), ("0", (0,)), ("1", (1,))):
                by_part(b, "%d%s" % (b, name), hs)
            for h in (0, 1):
                S["hf%d%d" % (b, h)] = (lambda h: lambda q: leave(PS[h], b, q, T.fh[:, C * b + H * h:C * b + H * h + H], 2.0 ** -6, "fh%d%d" % (b, h), H))(h)
                S["out%d%d" % (b, h)] = (lambda h: lambda q: leave(PS[h], b, q, T.xt[:, 4 * H * h + b:4 * H * (h + 1):4], 2.0 ** -5, "xt%d%d" % (b, h), H))(h)

        def by_part(b, name, hs):
            a, e = H * hs[0], H * hs[-1] + H
            at, fp, fq = T.at[:, 4 * a + b:4 * e:4], T.fp[:, 2 * C * b + a:2 * C * b + e], T.fq[:, C * b + a:C * b + e]
            picked = T.fp[:, 2 * C * b:2 * C * (b + 1)].indirect(noff[:, a // 16:e // 16])
            both, ak, qk = ["fp%d" % b, "fn%d" % b, nkey + "l"], ["at%d%d" % (b, h) for h in hs], ["fq%d%d" % (b, h) for h in hs]
            S["A" + name] = lambda: tt(at, picked, fq, A.add, both + qk, ak)
            S["pickA" + name] = lambda: act(fq, picked, both, qk)
            S["addA" + name] = lambda: tt(at, fq, fp, A.add, ["fp%d" % b] + qk, ak)

        def by_half(h):
            S["sc%d" % h] = lambda q: leave(PS[h], 3 - 2 * h, q, T.sc[:, H * h:H * h + H], None, "sc%d" % h, H)
            S["sd%d" % h] = lambda q: leave(PS[h], 2 - 2 * h, q, T.sc[:, C + H * h:C + H * h + H], None, "sd%d" % h, H)
            S["unpackF%d" % h] = lambda: unpack(PS[h], qx, True, True, h)
            S["restartF%d" % h] = lambda: unpack(PS[h], qx, True, False, h)
            S["W%d" % h] = lambda: [mm(PS[h], b, "qw", 128 * b, "qw", qz, False, False, h) for b in range(4)]
            S["packA%d" % h] = lambda: joined(h)
            S["packX%d" % h] = lambda: packed(nx, T.xt, ["xt%d%d" % (b, h) for b in range(4)], h, "qv" if last else "pu")
            S["y%d" % h] = lambda q: y_out(h, q)

        for b in range(4):
            by_row(b)
        for h in (0, 1):
            by_half(h)
        return S

    dma("y", T.md[:], T.m[:], [], ["md"], "ldd")
    dma("s", T.uin[:], T.u[:], [], ["uin"], "ldu")
    dma("y", T.mi[:], T.m[:], [], ["mi"], "ldm")
    dma("s", T.xin[:, 0:2 * C], T.x[:, 0:2 * C], [], ["xin0"], "ldx0")
    dma("y", T.xin[:, 2 * C:4 * C], T.x[:, 2 * C:4 * C], [], ["xin1"], "ldx1")
    op("g", lambda: g.iota(T.ia[:, 0:17], [[-1, 17]], 16, 1), [], ["ia"])
    op("g", lambda: g.iota(T.iota[:], [[1, C]], 0, 0, allow_small_or_imprecise_dtypes=True), [], ["iota"])
    send(0, T.lp0[:], T.md[:], ["md"], "ap0", "lp0")

    rounds = [steps(r) for r in range(ROUNDS)]
    rounds[0].update(opening())
    for r, order in enumerate([FIRST + " " + TAIL, HEAD + " " + TAIL, HEAD + " " + LAST]):
        for word in order.split():
            name, _, q = word.partition(":")
            step = rounds[r + 1].get(name[:-1]) if name.endswith("+") else rounds[r].get(name)
            if step is not None:
                step(*q)

    for s in sorted(total):
        if waited.get(s, 0) < total[s]:
            g.wait_ge(T.sem[s], total[s])
